import numpy as np, ml_dtypes
CORES = [16,18,20,22]
N = 4
import mx_ref
BF = ml_dtypes.bfloat16
def pick(q, e):
    c = np.concatenate([q[0].reshape(128, -1, 4), np.zeros((128, 1, 4), np.uint8)], axis=1); s = np.concatenate([q[1], np.ones((16, 1), np.uint8)], axis=1)
    return (np.ascontiguousarray(c[:, e].reshape(128, -1)), np.ascontiguousarray(s[:, e]))
def join(*qs):
    return (np.concatenate([q[0] for q in qs], axis=1), np.concatenate([q[1] for q in qs], axis=1))
def put(q, e, v):
    c, s = q[0].reshape(128, -1, 4).copy(), q[1].copy(); c[:, e] = v[0].reshape(128, -1, 4); s[:, e] = v[1]
    return (c.reshape(128, -1), s)
def pk(c, s):
    return (np.ascontiguousarray(c), mx_ref.live(s))
def emit(q):
    return q[0], q[1]
def decode(q):
    o = []
    for b in range(4):
        e = np.zeros((128, 128, 4), np.float32); e[np.arange(128), np.arange(128), b] = 1
        o.append(mx_ref.matmul(mx_ref.quantize(e.reshape(128, 512).astype(BF)), q))
    return np.stack(o, axis=2).reshape(128, -1)
def cols(t, e):
    v = np.concatenate([t.reshape(128, -1, 4), np.zeros((128, 1, 4), BF)], axis=1)
    return np.ascontiguousarray(v[:, e]).reshape(128, -1)
def cut(t, i, w=512):
    return t[:, w * i:w * i + w]
def f(rng, *shape):
    return mx_ref.flush((rng.standard_normal(shape, dtype=np.float32) * np.exp2(rng.integers(-2, 3, shape[:-1] + (1,)))).astype(BF))
def wide(rng, *shape, cols=0):
    v = rng.standard_normal(shape, dtype=np.float32) * np.exp2(rng.integers(-12, 13, shape)).astype(np.float32)
    if cols: v *= np.repeat(np.exp2(rng.integers(-cols, cols + 1, shape[:-2] + (1, shape[-1] // 4))) * (rng.random(shape[:-2] + (1, shape[-1] // 4)) > 0.0625), 4, axis=-1).astype(np.float32)
    return mx_ref.flush(v.astype(BF))
C, T, R, O = 384, 96, 2, 1
def trim(v):
    v = v.astype(np.float32)
    v[np.abs(v) < np.float32(2.0 ** -14)] = 0
    return v.astype(BF)
def given(rng, u, x):
    return {"kb": np.stack([trim(u.reshape(128, 4 * C))] * N), "x": trim(x.reshape(N, 128, 4 * R * T)), "w": f(rng, N, 128, 512 * O)}
def sturdy(rng, n):
    return (1 + rng.random((128, n, 4))) * rng.choice([-1.0, 1.0], (128, n, 4)) * np.exp2(rng.integers(-1, 2, (128, 1, 1)))
def kept(v):
    m, e = np.frexp(v)
    return np.ldexp(np.trunc(m * 8) * 0.125, e)
def near(rng, u, e):
    return u[:, e] + 0.5 * sturdy(rng, len(e))
def setup_inputs(rng):
    return given(rng, f(rng, 128, 4 * C), f(rng, N, 128, 4 * R * T))
def setup_inputs_both(rng):
    u, x, new = kept(sturdy(rng, C)), np.zeros((N, 128, R, T, 4)), np.zeros((N, C), bool)
    for b in range(R):
        for j, r in enumerate(rng.permutation([v for v in range(N) if v < v ^ (1 << b)])):
            p, e = r ^ (1 << b), rng.permutation(C)
            if j % 2: e = e[np.argsort(new[r, e] | ~new[p, e], kind="stable")]
            t = e[T:2 * T] if j % 2 else rng.permutation(e[:T])
            x[r, :, b] = near(rng, u, e[:T])
            x[r, :, b, :T // 4] = u[:, e[:T // 4]]
            x[p, :, b] = near(rng, u, t)
            for s in (r, p):
                new[s, e[:T]] = True
                new[s, t] = True
    return given(rng, u, x)
def setup_inputs_few(rng):
    u, x, four = sturdy(rng, C), np.zeros((N, 128, R, T, 4)), rng.permutation(C)[:4]
    for b in range(R):
        for j, r in enumerate(rng.permutation([v for v in range(N) if v < v ^ (1 << b)])):
            a = rng.permutation(four)[:2]
            for s, c in ((r, a[0]), (r ^ (1 << b), a[j % 2])):
                x[s, :, b] = near(rng, u, np.full(T, c)) * np.exp2(rng.integers(-1, 2, (1, T, 1)))
    return given(rng, u, x)
def setup_inputs_ties(rng):
    u = np.abs(cols(f(rng, 128, 4 * (C // 4)), rng.permutation(np.arange(C) % (C // 4))).astype(np.float32))
    x = np.abs(f(rng, N, 128, 4 * R * T).astype(np.float32)).reshape(N, 128, R, T, 4)
    for r in range(N):
        for b in range(R):
            x[r, :, b] *= (1 - 2 * (rng.permutation(T) % 2)).astype(np.float32)[:, None]
            x[r, :, b, int(rng.integers(0, T))] = 0
    return given(rng, u * np.float32(2.0 ** 18), x * np.float32(2.0 ** 18))
def setup_inputs_drift(rng):
    top = (rng.permutation(128) < 64)[:, None, None]
    u, z, x = sturdy(rng, C) * top, sturdy(rng, 8) * ~top, np.zeros((N, 128, R, T, 4))
    e = rng.permutation(C)
    for r in range(N):
        for b in range(R):
            t = rng.permutation(e[:C // 2] if b == 0 else e[C // 2:])[:T]
            x[r, :, b] = near(rng, u, t) * top + 8 * z[:, rng.permutation(np.arange(T) % 8)]
    return given(rng, u, x)
def setup_inputs_spread(rng):
    d = given(rng, wide(rng, 128, 4 * C, cols=2), wide(rng, N, 128, 4 * R * T, cols=6))
    d["kb"][:, :, :4] = BF(-0.0)
    for r in range(N):
        for b in range(R):
            i = 4 * (b * T + int(rng.integers(0, T)))
            d["x"][r, :, i:i + 4] = BF(0.0)
    return d
def check_inputs(d):
    b = []
    for n, lo, hi in (("kb", -14, 24), ("x", -14, 24), ("w", -30, 30)):
        v = np.abs(d[n].astype(np.float32))
        if not (np.isfinite(v).all() and ((v == 0) | (v >= 2.0 ** lo) & (v <= 2.0 ** hi)).all()): b.append("a value of " + n)
    if (d["kb"].astype(np.float32) != d["kb"][:1].astype(np.float32)).any(): b.append("kb isn't the same on all ranks")
    return b
def numbers(k, e):
    return decode(pick(k, np.concatenate([e, np.full(-len(e) % 4, -1)]))).reshape(128, -1, 4)[:, :len(e)]
def anew(k, e, v):
    t = np.zeros((128, len(e) + -len(e) % 4, 4), np.float32)
    t[:, :len(e)] = v
    return put(k, e, pick(mx_ref.quantize(t.reshape(128, -1).astype(BF)), np.arange(len(e))))
def reference(kb, x, w):
    k = join(*[mx_ref.quantize(np.ascontiguousarray(kb[r])) for r in range(N)])
    q = join(*[mx_ref.quantize(np.ascontiguousarray(x[r])) for r in range(N)])
    dx = decode(q).reshape(128, N, R, T, 4)
    ch = np.zeros((N, R, T), np.float32)
    for b in range(R):
        won, e, t = np.zeros((N, C), bool), [], []
        for r in range(N):
            v = pick(q, (r * R + b) * T + np.arange(T))
            s = np.concatenate([mx_ref.matmul(pick(k, C * r + 128 * m + np.arange(128)), v) for m in range(C // 128)])
            win = np.argmax(s + np.float32(0), axis=0)
            u, i = np.unique(win, return_index=True)
            won[r, u] = True
            e.append(C * r + u)
            t.append(dx[:, r, b, i])
            ch[r, b] = win
        e = np.concatenate(e)
        k = anew(k, e, np.float32(0.75) * numbers(k, e) + np.float32(0.25) * np.concatenate(t, axis=1))
        src, low, high = np.arange(N * C).reshape(N, C), [], []
        for r in range(N):
            p = r ^ (1 << b)
            src[r] = np.where(won[p] & ~won[r], C * p + np.arange(C), src[r])
            if r < p:
                u = np.flatnonzero(won[r] & won[p])
                low.append(C * r + u)
                high.append(C * p + u)
        low, high = np.concatenate(low), np.concatenate(high)
        if len(low):
            v = np.float32(0.5) * numbers(k, low) + np.float32(0.5) * numbers(k, high)
            k = anew(k, np.concatenate([low, high]), np.concatenate([v, v], axis=1))
        k = pick(k, src.reshape(-1))
    oc, osc, y = np.zeros((N, 128, 4 * C), np.uint8), np.zeros((N, 16, C), np.uint8), np.zeros((N, 128, O * C), np.float32)
    for r in range(N):
        t = pick(k, C * r + np.arange(C))
        oc[r], osc[r] = emit(t)
        for o in range(O): y[r, :, C * o:C * o + C] = mx_ref.matmul(mx_ref.quantize(np.ascontiguousarray(cut(w[r], o))), t)
    return {"oc": oc, "osc": osc, "ch": ch, "y": y}

@@ -1,0 +1,448 @@
+from concourse.mybir import dt, AluOpType, AxisListType, ActivationFunctionType
+
+A = AluOpType
+AF = ActivationFunctionType
+NU, NT, NR = 384, 96, 2
+OWN, PAR, MRG, WIN = 384, 512, 640, 736
+MQ = 608
+XC, XL = 128, 102
+BIG = 16384.0
+PIECES = ((4, 0, 128), (5, 128, 256), (6, 256, NU))
+F4, F32, BF, U16, I32, U8 = "float8_e4m3fn_x4", "float32", "bfloat16", "uint16", "int32", "uint8"
+
+
+def _decl():
+    s = {}
+
+    def add(n, w, t, where="sbuf"):
+        s[n] = (where, [128, w], t)
+
+    def pair(n, w):
+        add(n, w, F4)
+        add(n + "s", w, U8)
+    for b in range(NR):
+        pair("tab%d" % b, WIN)
+        pair("xq%d" % b, 128)
+        pair("xl%d" % b, 128)
+        pair("ex%d" % b, 128)
+        add("xt%d" % b, 512, BF)
+        for n in ("lown", "lx", "land", "look"):
+            add("%s%d" % (n, b), 6, U16)
+        add("src%d" % b, 480, F32)
+        add("win%d" % b, 1, F32)
+    for n in ("e25", "e75"):
+        pair(n, 512)
+    for n in ("r16", "r1", "negw"):
+        pair(n, 128)
+        add("t" + n, 512, BF)
+    for n in ("sel", "selm", "xf", "wq"):
+        pair(n, 128)
+    pair("fin", NU)
+    for n in range(8):
+        add("ps%d" % n, 512, F32, "psum")
+    for n, w, t in (("kbt", 1536, BF), ("wt", 512, BF), ("nt", 512, BF), ("mt", 512, BF), ("xtile", 4 * XC, BF), ("ones", 128, BF),
+                    ("ident", 128, BF), ("ze", 520, BF), ("mask", XL + 1, BF), ("junk", NU, BF), ("mb", XL, BF), ("mbh", XL, BF),
+                    ("mb2", XL, BF), ("negc", 128, BF), ("cmod", 128, BF), ("iotac", 128, BF), ("eq16", 128, BF), ("ma", 16, BF),
+                    ("mc", 16, BF), ("mw", NU, BF), ("m6", 6, BF), ("cdig", 24, BF), ("pre", 24, BF),
+                    ("ip", 1, I32), ("pmi", 1, I32), ("pdi", 1, I32), ("clist", 6, U16), ("blist", 24, U16)):
+        add(n, w, t)
+    for n, w in (("jown", NT), ("jpar", NT), ("pcol", 1), ("pm", 1), ("pd", 1), ("p", NU), ("zz", 24), ("h1", 1),
+                 ("dmin", 1), ("flag", 1), ("cf", 1), ("esc0", 1), ("esc", 1), ("c1", NT), ("c2", NT), ("sg", NT),
+                 ("both", NT), ("val", NT), ("srcs", NU), ("ysb", NU)):
+        add(n, w, F32)
+    return s
+
+
+SCRATCH = _decl()
+NCOMP, NHW = 90, 30
+REMOTE = ["%s%d" % (n, b) for b in range(NR) for n in ("ae", "al", "ac")] + ["le", "ll", "lc"]
+SEMAPHORES = ["c%d" % i for i in range(NCOMP)] + ["h%d" % i for i in range(NHW)] + REMOTE
+
+
+def _clash(u, v):
+    if u[1] >= v[2] or v[1] >= u[2]:
+        return False
+    return not (u[3] == v[3] and u[3] > 1 and (u[1] - v[1]) % u[3])
+
+
+def _record(rec, queue, kind, call, reads, writes, extra=()):
+    ops, acc = rec["ops"], rec["acc"]
+    i = len(ops)
+    deps = set(extra)
+    for vs, w in ((reads, False), (writes, True)):
+        for v in vs:
+            for (u, uw, j, uq) in acc.get(v[0], []):
+                if v[0] in rec["psum"]:
+                    if uq == "tensor" and queue == "tensor":
+                        continue
+                    if uq != queue or uw:
+                        deps.add(j)
+                elif (w or uw) and _clash(u, v):
+                    deps.add(j)
+    for vs, w in ((reads, False), (writes, True)):
+        for v in vs:
+            acc.setdefault(v[0], []).append((v, w, i, queue))
+    if kind == "arr" and deps:
+        raise ValueError("a landing buffer is in use")
+    known = rec["known"].setdefault(queue, set()) if kind != "arr" else set()
+    waits = []
+    for j in sorted(deps, reverse=True):
+        if j not in known:
+            waits.append(j)
+            known.add(j)
+            known |= ops[j]["known"]
+    ops.append({"queue": queue, "kind": kind, "call": call, "waits": waits, "known": set(known), "need": False})
+    for j in waits:
+        ops[j]["need"] = True
+    return i
+
+
+def _issue(rec, queues, sems):
+    ops = rec["ops"]
+    last, total = {}, {}
+    for i, o in enumerate(ops):
+        if o["kind"] == "arr":
+            o["sem"], o["val"] = o["call"]
+            continue
+        q = queues[o["queue"]]
+        for j in reversed(o["waits"]):
+            q.wait_ge(sems[ops[j]["sem"]], ops[j]["val"])
+        if o["kind"] == "end":
+            continue
+        ins = o["call"](q)
+        if not o["need"] or o["kind"] == "remote":
+            continue
+        pool = ["h%d" % k for k in range(NHW)] if o["kind"] == "dma" else ["c%d" % k for k in range(NCOMP)]
+        name = None
+        for s in pool:
+            if s not in last or last[s] in o["known"]:
+                name = s
+                break
+        if name is None:
+            raise ValueError("out of semaphores")
+        n = 16 if o["kind"] == "dma" else 1
+        ins.then_inc(sems[name], n)
+        last[name] = i
+        total[name] = total.get(name, 0) + n
+        o["sem"], o["val"] = name, total[name]
+
+
+def V(name, a, b, s=1):
+    return (name, a, b, s)
+
+
+def rank_program(g, core, T, topo):
+    rank = T.rank_of(core)
+    if rank is None:
+        return
+    rec = {"ops": [], "acc": {}, "known": {}, "psum": ["ps%d" % n for n in range(8)]}
+
+    def ap(v):
+        return T[v[0]][:, v[1]:v[2]] if v[3] == 1 else T[v[0]][:, v[1]:v[2]:v[3]]
+
+    def sc(v):
+        return (v[0] + "s", v[1], v[2], 1)
+
+    def views(*xs):
+        return [x for x in xs if isinstance(x, tuple)]
+
+    def val(x):
+        return ap(x) if isinstance(x, tuple) else x
+
+    def lanes(src, dst):
+        return topo.engines(src, dst)[::2]
+
+    def memset(out, c):
+        _record(rec, "vector", "comp", lambda q: q.memset(ap(out), c), [], [out])
+
+    def copy(out, in_, queue="vector", scale=None, bias=None, off=None, func=None):
+        src = (lambda: ap(in_)) if off is None else (lambda: ap(in_).indirect(ap(off)))
+        if queue == "vector":
+            _record(rec, "vector", "comp", lambda q: q.tensor_copy(ap(out), src()), views(in_, off), [out])
+            return
+        f = func or (AF.Copy if bias is None else AF.Identity)
+        kw = {}
+        if scale is not None:
+            kw["scale"] = val(scale)
+        if bias is not None:
+            kw["bias"] = bias
+        _record(rec, "scalar", "comp", lambda q: q.activation(ap(out), src(), f, **kw), views(in_, scale, off), [out])
+
+    def ts(out, in0, s1, op0, s2=None, op1=None):
+        def call(q):
+            if op1 is None:
+                return q.tensor_scalar(ap(out), ap(in0), val(s1), None, op0)
+            return q.tensor_scalar(ap(out), ap(in0), val(s1), val(s2), op0, op1)
+        _record(rec, "vector", "comp", call, views(in0, s1, s2), [out])
+
+    def tt(out, in0, in1, op):
+        _record(rec, "vector", "comp", lambda q: q.tensor_tensor(ap(out), ap(in0), ap(in1), op), [in0, in1], [out])
+
+    def scatter(win, off, in_):
+        _record(rec, "vector", "comp", lambda q: q.tensor_copy(ap(win).indirect(ap(off)), ap(in_)), [win, off, in_], [win])
+
+    def reduce(out, in_, op, absv=False):
+        def call(q):
+            if absv:
+                return q.tensor_reduce(ap(out), ap(in_), AxisListType.X, op, apply_absolute_value=True)
+            return q.tensor_reduce(ap(out), ap(in_), AxisListType.X, op)
+        _record(rec, "vector", "comp", call, [in_], [out])
+
+    def scan(out, d0, d1, init, op0, op1):
+        _record(rec, "vector", "comp", lambda q: q.tensor_tensor_scan(ap(out), ap(d0), ap(d1), val(init), op0, op1),
+                views(d0, d1, init), [out])
+
+    def quant(out, in_):
+        _record(rec, "vector", "comp", lambda q: q.quantize_mx(ap(out), ap(sc(out)), ap(in_)), [in_], [out, sc(out)])
+
+    def mm(ps, w, x, start=True, stop=True):
+        n = x[2] - x[1]
+        _record(rec, "tensor", "comp",
+                lambda q: q.matmul_mx(T["ps%d" % ps][:, 0:n], ap(w), ap(sc(w)), ap(x), ap(sc(x)), start, stop),
+                [w, sc(w), x, sc(x)], [V("ps%d" % ps, 0, n)])
+
+    def pick(out, win, off):
+        _record(rec, "vector", "comp",
+                lambda q: q.tensor_copy(ap(out).bitcast(dt.uint32), ap(win).bitcast(dt.uint32).indirect(ap(off))), [win, off], [out])
+        _record(rec, "scalar", "comp", lambda q: q.activation(ap(sc(out)), ap(sc(win)).indirect(ap(off)), AF.Copy),
+                [sc(win), off], [sc(out)])
+
+    def iota(out, pattern, base, cm):
+        f = SCRATCH[out[0]][2] != I32
+
+        def call(q):
+            if f:
+                return q.iota(ap(out), pattern, base, cm, allow_small_or_imprecise_dtypes=True)
+            return q.iota(ap(out), pattern, base, cm)
+        _record(rec, "gpsimd", "comp", call, [], [out])
+
+    def load(queue, out, src, after=()):
+        return _record(rec, queue, "dma", lambda q: q.dma_start(ap(out), src), [], [out], after)
+
+    def lay(out, in_):
+        _record(rec, "sync", "dma", lambda q: q.dma_start(ap(out).bitcast(dt.uint8), ap(in_).bitcast(dt.uint8)), [in_], [out])
+        _record(rec, "sync", "dma", lambda q: q.dma_start(ap(sc(out)), ap(sc(in_))), [sc(in_)], [sc(out)])
+
+    stores = []
+
+    def store(queue, dst, in_, view):
+        stores.append(_record(rec, queue, "dma", lambda q: q.dma_start(dst, view), [in_], []))
+
+    def send(dst, out, in_, arr, loc):
+        rid, pid, _s = topo.addr(dst)
+        codes = SCRATCH[in_[0]][2] == F4
+
+        def call(q):
+            o, i = ap(out), ap(in_)
+            if codes:
+                o, i = o.bitcast(dt.uint8), i.bitcast(dt.uint8)
+            return q.remote_dma(o, i, T.sem[arr], T.sem[loc], pid, rid, sum(1 << e for e in lanes(core, dst)))
+        _record(rec, "gpsimd", "remote", call, [in_], [])
+
+    def arrive(writes, sem, src, calls=1):
+        _record(rec, "network", "arr", (sem, calls * len(lanes(src, core))), [], writes)
+
+    load("sync", V("xt0", 0, 384), T.x[:, 0:384])
+    load("scalar", V("kbt", 0, 512), T.kb[:, 0:512])
+    load("sync", V("kbt", 512, 1024), T.kb[:, 512:1024])
+    kb2 = load("sync", V("kbt", 1024, 1536), T.kb[:, 1024:1536])
+
+    iota(V("ip", 0, 1), [[0, 1]], 0, 1)
+    memset(V("ones", 0, 128), 1.0)
+    _record(rec, "gpsimd", "comp", lambda q: q.affine_select(T.ident[:, 0:128], T.ones[:, 0:128], [[-1, 128]], A.is_equal, 0.0, 0, 1),
+            [V("ones", 0, 128)], [V("ident", 0, 128)])
+    iota(V("cmod", 0, 128), [[0, 8], [1, 16]], 0, 0)
+    iota(V("pcol", 0, 1), [[0, 1]], 0, 1)
+    iota(V("iotac", 0, 128), [[1, 128]], 0, 0)
+    iota(V("jown", 0, NT), [[1, NT]], OWN, 0)
+    iota(V("src0", 0, 480), [[1, 480]], 0, 0)
+    iota(V("jpar", 0, NT), [[1, NT]], (PAR + MRG) // 2, 0)
+    iota(V("src1", 0, 480), [[1, 480]], 0, 0)
+    memset(V("ze", 0, 520), 0.0)
+    copy(V("ze", 4, 516, 4), V("ident", 0, 128), "scalar", scale=0.25)
+    memset(V("xt0", 384, 512), 0.0)
+    memset(V("negc", 0, 128), -1e29)
+    ts(V("pmi", 0, 1), V("ip", 0, 1), 15, A.bitwise_and)
+    ts(V("pdi", 0, 1), V("ip", 0, 1), 4, A.logical_shift_right)
+    memset(V("xtile", 4 * XL, 4 * XC), 0.0)
+    copy(V("pm", 0, 1), V("pmi", 0, 1))
+    copy(V("pd", 0, 1), V("pdi", 0, 1))
+    memset(V("xtile", 4 * NT + 3, 4 * XL, 4), 0.0)
+    copy(V("xtile", 3, 4 * NT, 4), V("ident", 0, NT), "scalar")
+    copy(V("mask", 0, NT), V("ident", 0, NT), "scalar")
+
+    def etile(n, t):
+        quant(V(n, 128 * t, 128 * t + 128), V("ze", 4 - t, 516 - t))
+
+    def score(b, ps, u, v):
+        mm(ps, V("xq%d" % b, 0, 128), V("tab%d" % b, u, v))
+
+    def run_max(ps, u, v):
+        scan(V("p", u, v), V("ps%d" % ps, 0, v - u), V("negc", 0, v - u), V("p", u - 1, u) if u else -1e29, A.max, A.max)
+
+    def units(ps, u, v):
+        quant(V("tab0", u, v), V("kbt", 4 * u, 4 * v))
+        score(0, ps, u, v)
+
+    quant(V("xq0", 0, 128), V("xt0", 0, 512))
+    lay(V("sel", 96, 128), V("xq0", 96, 128))
+    lay(V("selm", 0, 32), V("xq0", 96, 128))
+    for b in range(NR):
+        lay(V("ex%d" % b, 6, 128), V("xq0", 0, 122))
+    load("sync", V("xt1", 0, 384), T.x[:, 384:768], [kb2])
+    load("sync", V("wt", 0, 512), T.w[:, 0:512], [kb2])
+    etile("e25", 0)
+    units(*PIECES[0])
+    etile("e25", 1)
+    units(*PIECES[1])
+    ts(V("eq16", 0, 128), V("cmod", 0, 128), V("pm", 0, 1), A.is_equal)
+    for t in range(4):
+        copy(V("tr16", t, 512, 4), V("eq16", 0, 128), "scalar", scale=16.0 if t == 3 else 1.0)
+    run_max(*PIECES[0])
+    units(*PIECES[2])
+    ts(V("mask", NT, XL + 1), V("iotac", 0, 7), V("pd", 0, 1), A.is_equal)
+    copy(V("mb", 0, XL), V("mask", 0, XL), "scalar", scale=1024.0, bias=-1024.0)
+    copy(V("mb2", 0, XL), V("mask", 0, XL), "scalar", scale=1024.0, bias=-1024.0 - 192.0)
+    run_max(*PIECES[1])
+    memset(V("tnegw", 0, 512), -1.0)
+    run_max(*PIECES[2])
+    memset(V("tnegw", 3, 512, 4), 0.0)
+    etile("e25", 2)
+
+    for b in range(NR):
+        tab, xq, nxt = "tab%d" % b, "xq%d" % b, "tab%d" % (b + 1) if b + 1 < NR else "fin"
+        win, src = "win%d" % b, V("src%d" % b, 0, 480)
+        lown, lx, land, look = [V("%s%d" % (n, b), 0, 6) for n in ("lown", "lx", "land", "look")]
+        xl, ex = V("xl%d" % b, 0, XC), V("ex%d" % b, 0, 128)
+        partner = T.cores[rank ^ (1 << b)]
+
+        def tokens(xq=xq):
+            for t in range(4):
+                mm(t, V("e25", 128 * t, 128 * t + 128), V(xq, 0, 128), True, False)
+
+        if b == 1:
+            tokens()
+        last = V("p", NU - 1, NU)
+        _record(rec, "scalar", "comp",
+                lambda q, w=win: q.activation(T.junk[:, 0:NU], T.p[:, 0:NU], AF.Sign, bias=T.p[:, NU - 1:NU], scale=-1.0,
+                                              accum_out=T[w][:, 0:1]), [V("p", 0, NU)], [V("junk", 0, NU), V(win, 0, 1)])
+        ts(V("zz", 0, 24), V("p", 15, NU, 16), last, A.is_lt, 16.0, A.mult)
+        if b == 0:
+            etile("e25", 3)
+        reduce(V("h1", 0, 1), V("zz", 0, 24), A.add)
+        if b == 0:
+            quant(V("r16", 0, 128), V("tr16", 0, 512))
+        ts(V("mbh", 0, XL), V("mb", 0, XL), V("h1", 0, 1), A.subtract)
+        ts(V("xtile", 1, 4 * XL, 4), V("mask", 0, XL), V("h1", 0, 1), A.mult, 192.0, A.min)
+        _record(rec, "scalar", "comp", lambda q: q.activation(T.xtile[:, 2:4 * XL:4], T.mb2[:, 0:XL], AF.Relu, bias=T.h1[:, 0:1]),
+                [V("mb2", 0, XL), V("h1", 0, 1)], [V("xtile", 2, 4 * XL, 4)])
+        if b == 0:
+            copy(V("ze", 4, 516, 4), V("ident", 0, 128), "scalar", scale=0.75)
+            for t in range(3):
+                copy(V("tr1", t, 512, 4), V("eq16", 0, 128), "scalar", scale=0.0, bias=1.0)
+            copy(V("ma", 0, 16), V("eq16", 0, 16), "scalar", scale=-1.0, bias=1.0)
+            copy(V("mc", 0, 1), V("eq16", 0, 1), "scalar", scale=0.0)
+            copy(V("mc", 1, 16), V("eq16", 0, 15), "scalar", scale=BIG)
+            copy(V("cf", 0, 1), V("pd", 0, 1), "scalar", bias=-5.0, func=AF.Relu)
+            copy(V("esc0", 0, 1), V("pm", 0, 1), "scalar", bias=-14.0, func=AF.Relu)
+            for n, c in (("nt", 4 * NT), ("mt", 0), ("xt1", 384)):
+                copy(V(n, c, c + 128), V("eq16", 0, 128), "scalar", scale=0.0)
+            copy(V("esc", 0, 1), V("esc0", 0, 1), "scalar", scale=1.0 - 1.0 / BIG, bias=1.0 / BIG)
+            ts(V("m6", 0, 6), V("mask", NT, XL), V("mask", XL, XL + 1), A.subtract)
+        ts(V("xtile", 0, 4 * XL, 4), V("mbh", 0, XL), V(win, 0, 1), A.add, 0.0, A.max)
+        if b == 0:
+            ts(V("tr1", 3, 512, 4), V("iotac", 0, 128), V("pcol", 0, 1), A.is_le, 512.0, A.mult)
+            tt(V("cdig", 3, 24, 4), V("m6", 0, 6), V("iotac", 0, 6), A.mult)
+            copy(V("cdig", 0, 24, 4), V("m6", 0, 6), "scalar", scale=V("pm", 0, 1))
+            copy(V("cdig", 1, 24, 4), V("m6", 0, 6), "scalar", scale=192.0)
+            copy(V("cdig", 2, 24, 4), V("m6", 0, 6), "scalar", scale=192.0)
+        quant(xl, V("xtile", 0, 4 * XC))
+        for x in ("", "s"):
+            send(partner, V(ex[0] + x, 0, 6), V(xl[0] + x, NT, XL), "ae%d" % b, "le")
+        mm(5, V("r16", 0, 128), xl)
+        if b == 0:
+            etile("e75", 0)
+            etile("e75", 1)
+            tokens()
+        else:
+            tt(V("pre", 0, 24), V("xtile", 4 * NT, 4 * XL), V("cdig", 0, 24), A.subtract)
+        copy(lown, V("ps5", NT, XL))
+        if b == 0:
+            quant(V("r1", 0, 128), V("tr1", 0, 512))
+        pick(V("sel", 0, NT), V(tab, 0, NU), lown)
+        if b == 0:
+            quant(V("negw", 0, 128), V("tnegw", 0, 512))
+        mm(6, V("r1", 0, 128), xl, True, False)
+        mm(6, xl, V("negw", 0, 128), False, True)
+        if b == 0:
+            etile("e75", 2)
+            etile("e75", 3)
+            tt(V("mw", 0, 16), V("ma", 0, 16), V("mc", 0, 16), A.max)
+            tt(V("pre", 0, 24), V("xtile", 4 * NT, 4 * XL), V("cdig", 0, 24), A.subtract)
+        for t in range(4):
+            mm(t, V("e75", 128 * t, 128 * t + 128), V("sel", 0, 128), False, True)
+        reduce(V("dmin", 0, 1), V("ps6", 0, NT), A.min, absv=True)
+        ts(V("flag", 0, 1), V("dmin", 0, 1), 1.0, A.min, V("cf", 0, 1), A.max)
+        ts(V("xtile", 4 * XL, 4 * XL + 24), V("pre", 0, 24), V("flag", 0, 1), A.mult)
+        quant(V("xf", 0, 128), V("xtile", 0, 512))
+        arrive([V(ex[0], 0, 6), V(ex[0] + "s", 0, 6)], "ae%d" % b, partner, 2)
+        mm(4, V("r16", 0, 128), ex)
+        mm(7, V("r16", 0, 128), V("xf", 0, 128))
+        for t in range(3):
+            copy(V("nt", t, 4 * NT, 4), V("ps%d" % t, 0, NT), "scalar")
+        copy(V("nt", 3, 4 * NT, 4), V("ps3", 0, NT))
+        quant(V(tab, OWN, OWN + 128), V("nt", 0, 512))
+        for x in (tab, tab + "s"):
+            send(partner, V(x, PAR, PAR + NT), V(x, OWN, OWN + NT), "ac%d" % b, "lc")
+        copy(lx, V("ps7", XL, XL + 6))
+        send(partner, land, lx, "al%d" % b, "ll")
+        store("sync", T.ch[b:b + 1, 0:NT], V(win, 0, 1), T[win][0:NT, 0:1])
+        if b == 0:
+            for c, n in ((16, 16), (32, 32), (64, 64), (128, 128), (256, 128)):
+                copy(V("mw", c, c + n), V("mw", 0, n), "scalar")
+        copy(look, V("ps4", 0, 6))
+        scatter(src, lx, V("jown", 0, NT))
+        arrive([land], "al%d" % b, partner)
+        arrive([V(tab, PAR, PAR + NT), V(tab + "s", PAR, PAR + NT)], "ac%d" % b, partner, 2)
+        copy(V("c1", 0, NT), src, off=look)
+        copy(V("sg", 0, NT), src, "scalar", bias=0.5 - OWN, off=look, func=AF.Sign)
+        copy(V("both", 0, NT), V("sg", 0, NT), "scalar", scale=(MRG - PAR) / 2.0)
+        scan(V("c2", 0, NT), V("mw", 0, NT), V("c1", 0, NT), 0.0, A.mult, A.add)
+        if b == 0:
+            quant(V("xq1", 0, 128), V("xt1", 0, 512))
+        else:
+            quant(V("wq", 0, 128), V("wt", 0, 512))
+        ts(V("clist", 0, 6), V("c2", 15, NT, 16), V("esc", 0, 1), A.mult, -0.34, A.add)
+        tt(V("val", 0, NT), V("both", 0, NT), V("jpar", 0, NT), A.add)
+        pick(V("selm", 32, 128), V(tab, 0, PAR), V("clist", 0, 6))
+        for k, x in enumerate((V(tab, PAR - 32, PAR + NT), V("selm", 0, 128))):
+            for t in range(4):
+                mm(t, V("e25", 128 * t, 128 * t + 128), x, k == 0, k == 1)
+        scatter(src, land, V("val", 0, NT))
+        scan(V("srcs", 0, NU), V("mw", 0, NU), V(src[0], 0, NU), 0.0, A.mult, A.add)
+        ts(V("blist", 0, 24), V("srcs", 15, NU, 16), V("esc", 0, 1), A.mult, -0.34, A.add)
+        for t in range(4):
+            copy(V("mt", 128 + t, 512, 4), V("ps%d" % t, 32, 128), "scalar", scale=2.0)
+        quant(V(tab, MQ, MQ + 128), V("mt", 0, 512))
+        for ps, u, v in PIECES:
+            pick(V(nxt, u, v), V(tab, 0, WIN), V("blist", u // 16, v // 16))
+            if b + 1 < NR:
+                score(b + 1, ps, u, v)
+        if b + 1 < NR:
+            for piece in PIECES:
+                run_max(*piece)
+
+    for ps, u, v in PIECES:
+        mm(ps, V("wq", 0, 128), V("fin", u, v))
+        store("sync", T.oc[:, 4 * u:4 * v], V("fin", u, v), T.fin[:, u:v].bitcast(dt.uint8))
+    for ps, u, v in PIECES:
+        copy(V("ysb", u, v), V("ps%d" % ps, 0, v - u), "scalar" if u == 128 else "vector")
+        store("sync", T.y[:, u:v], V("ysb", u, v), T.ysb[:, u:v])
+    for k in range(4):
+        store("scalar", T.osc[4 * k:4 * k + 4, 0:NU], V("fins", 0, NU), T.fins[32 * k:32 * k + 4, 0:NU])
+    _record(rec, "sync", "end", None, [], [], stores)
+    _issue(rec, {"vector": g.vector, "scalar": g.scalar, "tensor": g.tensor, "gpsimd": g, "sync": g.sync}, T.sem)
+    n = sum(len(lanes(core, T.cores[rank ^ (1 << b)])) for b in range(NR))
+    g.wait_ge(T.sem.ll, n)
+    g.wait_ge(T.sem.le, 2 * n)
+    g.wait_ge(T.sem.lc, 2 * n)

@@ -1,14 +1,28 @@
+import math
+from concourse.bass import DstId, RemoteDMATransfer
 from concourse.mybir import dt, AluOpType, AxisListType, ActivationFunctionType
 
 A = AluOpType
 AF = ActivationFunctionType
 NU, NT, NR = 384, 96, 2
-OWN, PAR, MRG, WIN = 384, 512, 640, 736
-MQ = 608
-XC, XL = 128, 102
+OWN, PAR, MRG, WIN = 384, 512, 608, 736
+XQ, SM = 96, 224
+ONE, MK, LX, EX = 96, 98, 122, 128
+MT, NTL, X0, ZZ, X1, KB = 0, 384, 768, 1152, 1280, 1664
 BIG = 16384.0
-PIECES = ((4, 0, 128), (5, 128, 256), (6, 256, NU))
 F4, F32, BF, U16, I32, U8 = "float8_e4m3fn_x4", "float32", "bfloat16", "uint16", "int32", "uint8"
+OPT = {"load": (256, 128), "tab": (128, 128, 128), "fin": (256, 128), "early": ("list", "codes"), "hact": (0, 0), "ownfirst": (1, 1),
+       "ntq": "sssv", "mtq": "svsv", "c1q": "scalar", "ocwhole": 0, "yq": "vs", "lq": ("sync", "scalar", "sync", "sync"), "cq": "svvs",
+       "merge": "BB", "gq": "ssss", "dq": "ssss", "re": 1, "valq": "v"}
+ORDER = [0, 1, 6, 12, 2, 5, 32, 16, 15, 23, 7, 17, 33, 13, 14, 25, 8, 58, 28, 37, 18, 38, 57, 9, 56, 21, 44, 30, 36, 67, 46, 45, 10, 22, 70, 40,
+         20, 35, 29, 39, 24, 19, 71, 4, 31, 3, 73, 74, 72, 11, 78, 55, 75, 26, 76, 59, 80, 81, 77, 64, 79, 82, 47, 34, 83, 53, 84, 86, 41, 27,
+         43, 85, 48, 65, 54, 42, 87, 49, 66, 50, 62, 88, 63, 93, 89, 94, 99, 90, 92, 100, 91, 51, 101, 98, 102, 97, 60, 61, 104, 108, 95, 52,
+         105, 96, 109, 106, 114, 113, 107, 103, 110, 68, 117, 112, 122, 115, 111, 124, 118, 123, 119, 126, 121, 125, 128, 127, 120, 138, 130,
+         116, 135, 129, 134, 131, 139, 137, 136, 133, 132, 141, 143, 144, 142, 160, 140, 158, 145, 159, 147, 146, 150, 151, 148, 154, 155, 152,
+         149, 156, 153, 161, 157, 163, 162, 164, 165, 166, 168, 167, 169, 69, 181, 171, 170, 175, 172, 176, 174, 173, 182, 179, 185, 183, 177,
+         184, 190, 178, 188, 180, 189, 186, 191, 187, 192, 195, 196, 194, 204, 193, 206, 208, 199, 210, 197, 205, 207, 200, 211, 201, 209, 203,
+         198, 213, 202, 217, 220, 212, 219, 215, 218, 223, 216, 221, 214, 226, 225, 224, 222, 227, 228, 229, 230, 231, 238, 232, 239, 241, 243,
+         235, 240, 242, 233, 236, 234, 237, 244]
 
 
 def _decl():
@@ -22,85 +36,95 @@ def _decl():
         add(n + "s", w, U8)
     for b in range(NR):
         pair("tab%d" % b, WIN)
-        pair("xq%d" % b, 128)
+        pair("xq%d" % b, SM + NT)
         pair("xl%d" % b, 128)
-        pair("ex%d" % b, 128)
-        add("xt%d" % b, 512, BF)
-        for n in ("lown", "lx", "land", "look"):
-            add("%s%d" % (n, b), 6, U16)
+        pair("xf%d" % b, EX + 32)
+        for n in ("lown", "land", "look"):
+            add("%s%d" % (n, b), 8, U16)
+        add("lx%d" % b, 12, U16)
         add("src%d" % b, 480, F32)
         add("win%d" % b, 1, F32)
     for n in ("e25", "e75"):
         pair(n, 512)
+        add("t" + n, 520, BF)
     for n in ("r16", "r1", "negw"):
         pair(n, 128)
         add("t" + n, 512, BF)
-    for n in ("sel", "selm", "xf", "wq"):
-        pair(n, 128)
+    pair("wq", 128)
     pair("fin", NU)
     for n in range(8):
         add("ps%d" % n, 512, F32, "psum")
-    for n, w, t in (("kbt", 1536, BF), ("wt", 512, BF), ("nt", 512, BF), ("mt", 512, BF), ("xtile", 4 * XC, BF), ("ones", 128, BF),
-                    ("ident", 128, BF), ("ze", 520, BF), ("mask", XL + 1, BF), ("junk", NU, BF), ("mb", XL, BF), ("mbh", XL, BF),
-                    ("mb2", XL, BF), ("negc", 128, BF), ("cmod", 128, BF), ("iotac", 128, BF), ("eq16", 128, BF), ("ma", 16, BF),
-                    ("mc", 16, BF), ("mw", NU, BF), ("m6", 6, BF), ("cdig", 24, BF), ("pre", 24, BF),
-                    ("ip", 1, I32), ("pmi", 1, I32), ("pdi", 1, I32), ("clist", 6, U16), ("blist", 24, U16)):
+    for n, w, t in (("tl", KB + 4 * NU, BF), ("wt", 512, BF), ("xtile", 512, BF), ("dd", 128, BF), ("mask", MK + 6, BF), ("junk", 2 * NU, BF),
+                    ("dg", NU, BF), ("junk2", 36, BF), ("mb", MK + 6, BF), ("mbh", MK + 6, BF), ("cmod", 128, BF), ("eq16", 128, BF), ("ma", 16, BF),
+                    ("mb16", MK + 6, BF), ("mc", 16, BF), ("mw", NU, BF), ("cdig", 24, BF), ("pre", 24, BF),
+                    ("ip", 1, I32), ("pi", 2, I32), ("clist", 6, U16), ("blist", 24, U16)):
         add(n, w, t)
-    for n, w in (("jown", NT), ("jpar", NT), ("pcol", 1), ("pm", 1), ("pd", 1), ("p", NU), ("zz", 24), ("h1", 1),
-                 ("dmin", 1), ("flag", 1), ("cf", 1), ("esc0", 1), ("esc", 1), ("c1", NT), ("c2", NT), ("sg", NT),
+    for n, w in (("jown", NT), ("jpar", NT), ("pf", 2), ("p", NU + 192), ("zz", 25), ("h1", 1),
+                 ("flag", 1), ("esc0", 1), ("esc", 1), ("c1", NT), ("c2", NT), ("sg", NT),
                  ("both", NT), ("val", NT), ("srcs", NU), ("ysb", NU)):
         add(n, w, F32)
     return s
 
 
 SCRATCH = _decl()
-NCOMP, NHW = 90, 30
+NCOMP, NHW = 100, 24
 REMOTE = ["%s%d" % (n, b) for b in range(NR) for n in ("ae", "al", "ac")] + ["le", "ll", "lc"]
 SEMAPHORES = ["c%d" % i for i in range(NCOMP)] + ["h%d" % i for i in range(NHW)] + REMOTE
 
 
 def _clash(u, v):
-    if u[1] >= v[2] or v[1] >= u[2]:
+    if u[1] >= v[2] or v[1] >= u[2] or u[4] >= v[5] or v[4] >= u[5]:
         return False
-    return not (u[3] == v[3] and u[3] > 1 and (u[1] - v[1]) % u[3])
+    return (u[1] - v[1]) % math.gcd(u[3], v[3]) == 0
 
 
-def _record(rec, queue, kind, call, reads, writes, extra=()):
+def _record(rec, queue, kind, call, reads, writes, extra=(), tag=None):
     ops, acc = rec["ops"], rec["acc"]
     i = len(ops)
-    deps = set(extra)
+    deps, soft = set(extra), set()
     for vs, w in ((reads, False), (writes, True)):
         for v in vs:
             for (u, uw, j, uq) in acc.get(v[0], []):
-                if v[0] in rec["psum"]:
+                if v[0][:2] == "ps":
                     if uq == "tensor" and queue == "tensor":
-                        continue
-                    if uq != queue or uw:
+                        soft.add(j)
+                    elif uq != queue or uw:
                         deps.add(j)
                 elif (w or uw) and _clash(u, v):
                     deps.add(j)
     for vs, w in ((reads, False), (writes, True)):
         for v in vs:
             acc.setdefault(v[0], []).append((v, w, i, queue))
-    if kind == "arr" and deps:
-        raise ValueError("a landing buffer is in use")
-    known = rec["known"].setdefault(queue, set()) if kind != "arr" else set()
-    waits = []
-    for j in sorted(deps, reverse=True):
-        if j not in known:
-            waits.append(j)
-            known.add(j)
-            known |= ops[j]["known"]
-    ops.append({"queue": queue, "kind": kind, "call": call, "waits": waits, "known": set(known), "need": False})
-    for j in waits:
-        ops[j]["need"] = True
+    if kind == "arr":
+        if deps:
+            raise ValueError("a landing buffer is in use")
+        soft = set(j for j in range(i) if ops[j]["tag"] == call[0])
+    ops.append({"queue": queue, "kind": kind, "call": call, "deps": deps, "soft": soft, "need": False, "tag": tag,
+                "out": writes[0] if writes else (reads[0] if reads else None)})
     return i
 
 
-def _issue(rec, queues, sems):
-    ops = rec["ops"]
+def _issue(ops, order, queues, sems):
+    place = {j: k for k, j in enumerate(order)}
+    if len(place) != len(ops):
+        raise ValueError("the order doesn't name every call once")
+    seen = {}
+    for i in order:
+        o = ops[i]
+        if any(place[j] > place[i] for j in o["deps"] | o["soft"]):
+            raise ValueError("the order puts a call ahead of what it needs")
+        known = seen.setdefault(o["queue"], set()) if o["kind"] != "arr" else set()
+        o["waits"] = []
+        for j in sorted(o["deps"], key=lambda j: -place[j]):
+            if j not in known:
+                o["waits"].append(j)
+                known.add(j)
+                known |= ops[j]["known"]
+                ops[j]["need"] = True
+        o["known"] = set(known)
     last, total = {}, {}
-    for i, o in enumerate(ops):
+    for i in order:
+        o = ops[i]
         if o["kind"] == "arr":
             o["sem"], o["val"] = o["call"]
             continue
@@ -127,21 +151,24 @@ def _issue(rec, queues, sems):
         o["sem"], o["val"] = name, total[name]
 
 
-def V(name, a, b, s=1):
-    return (name, a, b, s)
+def V(name, a, b, s=1, p0=0, p1=128):
+    return (name, a, b, s, p0, p1)
 
 
-def rank_program(g, core, T, topo):
+def _cut(sizes):
+    return [(sum(sizes[:k]), sum(sizes[:k + 1])) for k in range(len(sizes))]
+
+
+def _calls(core, T, topo):
     rank = T.rank_of(core)
-    if rank is None:
-        return
-    rec = {"ops": [], "acc": {}, "known": {}, "psum": ["ps%d" % n for n in range(8)]}
+    rec = {"ops": [], "acc": {}}
+    local = {"le": 0, "ll": 0, "lc": 0}
 
     def ap(v):
-        return T[v[0]][:, v[1]:v[2]] if v[3] == 1 else T[v[0]][:, v[1]:v[2]:v[3]]
+        return T[v[0]][v[4]:v[5], v[1]:v[2]] if v[3] == 1 else T[v[0]][v[4]:v[5], v[1]:v[2]:v[3]]
 
     def sc(v):
-        return (v[0] + "s", v[1], v[2], 1)
+        return V(v[0] + "s", v[1], v[2])
 
     def views(*xs):
         return [x for x in xs if isinstance(x, tuple)]
@@ -149,15 +176,16 @@ def rank_program(g, core, T, topo):
     def val(x):
         return ap(x) if isinstance(x, tuple) else x
 
-    def lanes(src, dst):
-        return topo.engines(src, dst)[::2]
-
     def memset(out, c):
         _record(rec, "vector", "comp", lambda q: q.memset(ap(out), c), [], [out])
 
-    def copy(out, in_, queue="vector", scale=None, bias=None, off=None, func=None):
+    def copy(out, in_, queue="vector", scale=None, bias=None, off=None, func=None, accum=None):
         src = (lambda: ap(in_)) if off is None else (lambda: ap(in_).indirect(ap(off)))
         if queue == "vector":
+            if bias is not None:
+                return ts(out, in_, scale, A.mult, bias, A.add)
+            if scale is not None:
+                return ts(out, in_, scale, A.mult)
             _record(rec, "vector", "comp", lambda q: q.tensor_copy(ap(out), src()), views(in_, off), [out])
             return
         f = func or (AF.Copy if bias is None else AF.Identity)
@@ -165,8 +193,10 @@ def rank_program(g, core, T, topo):
         if scale is not None:
             kw["scale"] = val(scale)
         if bias is not None:
-            kw["bias"] = bias
-        _record(rec, "scalar", "comp", lambda q: q.activation(ap(out), src(), f, **kw), views(in_, scale, off), [out])
+            kw["bias"] = val(bias)
+        if accum is not None:
+            kw["accum_out"] = ap(accum)
+        _record(rec, "scalar", "comp", lambda q: q.activation(ap(out), src(), f, **kw), views(in_, scale, bias, off), views(accum, out))
 
     def ts(out, in0, s1, op0, s2=None, op1=None):
         def call(q):
@@ -219,230 +249,238 @@ def rank_program(g, core, T, topo):
     def load(queue, out, src, after=()):
         return _record(rec, queue, "dma", lambda q: q.dma_start(ap(out), src), [], [out], after)
 
-    def lay(out, in_):
-        _record(rec, "sync", "dma", lambda q: q.dma_start(ap(out).bitcast(dt.uint8), ap(in_).bitcast(dt.uint8)), [in_], [out])
-        _record(rec, "sync", "dma", lambda q: q.dma_start(ap(sc(out)), ap(sc(in_))), [sc(in_)], [sc(out)])
-
     stores = []
 
     def store(queue, dst, in_, view):
         stores.append(_record(rec, queue, "dma", lambda q: q.dma_start(dst, view), [in_], []))
 
+    def raw(v):
+        return ap(v).bitcast(dt.uint8) if SCRATCH[v[0]][2] == F4 else ap(v)
+
     def send(dst, out, in_, arr, loc):
         rid, pid, _s = topo.addr(dst)
-        codes = SCRATCH[in_[0]][2] == F4
+        local[loc] += len(topo.engines(core, dst))
+        _record(rec, "gpsimd", "remote", lambda q: q.remote_dma(raw(out), raw(in_), T.sem[arr], T.sem[loc], pid, rid, topo.mask(core, dst)),
+                [in_], [], tag=arr)
+
+    def send2(dst, outs, ins, arr, loc):
+        rid, pid, _s = topo.addr(dst)
+        es = topo.engines(core, dst)
+        local[loc] += len(es)
 
         def call(q):
-            o, i = ap(out), ap(in_)
-            if codes:
-                o, i = o.bitcast(dt.uint8), i.bitcast(dt.uint8)
-            return q.remote_dma(o, i, T.sem[arr], T.sem[loc], pid, rid, sum(1 << e for e in lanes(core, dst)))
-        _record(rec, "gpsimd", "remote", call, [in_], [])
+            return q.remote_dma_fused([RemoteDMATransfer(dst_ids=[DstId(rid=rid, pnc=pid)], dma_engine_mask=sum(1 << e for e in es[k::2]),
+                                                         remote_sem=T.sem[arr], src=raw(ins[k]), dst=raw(outs[k])) for k in range(2)],
+                                      local_sem=T.sem[loc])
+        _record(rec, "gpsimd", "remote", call, list(ins), [], tag=arr)
 
     def arrive(writes, sem, src, calls=1):
-        _record(rec, "network", "arr", (sem, calls * len(lanes(src, core))), [], writes)
+        _record(rec, "network", "arr", (sem, calls * len(topo.engines(src, core))), [], writes)
 
-    load("sync", V("xt0", 0, 384), T.x[:, 0:384])
-    load("scalar", V("kbt", 0, 512), T.kb[:, 0:512])
-    load("sync", V("kbt", 512, 1024), T.kb[:, 512:1024])
-    kb2 = load("sync", V("kbt", 1024, 1536), T.kb[:, 1024:1536])
+    def eng(c):
+        return "vector" if c == "v" else "scalar"
 
+    pm, pd = V("pf", 0, 1), V("pf", 1, 2)
+    XL = MK + 6
+    first = [load(OPT["lq"][0], V("tl", X0, X0 + 384), T.x[:, 0:384])]
+    for k, (u, v) in enumerate(_cut(OPT["load"])):
+        first.append(load(OPT["lq"][k + 1], V("tl", KB + 4 * u, KB + 4 * v), T.kb[:, 4 * u:4 * v]))
+    load("sync", V("tl", X1, X1 + 384), T.x[:, 384:768], first)
+    load("sync", V("wt", 0, 512), T.w[:, 0:512], first)
+
+    iota(V("dd", 0, 128), [[1, 128]], 0, -1)
     iota(V("ip", 0, 1), [[0, 1]], 0, 1)
-    memset(V("ones", 0, 128), 1.0)
-    _record(rec, "gpsimd", "comp", lambda q: q.affine_select(T.ident[:, 0:128], T.ones[:, 0:128], [[-1, 128]], A.is_equal, 0.0, 0, 1),
-            [V("ones", 0, 128)], [V("ident", 0, 128)])
     iota(V("cmod", 0, 128), [[0, 8], [1, 16]], 0, 0)
-    iota(V("pcol", 0, 1), [[0, 1]], 0, 1)
-    iota(V("iotac", 0, 128), [[1, 128]], 0, 0)
     iota(V("jown", 0, NT), [[1, NT]], OWN, 0)
-    iota(V("src0", 0, 480), [[1, 480]], 0, 0)
-    iota(V("jpar", 0, NT), [[1, NT]], (PAR + MRG) // 2, 0)
-    iota(V("src1", 0, 480), [[1, 480]], 0, 0)
-    memset(V("ze", 0, 520), 0.0)
-    copy(V("ze", 4, 516, 4), V("ident", 0, 128), "scalar", scale=0.25)
-    memset(V("xt0", 384, 512), 0.0)
-    memset(V("negc", 0, 128), -1e29)
-    ts(V("pmi", 0, 1), V("ip", 0, 1), 15, A.bitwise_and)
-    ts(V("pdi", 0, 1), V("ip", 0, 1), 4, A.logical_shift_right)
-    memset(V("xtile", 4 * XL, 4 * XC), 0.0)
-    copy(V("pm", 0, 1), V("pmi", 0, 1))
-    copy(V("pd", 0, 1), V("pdi", 0, 1))
-    memset(V("xtile", 4 * NT + 3, 4 * XL, 4), 0.0)
-    copy(V("xtile", 3, 4 * NT, 4), V("ident", 0, NT), "scalar")
-    copy(V("mask", 0, NT), V("ident", 0, NT), "scalar")
-
-    def etile(n, t):
-        quant(V(n, 128 * t, 128 * t + 128), V("ze", 4 - t, 516 - t))
-
-    def score(b, ps, u, v):
-        mm(ps, V("xq%d" % b, 0, 128), V("tab%d" % b, u, v))
-
-    def run_max(ps, u, v):
-        scan(V("p", u, v), V("ps%d" % ps, 0, v - u), V("negc", 0, v - u), V("p", u - 1, u) if u else -1e29, A.max, A.max)
-
-    def units(ps, u, v):
-        quant(V("tab0", u, v), V("kbt", 4 * u, 4 * v))
-        score(0, ps, u, v)
-
-    quant(V("xq0", 0, 128), V("xt0", 0, 512))
-    lay(V("sel", 96, 128), V("xq0", 96, 128))
-    lay(V("selm", 0, 32), V("xq0", 96, 128))
+    iota(V("jpar", 0, NT), [[1, NT]], PAR if OPT["valq"] == "v" else (PAR + MRG) // 2, 0)
     for b in range(NR):
-        lay(V("ex%d" % b, 6, 128), V("xq0", 0, 122))
-    load("sync", V("xt1", 0, 384), T.x[:, 384:768], [kb2])
-    load("sync", V("wt", 0, 512), T.w[:, 0:512], [kb2])
-    etile("e25", 0)
-    units(*PIECES[0])
-    etile("e25", 1)
-    units(*PIECES[1])
-    ts(V("eq16", 0, 128), V("cmod", 0, 128), V("pm", 0, 1), A.is_equal)
+        iota(V("src%d" % b, 0, 480), [[1, 480]], 0, 0)
+    memset(V("te25", 0, 520), 0.0)
+    ts(V("te25", 4, 516, 4), V("dd", 0, 128), 0.0, A.is_equal, 0.5, A.mult)
+    if not OPT["re"]:
+        copy(V("te75", 0, 520), V("te25", 0, 520), "scalar", scale=3.0)
+    memset(V("tl", ZZ, ZZ + 128), 0.0)
+    ts(V("pi", 0, 1), V("ip", 0, 1), 15, A.bitwise_and)
+    ts(V("pi", 1, 2), V("ip", 0, 1), 4, A.logical_shift_right)
+    copy(V("pf", 0, 2), V("pi", 0, 2))
+    ts(V("eq16", 0, 128), V("cmod", 0, 128), pm, A.is_equal)
+    cq = [eng(c) for c in OPT["cq"]]
     for t in range(4):
-        copy(V("tr16", t, 512, 4), V("eq16", 0, 128), "scalar", scale=16.0 if t == 3 else 1.0)
-    run_max(*PIECES[0])
-    units(*PIECES[2])
-    ts(V("mask", NT, XL + 1), V("iotac", 0, 7), V("pd", 0, 1), A.is_equal)
-    copy(V("mb", 0, XL), V("mask", 0, XL), "scalar", scale=1024.0, bias=-1024.0)
-    copy(V("mb2", 0, XL), V("mask", 0, XL), "scalar", scale=1024.0, bias=-1024.0 - 192.0)
-    run_max(*PIECES[1])
-    memset(V("tnegw", 0, 512), -1.0)
-    run_max(*PIECES[2])
-    memset(V("tnegw", 3, 512, 4), 0.0)
-    etile("e25", 2)
+        copy(V("tr16", t, 512, 4), V("eq16", 0, 128), cq[0], scale=16.0 if t == 3 else 1.0)
+    for n, c, q in (("tr1", 1.0, cq[1]), ("tnegw", -1.0, cq[2])):
+        if q == "vector":
+            memset(V(n, 0, 512), c)
+        else:
+            for t in range(3):
+                copy(V(n, t, 512, 4), V("dd", 0, 128), q, scale=0.0, bias=c)
+    ts(V("tr1", 3, 512, 4), V("dd", 0, 128), 0.0, A.is_le, 512.0, A.mult)
+    copy(V("tnegw", 3, 512, 4), V("dd", 0, 128), cq[2], scale=0.0)
+    copy(V("tnegw", 4 * ONE, 4 * ONE + 4), V("dd", 0, 4), cq[2], scale=0.0)
+    q = cq[3]
+    copy(V("mask", 0, MK), V("te25", 4, 4 + 4 * MK, 4), q, scale=2.0)
+    memset(V("mask", NT, MK), 0.0)
+    ts(V("mask", MK, XL), V("cmod", 0, 6), pd, A.is_equal)
+    copy(V("mb", 0, XL), V("mask", 0, XL), q, scale=1024.0, bias=-1024.0 - 192.0)
+    if any(OPT["hact"]):
+        copy(V("mb16", 0, XL), V("mask", 0, XL), q, scale=64.0, bias=-76.0)
+        memset(V("p", NU + 15, NU + 192, 16), 1e29)
+    if not all(OPT["hact"]):
+        memset(V("zz", 24, 25), -192.0)
+    copy(V("xtile", 4 * NT, 512), V("dd", 0, 128), q, scale=0.0)
+    copy(V("xtile", 2, 4 * NT, 4), V("dd", 0, NT), q, scale=0.0)
+    copy(V("xtile", 3, 4 * NT, 4), V("mask", 0, NT), q)
+    copy(V("xtile", 4 * ONE + 2, 4 * ONE + 3), V("mask", 0, 1), q)
+    copy(V("xtile", 4 * LX, 4 * LX + 24, 4, 96, 112), V("dd", 0, 6, 1, 96, 112), q, scale=0.0, bias=V("pf", 0, 1, 1, 96, 112))
+    copy(V("xtile", 4 * LX + 1, 4 * LX + 24, 4, 96, 112), V("dd", 0, 6, 1, 96, 112), q, scale=0.0, bias=192.0)
+    copy(V("xtile", 4 * LX + 3, 4 * LX + 24, 4, 96, 112), V("cmod", 0, 6, 1, 96, 112), q)
+    for t, s in enumerate((pm, 0.0, 192.0, pd)):
+        copy(V("cdig", t, 24, 4), V("mask", MK, XL), q, scale=s)
+    copy(V("ma", 0, 16), V("eq16", 0, 16), "scalar", scale=-1.0, bias=1.0)
+    copy(V("mc", 0, 1), V("eq16", 0, 1), "scalar", scale=0.0)
+    copy(V("mc", 1, 16), V("eq16", 0, 15), "scalar", scale=BIG)
+    tt(V("mw", 0, 16), V("ma", 0, 16), V("mc", 0, 16), A.max)
+    for c, n in ((16, 16), (32, 32), (64, 64), (128, 128), (256, 128)):
+        copy(V("mw", c, c + n), V("mw", 0, n), "scalar")
+    copy(V("esc0", 0, 1), pm, "scalar", bias=-14.0, func=AF.Relu)
+    copy(V("esc", 0, 1), V("esc0", 0, 1), "scalar", scale=1.0 - 1.0 / BIG, bias=1.0 / BIG)
+    for n in ("e25", "e75"):
+        if n == "e75" and OPT["re"]:
+            ts(V("te25", 4, 516, 4), V("dd", 0, 128), 0.0, A.is_equal, 1.5, A.mult)
+        for t in range(4):
+            quant(V(n, 128 * t, 128 * t + 128), V("te25" if OPT["re"] else "t" + n, 4 - t, 516 - t))
+    for n in ("r16", "r1", "negw"):
+        quant(V(n, 0, 128), V("t" + n, 0, 512))
+    quant(V("xq0", XQ, XQ + 128), V("tl", X0, X0 + 512))
+    quant(V("xq1", XQ, XQ + 128), V("tl", X1, X1 + 512))
+    quant(V("wq", 0, 128), V("wt", 0, 512))
+
+    def E(n, t):
+        return V(n, 128 * t, 128 * t + 128)
+
+    def score(b, k, u, v):
+        mm(4 + k, V("xq%d" % b, XQ, XQ + 128), V("tab%d" % b, u, v))
+
+    def run_max(k, u, v):
+        scan(V("p", u, v), V("te25", 1, 1 + 2 * (v - u), 2), V("ps%d" % (4 + k), 0, v - u), V("p", u - 1, u) if u else -1e29, A.add, A.max)
+
+    for k, (u, v) in enumerate(_cut(OPT["load"])):
+        quant(V("tab0", u, v), V("tl", KB + 4 * u, KB + 4 * v))
+        score(0, k, u, v)
+        run_max(k, u, v)
 
     for b in range(NR):
         tab, xq, nxt = "tab%d" % b, "xq%d" % b, "tab%d" % (b + 1) if b + 1 < NR else "fin"
-        win, src = "win%d" % b, V("src%d" % b, 0, 480)
-        lown, lx, land, look = [V("%s%d" % (n, b), 0, 6) for n in ("lown", "lx", "land", "look")]
-        xl, ex = V("xl%d" % b, 0, XC), V("ex%d" % b, 0, 128)
+        win, src = V("win%d" % b, 0, 1), V("src%d" % b, 0, 480)
+        lown, lx, land = [V("%s%d" % (n, b), 0, 6) for n in ("lown", "lx", "land")]
+        xl, xf = V("xl%d" % b, 0, 128), "xf%d" % b
         partner = T.cores[rank ^ (1 << b)]
-
-        def tokens(xq=xq):
-            for t in range(4):
-                mm(t, V("e25", 128 * t, 128 * t + 128), V(xq, 0, 128), True, False)
-
-        if b == 1:
-            tokens()
-        last = V("p", NU - 1, NU)
-        _record(rec, "scalar", "comp",
-                lambda q, w=win: q.activation(T.junk[:, 0:NU], T.p[:, 0:NU], AF.Sign, bias=T.p[:, NU - 1:NU], scale=-1.0,
-                                              accum_out=T[w][:, 0:1]), [V("p", 0, NU)], [V("junk", 0, NU), V(win, 0, 1)])
-        ts(V("zz", 0, 24), V("p", 15, NU, 16), last, A.is_lt, 16.0, A.mult)
-        if b == 0:
-            etile("e25", 3)
-        reduce(V("h1", 0, 1), V("zz", 0, 24), A.add)
-        if b == 0:
-            quant(V("r16", 0, 128), V("tr16", 0, 512))
-        ts(V("mbh", 0, XL), V("mb", 0, XL), V("h1", 0, 1), A.subtract)
-        ts(V("xtile", 1, 4 * XL, 4), V("mask", 0, XL), V("h1", 0, 1), A.mult, 192.0, A.min)
-        _record(rec, "scalar", "comp", lambda q: q.activation(T.xtile[:, 2:4 * XL:4], T.mb2[:, 0:XL], AF.Relu, bias=T.h1[:, 0:1]),
-                [V("mb2", 0, XL), V("h1", 0, 1)], [V("xtile", 2, 4 * XL, 4)])
-        if b == 0:
-            copy(V("ze", 4, 516, 4), V("ident", 0, 128), "scalar", scale=0.75)
-            for t in range(3):
-                copy(V("tr1", t, 512, 4), V("eq16", 0, 128), "scalar", scale=0.0, bias=1.0)
-            copy(V("ma", 0, 16), V("eq16", 0, 16), "scalar", scale=-1.0, bias=1.0)
-            copy(V("mc", 0, 1), V("eq16", 0, 1), "scalar", scale=0.0)
-            copy(V("mc", 1, 16), V("eq16", 0, 15), "scalar", scale=BIG)
-            copy(V("cf", 0, 1), V("pd", 0, 1), "scalar", bias=-5.0, func=AF.Relu)
-            copy(V("esc0", 0, 1), V("pm", 0, 1), "scalar", bias=-14.0, func=AF.Relu)
-            for n, c in (("nt", 4 * NT), ("mt", 0), ("xt1", 384)):
-                copy(V(n, c, c + 128), V("eq16", 0, 128), "scalar", scale=0.0)
-            copy(V("esc", 0, 1), V("esc0", 0, 1), "scalar", scale=1.0 - 1.0 / BIG, bias=1.0 / BIG)
-            ts(V("m6", 0, 6), V("mask", NT, XL), V("mask", XL, XL + 1), A.subtract)
-        ts(V("xtile", 0, 4 * XL, 4), V("mbh", 0, XL), V(win, 0, 1), A.add, 0.0, A.max)
-        if b == 0:
-            ts(V("tr1", 3, 512, 4), V("iotac", 0, 128), V("pcol", 0, 1), A.is_le, 512.0, A.mult)
-            tt(V("cdig", 3, 24, 4), V("m6", 0, 6), V("iotac", 0, 6), A.mult)
-            copy(V("cdig", 0, 24, 4), V("m6", 0, 6), "scalar", scale=V("pm", 0, 1))
-            copy(V("cdig", 1, 24, 4), V("m6", 0, 6), "scalar", scale=192.0)
-            copy(V("cdig", 2, 24, 4), V("m6", 0, 6), "scalar", scale=192.0)
-        quant(xl, V("xtile", 0, 4 * XC))
-        for x in ("", "s"):
-            send(partner, V(ex[0] + x, 0, 6), V(xl[0] + x, NT, XL), "ae%d" % b, "le")
-        mm(5, V("r16", 0, 128), xl)
-        if b == 0:
-            etile("e75", 0)
-            etile("e75", 1)
-            tokens()
-        else:
-            tt(V("pre", 0, 24), V("xtile", 4 * NT, 4 * XL), V("cdig", 0, 24), A.subtract)
-        copy(lown, V("ps5", NT, XL))
-        if b == 0:
-            quant(V("r1", 0, 128), V("tr1", 0, 512))
-        pick(V("sel", 0, NT), V(tab, 0, NU), lown)
-        if b == 0:
-            quant(V("negw", 0, 128), V("tnegw", 0, 512))
-        mm(6, V("r1", 0, 128), xl, True, False)
-        mm(6, xl, V("negw", 0, 128), False, True)
-        if b == 0:
-            etile("e75", 2)
-            etile("e75", 3)
-            tt(V("mw", 0, 16), V("ma", 0, 16), V("mc", 0, 16), A.max)
-            tt(V("pre", 0, 24), V("xtile", 4 * NT, 4 * XL), V("cdig", 0, 24), A.subtract)
         for t in range(4):
-            mm(t, V("e75", 128 * t, 128 * t + 128), V("sel", 0, 128), False, True)
-        reduce(V("dmin", 0, 1), V("ps6", 0, NT), A.min, absv=True)
-        ts(V("flag", 0, 1), V("dmin", 0, 1), 1.0, A.min, V("cf", 0, 1), A.max)
-        ts(V("xtile", 4 * XL, 4 * XL + 24), V("pre", 0, 24), V("flag", 0, 1), A.mult)
-        quant(V("xf", 0, 128), V("xtile", 0, 512))
-        arrive([V(ex[0], 0, 6), V(ex[0] + "s", 0, 6)], "ae%d" % b, partner, 2)
-        mm(4, V("r16", 0, 128), ex)
-        mm(7, V("r16", 0, 128), V("xf", 0, 128))
-        for t in range(3):
-            copy(V("nt", t, 4 * NT, 4), V("ps%d" % t, 0, NT), "scalar")
-        copy(V("nt", 3, 4 * NT, 4), V("ps3", 0, NT))
-        quant(V(tab, OWN, OWN + 128), V("nt", 0, 512))
+            mm(t, E("e25", t), V(xq, XQ, XQ + 128), True, False)
+        last, h1 = V("p", NU - 1, NU), V("h1", 0, 1)
+        if OPT["hact"][b]:
+            copy(V("junk2", 0, 36), V("p", 15, NU + 192, 16), "scalar", scale=-1.0, bias=last, func=AF.Sign, accum=h1)
+        copy(V("junk", 0, NU), V("p", 0, NU), "scalar", scale=-1.0, bias=last, func=AF.Sign, accum=win)
+        if OPT["hact"][b]:
+            ts(V("mbh", 0, XL), V("mb16", 0, XL), h1, A.subtract, 16.0, A.mult)
+            ts(V("xtile", 1, 4 * XL, 4), V("mask", 0, XL), h1, A.mult, 16.0, A.mult)
+        else:
+            ts(V("zz", 0, 24), V("p", 15, NU, 16), last, A.is_lt, 16.0, A.mult)
+            reduce(h1, V("zz", 0, 25), A.add)
+            ts(V("mbh", 0, XL), V("mb", 0, XL), h1, A.subtract)
+            ts(V("xtile", 1, 4 * XL, 4), V("mask", 0, XL), h1, A.mult)
+        ts(V("xtile", 0, 4 * XL, 4), V("mbh", 0, XL), win, A.add, 0.0, A.max)
+        store("sync", T.ch[b:b + 1, 0:NT], win, T[win[0]][0:NT, 0:1])
+        quant(xl, V("xtile", 0, 512))
+        codes = OPT["early"][b] == "codes"
+        if codes:
+            send2(partner, (V(xf, EX, EX + 6), V(xf + "s", EX, EX + 24)), (V(xl[0], MK, XL), V(xl[0] + "s", MK, MK + 24)), "ae%d" % b, "le")
+        mm(6, V("r16", 0, 128), xl)
+        ts(lown, V("ps6", MK, XL), 192.0, A.add)
+        look = V(lx[0], 6, 12) if codes else V("look%d" % b, 0, 6)
+        if not codes:
+            send(partner, look, lown, "ae%d" % b, "le")
+        pick(V(xq, 0, NT), V(tab, 0, NU), lown)
+        mm(7, V("r1", 0, 128), xl, True, False)
+        mm(7, xl, V("negw", 0, 128), False, True)
+        for t in range(4):
+            mm(t, E("e75", t), V(xq, 0, 128), False, True)
+        tt(V("pre", 0, 24), V("xtile", 4 * MK, 4 * XL), V("cdig", 0, 24), A.subtract)
+        reduce(V("flag", 0, 1), V("ps7", 0, ONE + 1), A.min, absv=True)
+        ts(V("xtile", 4 * LX, 4 * LX + 24, 1, 0, NT), V("pre", 0, 24, 1, 0, NT), V("flag", 0, 1, 1, 0, NT), A.mult)
+        quant(V(xf, 0, 128), V("xtile", 0, 512))
+        if codes:
+            arrive([V(xf, EX, EX + 6), V(xf + "s", EX, EX + 24)], "ae%d" % b, partner)
+            mm(4, V("r16", 0, 128), V(xf, 6, 134))
+            ts(V(lx[0], 0, 12), V("ps4", LX - 6, 128), 192.0, A.add)
+        else:
+            arrive([look], "ae%d" % b, partner)
+            mm(4, V("r16", 0, 128), V(xf, 0, 128))
+            ts(lx, V("ps4", LX, 128), 192.0, A.add)
+        for t in range(4):
+            copy(V("tl", NTL + t, NTL + 4 * NT, 4), V("ps%d" % t, 0, NT), eng(OPT["ntq"][t]), scale=0.5)
+        quant(V(tab, OWN, OWN + 128), V("tl", NTL, NTL + 512))
         for x in (tab, tab + "s"):
             send(partner, V(x, PAR, PAR + NT), V(x, OWN, OWN + NT), "ac%d" % b, "lc")
-        copy(lx, V("ps7", XL, XL + 6))
         send(partner, land, lx, "al%d" % b, "ll")
-        store("sync", T.ch[b:b + 1, 0:NT], V(win, 0, 1), T[win][0:NT, 0:1])
-        if b == 0:
-            for c, n in ((16, 16), (32, 32), (64, 64), (128, 128), (256, 128)):
-                copy(V("mw", c, c + n), V("mw", 0, n), "scalar")
-        copy(look, V("ps4", 0, 6))
         scatter(src, lx, V("jown", 0, NT))
         arrive([land], "al%d" % b, partner)
         arrive([V(tab, PAR, PAR + NT), V(tab + "s", PAR, PAR + NT)], "ac%d" % b, partner, 2)
-        copy(V("c1", 0, NT), src, off=look)
-        copy(V("sg", 0, NT), src, "scalar", bias=0.5 - OWN, off=look, func=AF.Sign)
-        copy(V("both", 0, NT), V("sg", 0, NT), "scalar", scale=(MRG - PAR) / 2.0)
-        scan(V("c2", 0, NT), V("mw", 0, NT), V("c1", 0, NT), 0.0, A.mult, A.add)
-        if b == 0:
-            quant(V("xq1", 0, 128), V("xt1", 0, 512))
+        copy(V("c1", 0, NT), src, OPT["c1q"], off=look)
+        if OPT["valq"] == "s":
+            copy(V("sg", 0, NT), V("c1", 0, NT), "scalar", bias=0.5 - OWN, func=AF.Sign)
+            copy(V("both", 0, NT), V("sg", 0, NT), "scalar", scale=(MRG - PAR) / 2.0)
+        elif OPT["valq"] == "g":
+            copy(V("sg", 0, NT), src, "scalar", bias=0.5 - OWN, func=AF.Sign, off=look)
+            copy(V("both", 0, NT), V("sg", 0, NT), "scalar", scale=(MRG - PAR) / 2.0)
         else:
-            quant(V("wq", 0, 128), V("wt", 0, 512))
+            ts(V("both", 0, NT), V("c1", 0, NT), OWN - 0.5, A.is_ge, float(MRG - PAR), A.mult)
+        scan(V("c2", 0, NT), V("mw", 0, NT), V("c1", 0, NT), 0.0, A.mult, A.add)
         ts(V("clist", 0, 6), V("c2", 15, NT, 16), V("esc", 0, 1), A.mult, -0.34, A.add)
         tt(V("val", 0, NT), V("both", 0, NT), V("jpar", 0, NT), A.add)
-        pick(V("selm", 32, 128), V(tab, 0, PAR), V("clist", 0, 6))
-        for k, x in enumerate((V(tab, PAR - 32, PAR + NT), V("selm", 0, 128))):
+        if OPT["merge"][b] == "A":
+            pick(V(xq, SM, SM + NT), V(tab, 0, PAR), V("clist", 0, 6))
+            sides = (V(xq, SM - 32, SM + NT), V(tab, PAR - 32, PAR + NT))
+            for k, x in enumerate(sides if OPT["ownfirst"][b] else sides[::-1]):
+                for t in range(4):
+                    mm(t, E("e25", t), x, k == 0, k == 1)
+        else:
             for t in range(4):
-                mm(t, V("e25", 128 * t, 128 * t + 128), x, k == 0, k == 1)
+                mm(t, E("e25", t), V(tab, OWN, OWN + 128))
+                copy(V("junk", NU + NT * t, NU + NT * t + NT), V("ps%d" % t, 0, NT), eng(OPT["dq"][t]))
+            for t in range(4):
+                copy(V("dg", NT * t, NT * t + NT), V("junk", NT * t, NU + NT * t + NT), eng(OPT["gq"][t]), off=V("clist", 0, 6))
+                mm(t, E("e25", t), V(tab, PAR - 32, PAR + NT))
         scatter(src, land, V("val", 0, NT))
         scan(V("srcs", 0, NU), V("mw", 0, NU), V(src[0], 0, NU), 0.0, A.mult, A.add)
         ts(V("blist", 0, 24), V("srcs", 15, NU, 16), V("esc", 0, 1), A.mult, -0.34, A.add)
         for t in range(4):
-            copy(V("mt", 128 + t, 512, 4), V("ps%d" % t, 32, 128), "scalar", scale=2.0)
-        quant(V(tab, MQ, MQ + 128), V("mt", 0, 512))
-        for ps, u, v in PIECES:
+            if OPT["merge"][b] == "A":
+                copy(V("tl", MT + t, MT + 4 * NT, 4), V("ps%d" % t, 32, 128), eng(OPT["mtq"][t]))
+            else:
+                tt(V("tl", MT + t, MT + 4 * NT, 4), V("dg", NT * t, NT * t + NT), V("ps%d" % t, 32, 128), A.add)
+        quant(V(tab, MRG, MRG + 128), V("tl", MT, MT + 512))
+        for k, (u, v) in enumerate(_cut(OPT["tab" if b + 1 < NR else "fin"])):
             pick(V(nxt, u, v), V(tab, 0, WIN), V("blist", u // 16, v // 16))
             if b + 1 < NR:
-                score(b + 1, ps, u, v)
-        if b + 1 < NR:
-            for piece in PIECES:
-                run_max(*piece)
+                score(b + 1, k, u, v)
+                run_max(k, u, v)
 
-    for ps, u, v in PIECES:
-        mm(ps, V("wq", 0, 128), V("fin", u, v))
-        store("sync", T.oc[:, 4 * u:4 * v], V("fin", u, v), T.fin[:, u:v].bitcast(dt.uint8))
-    for ps, u, v in PIECES:
-        copy(V("ysb", u, v), V("ps%d" % ps, 0, v - u), "scalar" if u == 128 else "vector")
+    for k, (u, v) in enumerate(_cut(OPT["fin"])):
+        mm(4 + k, V("wq", 0, 128), V("fin", u, v))
+        copy(V("ysb", u, v), V("ps%d" % (4 + k), 0, v - u), eng(OPT["yq"][k]))
         store("sync", T.y[:, u:v], V("ysb", u, v), T.ysb[:, u:v])
+    for u, v in [(0, NU)] if OPT["ocwhole"] else _cut(OPT["fin"]):
+        store("sync", T.oc[:, 4 * u:4 * v], V("fin", u, v), T.fin[:, u:v].bitcast(dt.uint8))
     for k in range(4):
         store("scalar", T.osc[4 * k:4 * k + 4, 0:NU], V("fins", 0, NU), T.fins[32 * k:32 * k + 4, 0:NU])
     _record(rec, "sync", "end", None, [], [], stores)
-    _issue(rec, {"vector": g.vector, "scalar": g.scalar, "tensor": g.tensor, "gpsimd": g, "sync": g.sync}, T.sem)
-    n = sum(len(lanes(core, T.cores[rank ^ (1 << b)])) for b in range(NR))
-    g.wait_ge(T.sem.ll, n)
-    g.wait_ge(T.sem.le, 2 * n)
-    g.wait_ge(T.sem.lc, 2 * n)
+    return rec["ops"], local
+
+
+def rank_program(g, core, T, topo):
+    if T.rank_of(core) is None:
+        return
+    ops, local = _calls(core, T, topo)
+    _issue(ops, ORDER or list(range(len(ops))), {"vector": g.vector, "scalar": g.scalar, "tensor": g.tensor, "gpsimd": g, "sync": g.sync}, T.sem)
+    for n in sorted(local):
+        g.wait_ge(T.sem[n], local[n])

@@ -6,23 +6,25 @@ A = AluOpType
 AF = ActivationFunctionType
 NU, NT, NR = 384, 96, 2
 OWN, PAR, MRG, WIN = 384, 512, 608, 736
-XQ, SM = 96, 224
-ONE, MK, LX, EX = 96, 98, 122, 128
+XQ = 96
+MK, XL, ONE, LX, EX = 96, 102, 102, 122, 128
+OFF = 8192.0
+LO = 192.0 + 7 * OFF
 MT, NTL, X0, ZZ, X1, KB = 0, 384, 768, 1152, 1280, 1664
 BIG = 16384.0
 F4, F32, BF, U16, I32, U8 = "float8_e4m3fn_x4", "float32", "bfloat16", "uint16", "int32", "uint8"
-OPT = {"load": (256, 128), "tab": (128, 128, 128), "fin": (256, 128), "early": ("list", "codes"), "hact": (0, 0), "ownfirst": (1, 1),
-       "ntq": "sssv", "mtq": "svsv", "c1q": "scalar", "ocwhole": 0, "yq": "vs", "lq": ("sync", "scalar", "sync", "sync"), "cq": "svvs",
-       "merge": "BB", "gq": "ssss", "dq": "ssss", "re": 1, "valq": "v"}
-ORDER = [0, 1, 6, 12, 2, 5, 32, 16, 15, 23, 7, 17, 33, 13, 14, 25, 8, 58, 28, 37, 18, 38, 57, 9, 56, 21, 44, 30, 36, 67, 46, 45, 10, 22, 70, 40,
-         20, 35, 29, 39, 24, 19, 71, 4, 31, 3, 73, 74, 72, 11, 78, 55, 75, 26, 76, 59, 80, 81, 77, 64, 79, 82, 47, 34, 83, 53, 84, 86, 41, 27,
-         43, 85, 48, 65, 54, 42, 87, 49, 66, 50, 62, 88, 63, 93, 89, 94, 99, 90, 92, 100, 91, 51, 101, 98, 102, 97, 60, 61, 104, 108, 95, 52,
-         105, 96, 109, 106, 114, 113, 107, 103, 110, 68, 117, 112, 122, 115, 111, 124, 118, 123, 119, 126, 121, 125, 128, 127, 120, 138, 130,
-         116, 135, 129, 134, 131, 139, 137, 136, 133, 132, 141, 143, 144, 142, 160, 140, 158, 145, 159, 147, 146, 150, 151, 148, 154, 155, 152,
-         149, 156, 153, 161, 157, 163, 162, 164, 165, 166, 168, 167, 169, 69, 181, 171, 170, 175, 172, 176, 174, 173, 182, 179, 185, 183, 177,
-         184, 190, 178, 188, 180, 189, 186, 191, 187, 192, 195, 196, 194, 204, 193, 206, 208, 199, 210, 197, 205, 207, 200, 211, 201, 209, 203,
-         198, 213, 202, 217, 220, 212, 219, 215, 218, 223, 216, 221, 214, 226, 225, 224, 222, 227, 228, 229, 230, 231, 238, 232, 239, 241, 243,
-         235, 240, 242, 233, 236, 234, 237, 244]
+OPT = {"load": (256, 128), "tab": (192, 192), "fin": (192, 192), "bs": ((192, 192), (192, 192)), "early": ("apart", "list"),
+       "ntq": "sssv", "c1q": "s", "yq": "vv", "lq": "ysyy", "cq": "svvs", "gq": "ssss", "dq": "ssss", "flq": "vv", "x1q": "vv",
+       "oscq": "ssyy", "ysq": "yyy", "ocq": "yyy"}
+ORDER = [0, 1, 6, 31, 12, 5, 2, 14, 15, 16, 23, 7, 32, 17, 33, 13, 24, 37, 11, 36, 28, 25, 18, 29, 54, 19, 38, 45, 42, 39, 41, 66, 43, 46, 40, 34,
+         9, 21, 35, 44, 69, 30, 10, 20, 22, 57, 3, 70, 56, 4, 72, 71, 73, 78, 47, 26, 74, 8, 48, 55, 79, 80, 63, 76, 75, 81, 27, 77, 58, 82, 83,
+         84, 60, 85, 59, 86, 87, 64, 65, 91, 97, 88, 92, 61, 90, 89, 49, 98, 52, 62, 94, 50, 93, 99, 95, 104, 96, 100, 105, 106, 103, 53, 101,
+         51, 102, 110, 113, 114, 111, 112, 107, 108, 122, 126, 109, 124, 68, 115, 128, 117, 118, 127, 123, 116, 135, 119, 125, 131, 121, 133,
+         129, 137, 120, 138, 130, 134, 67, 132, 139, 136, 145, 143, 140, 158, 144, 146, 141, 157, 156, 147, 142, 148, 149, 152, 153, 150, 151,
+         154, 155, 160, 161, 162, 163, 165, 164, 166, 178, 167, 172, 173, 168, 159, 179, 169, 171, 170, 180, 176, 181, 177, 187, 188, 182, 174,
+         175, 183, 185, 186, 192, 193, 184, 189, 196, 197, 190, 207, 201, 191, 203, 198, 208, 205, 200, 202, 204, 199, 206, 194, 217, 209, 211,
+         215, 218, 220, 213, 195, 210, 212, 216, 222, 214, 223, 225, 224, 221, 226, 219, 229, 230, 227, 228, 238, 234, 235, 237, 231, 239, 236,
+         240, 232, 241, 233, 242, 243]
 
 
 def _decl():
@@ -36,17 +38,15 @@ def _decl():
         add(n + "s", w, U8)
     for b in range(NR):
         pair("tab%d" % b, WIN)
-        pair("xq%d" % b, SM + NT)
+        pair("xq%d" % b, XQ + 128)
         pair("xl%d" % b, 128)
         pair("xf%d" % b, EX + 32)
-        for n in ("lown", "land", "look"):
+        for n in ("lown", "land", "look", "lx"):
             add("%s%d" % (n, b), 8, U16)
-        add("lx%d" % b, 12, U16)
         add("src%d" % b, 480, F32)
         add("win%d" % b, 1, F32)
-    for n in ("e25", "e75"):
+    for n in ("e1", "e3"):
         pair(n, 512)
-        add("t" + n, 520, BF)
     for n in ("r16", "r1", "negw"):
         pair(n, 128)
         add("t" + n, 512, BF)
@@ -54,14 +54,13 @@ def _decl():
     pair("fin", NU)
     for n in range(8):
         add("ps%d" % n, 512, F32, "psum")
-    for n, w, t in (("tl", KB + 4 * NU, BF), ("wt", 512, BF), ("xtile", 512, BF), ("dd", 128, BF), ("mask", MK + 6, BF), ("junk", 2 * NU, BF),
-                    ("dg", NU, BF), ("junk2", 36, BF), ("mb", MK + 6, BF), ("mbh", MK + 6, BF), ("cmod", 128, BF), ("eq16", 128, BF), ("ma", 16, BF),
-                    ("mb16", MK + 6, BF), ("mc", 16, BF), ("mw", NU, BF), ("cdig", 24, BF), ("pre", 24, BF),
+    for n, w, t in (("tl", KB + 4 * NU, BF), ("te", 520, BF), ("wt", 512, BF), ("xtile", 512, BF), ("dd", 128, BF), ("mask", XL, BF),
+                    ("junk", 2 * NU, BF), ("dg", NU, BF), ("mb", XL, BF), ("cmod", 128, BF), ("eq16", 128, BF), ("ma", 16, BF),
+                    ("mc", 16, BF), ("mw", NU, BF), ("cdig", 24, BF), ("pre", 24, BF),
                     ("ip", 1, I32), ("pi", 2, I32), ("clist", 6, U16), ("blist", 24, U16)):
         add(n, w, t)
-    for n, w in (("jown", NT), ("jpar", NT), ("pf", 2), ("p", NU + 192), ("zz", 25), ("h1", 1),
-                 ("flag", 1), ("esc0", 1), ("esc", 1), ("c1", NT), ("c2", NT), ("sg", NT),
-                 ("both", NT), ("val", NT), ("srcs", NU), ("ysb", NU)):
+    for n, w in (("jown", NT), ("jpar", NT), ("pf", 2), ("p", NU), ("zz", 25), ("h1", 1), ("flag", 1), ("pmo", 1), ("esc0", 1), ("esc", 1),
+                 ("c1", NT), ("c2", NT), ("both", NT), ("val", NT), ("srcs", NU), ("ysb", NU)):
         add(n, w, F32)
     return s
 
@@ -163,6 +162,7 @@ def _calls(core, T, topo):
     rank = T.rank_of(core)
     rec = {"ops": [], "acc": {}}
     local = {"le": 0, "ll": 0, "lc": 0}
+    eng = {"v": "vector", "s": "scalar", "y": "sync"}
 
     def ap(v):
         return T[v[0]][v[4]:v[5], v[1]:v[2]] if v[3] == 1 else T[v[0]][v[4]:v[5], v[1]:v[2]:v[3]]
@@ -176,17 +176,19 @@ def _calls(core, T, topo):
     def val(x):
         return ap(x) if isinstance(x, tuple) else x
 
+    def by(v, off):
+        return ap(v) if off is None else ap(v).indirect(ap(off))
+
     def memset(out, c):
         _record(rec, "vector", "comp", lambda q: q.memset(ap(out), c), [], [out])
 
-    def copy(out, in_, queue="vector", scale=None, bias=None, off=None, func=None, accum=None):
-        src = (lambda: ap(in_)) if off is None else (lambda: ap(in_).indirect(ap(off)))
-        if queue == "vector":
+    def copy(out, in_, queue="v", scale=None, bias=None, off=None, func=None, accum=None):
+        if queue == "v":
             if bias is not None:
                 return ts(out, in_, scale, A.mult, bias, A.add)
             if scale is not None:
                 return ts(out, in_, scale, A.mult)
-            _record(rec, "vector", "comp", lambda q: q.tensor_copy(ap(out), src()), views(in_, off), [out])
+            _record(rec, "vector", "comp", lambda q: q.tensor_copy(ap(out), by(in_, off)), views(in_, off), [out])
             return
         f = func or (AF.Copy if bias is None else AF.Identity)
         kw = {}
@@ -196,14 +198,14 @@ def _calls(core, T, topo):
             kw["bias"] = val(bias)
         if accum is not None:
             kw["accum_out"] = ap(accum)
-        _record(rec, "scalar", "comp", lambda q: q.activation(ap(out), src(), f, **kw), views(in_, scale, bias, off), views(accum, out))
+        _record(rec, "scalar", "comp", lambda q: q.activation(ap(out), by(in_, off), f, **kw), views(in_, scale, bias, off), views(accum, out))
 
-    def ts(out, in0, s1, op0, s2=None, op1=None):
+    def ts(out, in0, s1, op0, s2=None, op1=None, off=None):
         def call(q):
             if op1 is None:
-                return q.tensor_scalar(ap(out), ap(in0), val(s1), None, op0)
-            return q.tensor_scalar(ap(out), ap(in0), val(s1), val(s2), op0, op1)
-        _record(rec, "vector", "comp", call, views(in0, s1, s2), [out])
+                return q.tensor_scalar(ap(out), by(in0, off), val(s1), None, op0)
+            return q.tensor_scalar(ap(out), by(in0, off), val(s1), val(s2), op0, op1)
+        _record(rec, "vector", "comp", call, views(in0, s1, s2, off), [out])
 
     def tt(out, in0, in1, op):
         _record(rec, "vector", "comp", lambda q: q.tensor_tensor(ap(out), ap(in0), ap(in1), op), [in0, in1], [out])
@@ -247,12 +249,12 @@ def _calls(core, T, topo):
         _record(rec, "gpsimd", "comp", call, [], [out])
 
     def load(queue, out, src, after=()):
-        return _record(rec, queue, "dma", lambda q: q.dma_start(ap(out), src), [], [out], after)
+        return _record(rec, eng[queue], "dma", lambda q: q.dma_start(ap(out), src), [], [out], after)
 
     stores = []
 
     def store(queue, dst, in_, view):
-        stores.append(_record(rec, queue, "dma", lambda q: q.dma_start(dst, view), [in_], []))
+        stores.append(_record(rec, eng[queue], "dma", lambda q: q.dma_start(dst, view), [in_], []))
 
     def raw(v):
         return ap(v).bitcast(dt.uint8) if SCRATCH[v[0]][2] == F4 else ap(v)
@@ -277,55 +279,44 @@ def _calls(core, T, topo):
     def arrive(writes, sem, src, calls=1):
         _record(rec, "network", "arr", (sem, calls * len(topo.engines(src, core))), [], writes)
 
-    def eng(c):
-        return "vector" if c == "v" else "scalar"
-
     pm, pd = V("pf", 0, 1), V("pf", 1, 2)
-    XL = MK + 6
     first = [load(OPT["lq"][0], V("tl", X0, X0 + 384), T.x[:, 0:384])]
     for k, (u, v) in enumerate(_cut(OPT["load"])):
         first.append(load(OPT["lq"][k + 1], V("tl", KB + 4 * u, KB + 4 * v), T.kb[:, 4 * u:4 * v]))
-    load("sync", V("tl", X1, X1 + 384), T.x[:, 384:768], first)
-    load("sync", V("wt", 0, 512), T.w[:, 0:512], first)
+    load("y", V("tl", X1, X1 + 384), T.x[:, 384:768], first)
+    load("y", V("wt", 0, 512), T.w[:, 0:512], first)
 
     iota(V("dd", 0, 128), [[1, 128]], 0, -1)
     iota(V("ip", 0, 1), [[0, 1]], 0, 1)
     iota(V("cmod", 0, 128), [[0, 8], [1, 16]], 0, 0)
     iota(V("jown", 0, NT), [[1, NT]], OWN, 0)
-    iota(V("jpar", 0, NT), [[1, NT]], PAR if OPT["valq"] == "v" else (PAR + MRG) // 2, 0)
+    iota(V("jpar", 0, NT), [[1, NT]], PAR, 0)
     for b in range(NR):
         iota(V("src%d" % b, 0, 480), [[1, 480]], 0, 0)
-    memset(V("te25", 0, 520), 0.0)
-    ts(V("te25", 4, 516, 4), V("dd", 0, 128), 0.0, A.is_equal, 0.5, A.mult)
-    if not OPT["re"]:
-        copy(V("te75", 0, 520), V("te25", 0, 520), "scalar", scale=3.0)
+    memset(V("te", 0, 520), 0.0)
+    ts(V("te", 4, 516, 4), V("dd", 0, 128), 0.0, A.is_equal, 0.5, A.mult)
     memset(V("tl", ZZ, ZZ + 128), 0.0)
     ts(V("pi", 0, 1), V("ip", 0, 1), 15, A.bitwise_and)
     ts(V("pi", 1, 2), V("ip", 0, 1), 4, A.logical_shift_right)
     copy(V("pf", 0, 2), V("pi", 0, 2))
     ts(V("eq16", 0, 128), V("cmod", 0, 128), pm, A.is_equal)
-    cq = [eng(c) for c in OPT["cq"]]
+    cq = OPT["cq"]
     for t in range(4):
         copy(V("tr16", t, 512, 4), V("eq16", 0, 128), cq[0], scale=16.0 if t == 3 else 1.0)
     for n, c, q in (("tr1", 1.0, cq[1]), ("tnegw", -1.0, cq[2])):
-        if q == "vector":
+        if q == "v":
             memset(V(n, 0, 512), c)
         else:
             for t in range(3):
                 copy(V(n, t, 512, 4), V("dd", 0, 128), q, scale=0.0, bias=c)
     ts(V("tr1", 3, 512, 4), V("dd", 0, 128), 0.0, A.is_le, 512.0, A.mult)
     copy(V("tnegw", 3, 512, 4), V("dd", 0, 128), cq[2], scale=0.0)
-    copy(V("tnegw", 4 * ONE, 4 * ONE + 4), V("dd", 0, 4), cq[2], scale=0.0)
+    copy(V("tnegw", 4 * MK, 4 * ONE + 4), V("dd", 0, 28), cq[2], scale=0.0)
     q = cq[3]
-    copy(V("mask", 0, MK), V("te25", 4, 4 + 4 * MK, 4), q, scale=2.0)
-    memset(V("mask", NT, MK), 0.0)
+    copy(V("mask", 0, MK), V("te", 4, 4 + 4 * MK, 4), q, scale=2.0)
     ts(V("mask", MK, XL), V("cmod", 0, 6), pd, A.is_equal)
-    copy(V("mb", 0, XL), V("mask", 0, XL), q, scale=1024.0, bias=-1024.0 - 192.0)
-    if any(OPT["hact"]):
-        copy(V("mb16", 0, XL), V("mask", 0, XL), q, scale=64.0, bias=-76.0)
-        memset(V("p", NU + 15, NU + 192, 16), 1e29)
-    if not all(OPT["hact"]):
-        memset(V("zz", 24, 25), -192.0)
+    copy(V("mb", 0, XL), V("mask", 0, XL), q, scale=OFF, bias=-OFF - 192.0)
+    memset(V("zz", 24, 25), -192.0)
     copy(V("xtile", 4 * NT, 512), V("dd", 0, 128), q, scale=0.0)
     copy(V("xtile", 2, 4 * NT, 4), V("dd", 0, NT), q, scale=0.0)
     copy(V("xtile", 3, 4 * NT, 4), V("mask", 0, NT), q)
@@ -333,21 +324,22 @@ def _calls(core, T, topo):
     copy(V("xtile", 4 * LX, 4 * LX + 24, 4, 96, 112), V("dd", 0, 6, 1, 96, 112), q, scale=0.0, bias=V("pf", 0, 1, 1, 96, 112))
     copy(V("xtile", 4 * LX + 1, 4 * LX + 24, 4, 96, 112), V("dd", 0, 6, 1, 96, 112), q, scale=0.0, bias=192.0)
     copy(V("xtile", 4 * LX + 3, 4 * LX + 24, 4, 96, 112), V("cmod", 0, 6, 1, 96, 112), q)
-    for t, s in enumerate((pm, 0.0, 192.0, pd)):
-        copy(V("cdig", t, 24, 4), V("mask", MK, XL), q, scale=s)
-    copy(V("ma", 0, 16), V("eq16", 0, 16), "scalar", scale=-1.0, bias=1.0)
-    copy(V("mc", 0, 1), V("eq16", 0, 1), "scalar", scale=0.0)
-    copy(V("mc", 1, 16), V("eq16", 0, 15), "scalar", scale=BIG)
+    copy(V("pmo", 0, 1), pm, q, scale=1.0, bias=OFF)
+    for t, s in enumerate((V("pmo", 0, 1), 0.0, 192.0, pd)):
+        copy(V("cdig", t, 24, 4), V("mask", MK, XL), q, scale=s, bias=None if t else -OFF)
+    copy(V("ma", 0, 16), V("eq16", 0, 16), "s", scale=-1.0, bias=1.0)
+    copy(V("mc", 0, 1), V("eq16", 0, 1), "s", scale=0.0)
+    copy(V("mc", 1, 16), V("eq16", 0, 15), "s", scale=BIG)
     tt(V("mw", 0, 16), V("ma", 0, 16), V("mc", 0, 16), A.max)
-    for c, n in ((16, 16), (32, 32), (64, 64), (128, 128), (256, 128)):
-        copy(V("mw", c, c + n), V("mw", 0, n), "scalar")
-    copy(V("esc0", 0, 1), pm, "scalar", bias=-14.0, func=AF.Relu)
-    copy(V("esc", 0, 1), V("esc0", 0, 1), "scalar", scale=1.0 - 1.0 / BIG, bias=1.0 / BIG)
-    for n in ("e25", "e75"):
-        if n == "e75" and OPT["re"]:
-            ts(V("te25", 4, 516, 4), V("dd", 0, 128), 0.0, A.is_equal, 1.5, A.mult)
+    for c, n in ((16, 16), (32, 32), (64, 64), (128, 128), (256, 128))[:5 if max(max(x) for x in OPT["bs"]) > 256 else 4]:
+        copy(V("mw", c, c + n), V("mw", 0, n), "s")
+    copy(V("esc0", 0, 1), pm, "s", bias=-14.0, func=AF.Relu)
+    copy(V("esc", 0, 1), V("esc0", 0, 1), "s", scale=1.0 - 1.0 / BIG, bias=1.0 / BIG)
+    for n in ("e1", "e3"):
+        if n == "e3":
+            ts(V("te", 4, 516, 4), V("dd", 0, 128), 0.0, A.is_equal, 1.5, A.mult)
         for t in range(4):
-            quant(V(n, 128 * t, 128 * t + 128), V("te25" if OPT["re"] else "t" + n, 4 - t, 516 - t))
+            quant(V(n, 128 * t, 128 * t + 128), V("te", 4 - t, 516 - t))
     for n in ("r16", "r1", "negw"):
         quant(V(n, 0, 128), V("t" + n, 0, 512))
     quant(V("xq0", XQ, XQ + 128), V("tl", X0, X0 + 512))
@@ -361,7 +353,7 @@ def _calls(core, T, topo):
         mm(4 + k, V("xq%d" % b, XQ, XQ + 128), V("tab%d" % b, u, v))
 
     def run_max(k, u, v):
-        scan(V("p", u, v), V("te25", 1, 1 + 2 * (v - u), 2), V("ps%d" % (4 + k), 0, v - u), V("p", u - 1, u) if u else -1e29, A.add, A.max)
+        scan(V("p", u, v), V("te", 1, 1 + 2 * (v - u), 2), V("ps%d" % (4 + k), 0, v - u), V("p", u - 1, u) if u else -1e29, A.add, A.max)
 
     for k, (u, v) in enumerate(_cut(OPT["load"])):
         quant(V("tab0", u, v), V("tl", KB + 4 * u, KB + 4 * v))
@@ -371,53 +363,45 @@ def _calls(core, T, topo):
     for b in range(NR):
         tab, xq, nxt = "tab%d" % b, "xq%d" % b, "tab%d" % (b + 1) if b + 1 < NR else "fin"
         win, src = V("win%d" % b, 0, 1), V("src%d" % b, 0, 480)
-        lown, lx, land = [V("%s%d" % (n, b), 0, 6) for n in ("lown", "lx", "land")]
+        lown, lx, land, look = [V("%s%d" % (n, b), 0, 6) for n in ("lown", "lx", "land", "look")]
         xl, xf = V("xl%d" % b, 0, 128), "xf%d" % b
         partner = T.cores[rank ^ (1 << b)]
         for t in range(4):
-            mm(t, E("e25", t), V(xq, XQ, XQ + 128), True, False)
+            mm(t, E("e1", t), V(xq, XQ, XQ + 128), True, False)
         last, h1 = V("p", NU - 1, NU), V("h1", 0, 1)
-        if OPT["hact"][b]:
-            copy(V("junk2", 0, 36), V("p", 15, NU + 192, 16), "scalar", scale=-1.0, bias=last, func=AF.Sign, accum=h1)
-        copy(V("junk", 0, NU), V("p", 0, NU), "scalar", scale=-1.0, bias=last, func=AF.Sign, accum=win)
-        if OPT["hact"][b]:
-            ts(V("mbh", 0, XL), V("mb16", 0, XL), h1, A.subtract, 16.0, A.mult)
-            ts(V("xtile", 1, 4 * XL, 4), V("mask", 0, XL), h1, A.mult, 16.0, A.mult)
-        else:
-            ts(V("zz", 0, 24), V("p", 15, NU, 16), last, A.is_lt, 16.0, A.mult)
-            reduce(h1, V("zz", 0, 25), A.add)
-            ts(V("mbh", 0, XL), V("mb", 0, XL), h1, A.subtract)
-            ts(V("xtile", 1, 4 * XL, 4), V("mask", 0, XL), h1, A.mult)
-        ts(V("xtile", 0, 4 * XL, 4), V("mbh", 0, XL), win, A.add, 0.0, A.max)
-        store("sync", T.ch[b:b + 1, 0:NT], win, T[win[0]][0:NT, 0:1])
+        copy(V("junk", 0, NU), V("p", 0, NU), "s", scale=-1.0, bias=last, func=AF.Sign, accum=win)
+        ts(V("zz", 0, 24), V("p", 15, NU, 16), last, A.is_lt, 16.0, A.mult)
+        reduce(h1, V("zz", 0, 25), A.add)
+        copy(V("xtile", 1, 4 * XL, 4), V("mask", 0, XL), OPT["x1q"][b], scale=h1)
+        ts(V("xtile", 0, 4 * XL, 4), V("mb", 0, XL), win, A.add, h1, A.subtract)
+        store("y", T.ch[b:b + 1, 0:NT], win, T[win[0]][0:NT, 0:1])
         quant(xl, V("xtile", 0, 512))
-        codes = OPT["early"][b] == "codes"
-        if codes:
+        apart = OPT["early"][b] == "apart"
+        if apart:
             send2(partner, (V(xf, EX, EX + 6), V(xf + "s", EX, EX + 24)), (V(xl[0], MK, XL), V(xl[0] + "s", MK, MK + 24)), "ae%d" % b, "le")
         mm(6, V("r16", 0, 128), xl)
-        ts(lown, V("ps6", MK, XL), 192.0, A.add)
-        look = V(lx[0], 6, 12) if codes else V("look%d" % b, 0, 6)
-        if not codes:
+        ts(lown, V("ps6", MK, XL), LO, A.add)
+        if not apart:
             send(partner, look, lown, "ae%d" % b, "le")
         pick(V(xq, 0, NT), V(tab, 0, NU), lown)
         mm(7, V("r1", 0, 128), xl, True, False)
         mm(7, xl, V("negw", 0, 128), False, True)
         for t in range(4):
-            mm(t, E("e75", t), V(xq, 0, 128), False, True)
+            mm(t, E("e3", t), V(xq, 0, 128), False, True)
         tt(V("pre", 0, 24), V("xtile", 4 * MK, 4 * XL), V("cdig", 0, 24), A.subtract)
         reduce(V("flag", 0, 1), V("ps7", 0, ONE + 1), A.min, absv=True)
-        ts(V("xtile", 4 * LX, 4 * LX + 24, 1, 0, NT), V("pre", 0, 24, 1, 0, NT), V("flag", 0, 1, 1, 0, NT), A.mult)
+        copy(V("xtile", 4 * LX, 4 * LX + 24, 1, 0, NT), V("pre", 0, 24, 1, 0, NT), OPT["flq"][b], scale=V("flag", 0, 1, 1, 0, NT))
         quant(V(xf, 0, 128), V("xtile", 0, 512))
-        if codes:
-            arrive([V(xf, EX, EX + 6), V(xf + "s", EX, EX + 24)], "ae%d" % b, partner)
-            mm(4, V("r16", 0, 128), V(xf, 6, 134))
-            ts(V(lx[0], 0, 12), V("ps4", LX - 6, 128), 192.0, A.add)
-        else:
+        mm(4, V("r16", 0, 128), V(xf, 0, 128))
+        ts(lx, V("ps4", LX, 128), 192.0, A.add)
+        if not apart:
             arrive([look], "ae%d" % b, partner)
-            mm(4, V("r16", 0, 128), V(xf, 0, 128))
-            ts(lx, V("ps4", LX, 128), 192.0, A.add)
         for t in range(4):
-            copy(V("tl", NTL + t, NTL + 4 * NT, 4), V("ps%d" % t, 0, NT), eng(OPT["ntq"][t]), scale=0.5)
+            copy(V("tl", NTL + t, NTL + 4 * NT, 4), V("ps%d" % t, 0, NT), OPT["ntq"][t], scale=0.5)
+        if apart:
+            arrive([V(xf, EX, EX + 6), V(xf + "s", EX, EX + 24)], "ae%d" % b, partner)
+            mm(0, V("r16", 0, 128), V(xf, 6, 134))
+            ts(look, V("ps0", LX, 128), LO, A.add)
         quant(V(tab, OWN, OWN + 128), V("tl", NTL, NTL + 512))
         for x in (tab, tab + "s"):
             send(partner, V(x, PAR, PAR + NT), V(x, OWN, OWN + NT), "ac%d" % b, "lc")
@@ -426,38 +410,22 @@ def _calls(core, T, topo):
         arrive([land], "al%d" % b, partner)
         arrive([V(tab, PAR, PAR + NT), V(tab + "s", PAR, PAR + NT)], "ac%d" % b, partner, 2)
         copy(V("c1", 0, NT), src, OPT["c1q"], off=look)
-        if OPT["valq"] == "s":
-            copy(V("sg", 0, NT), V("c1", 0, NT), "scalar", bias=0.5 - OWN, func=AF.Sign)
-            copy(V("both", 0, NT), V("sg", 0, NT), "scalar", scale=(MRG - PAR) / 2.0)
-        elif OPT["valq"] == "g":
-            copy(V("sg", 0, NT), src, "scalar", bias=0.5 - OWN, func=AF.Sign, off=look)
-            copy(V("both", 0, NT), V("sg", 0, NT), "scalar", scale=(MRG - PAR) / 2.0)
-        else:
-            ts(V("both", 0, NT), V("c1", 0, NT), OWN - 0.5, A.is_ge, float(MRG - PAR), A.mult)
+        ts(V("both", 0, NT), src, OWN - 0.5, A.is_ge, float(MRG - PAR), A.mult, off=look)
         scan(V("c2", 0, NT), V("mw", 0, NT), V("c1", 0, NT), 0.0, A.mult, A.add)
         ts(V("clist", 0, 6), V("c2", 15, NT, 16), V("esc", 0, 1), A.mult, -0.34, A.add)
         tt(V("val", 0, NT), V("both", 0, NT), V("jpar", 0, NT), A.add)
-        if OPT["merge"][b] == "A":
-            pick(V(xq, SM, SM + NT), V(tab, 0, PAR), V("clist", 0, 6))
-            sides = (V(xq, SM - 32, SM + NT), V(tab, PAR - 32, PAR + NT))
-            for k, x in enumerate(sides if OPT["ownfirst"][b] else sides[::-1]):
-                for t in range(4):
-                    mm(t, E("e25", t), x, k == 0, k == 1)
-        else:
-            for t in range(4):
-                mm(t, E("e25", t), V(tab, OWN, OWN + 128))
-                copy(V("junk", NU + NT * t, NU + NT * t + NT), V("ps%d" % t, 0, NT), eng(OPT["dq"][t]))
-            for t in range(4):
-                copy(V("dg", NT * t, NT * t + NT), V("junk", NT * t, NU + NT * t + NT), eng(OPT["gq"][t]), off=V("clist", 0, 6))
-                mm(t, E("e25", t), V(tab, PAR - 32, PAR + NT))
-        scatter(src, land, V("val", 0, NT))
-        scan(V("srcs", 0, NU), V("mw", 0, NU), V(src[0], 0, NU), 0.0, A.mult, A.add)
-        ts(V("blist", 0, 24), V("srcs", 15, NU, 16), V("esc", 0, 1), A.mult, -0.34, A.add)
         for t in range(4):
-            if OPT["merge"][b] == "A":
-                copy(V("tl", MT + t, MT + 4 * NT, 4), V("ps%d" % t, 32, 128), eng(OPT["mtq"][t]))
-            else:
-                tt(V("tl", MT + t, MT + 4 * NT, 4), V("dg", NT * t, NT * t + NT), V("ps%d" % t, 32, 128), A.add)
+            mm(4 + t, E("e1", t), V(tab, OWN, OWN + 128))
+            copy(V("junk", NU + NT * t, NU + NT * t + NT), V("ps%d" % (4 + t), 0, NT), OPT["dq"][t])
+        for t in range(4):
+            copy(V("dg", NT * t, NT * t + NT), V("junk", NT * t, NU + NT * t + NT), OPT["gq"][t], off=V("clist", 0, 6))
+            mm(t, E("e1", t), V(tab, PAR - 32, PAR + NT))
+        scatter(src, land, V("val", 0, NT))
+        for u, v in _cut(OPT["bs"][b]):
+            scan(V("srcs", u, v), V("mw", 0, v - u), V(src[0], u, v), 0.0, A.mult, A.add)
+            ts(V("blist", u // 16, v // 16), V("srcs", u + 15, v, 16), V("esc", 0, 1), A.mult, -0.34, A.add)
+        for t in range(4):
+            tt(V("tl", MT + t, MT + 4 * NT, 4), V("dg", NT * t, NT * t + NT), V("ps%d" % t, 32, 128), A.add)
         quant(V(tab, MRG, MRG + 128), V("tl", MT, MT + 512))
         for k, (u, v) in enumerate(_cut(OPT["tab" if b + 1 < NR else "fin"])):
             pick(V(nxt, u, v), V(tab, 0, WIN), V("blist", u // 16, v // 16))
@@ -467,12 +435,12 @@ def _calls(core, T, topo):
 
     for k, (u, v) in enumerate(_cut(OPT["fin"])):
         mm(4 + k, V("wq", 0, 128), V("fin", u, v))
-        copy(V("ysb", u, v), V("ps%d" % (4 + k), 0, v - u), eng(OPT["yq"][k]))
-        store("sync", T.y[:, u:v], V("ysb", u, v), T.ysb[:, u:v])
-    for u, v in [(0, NU)] if OPT["ocwhole"] else _cut(OPT["fin"]):
-        store("sync", T.oc[:, 4 * u:4 * v], V("fin", u, v), T.fin[:, u:v].bitcast(dt.uint8))
+        copy(V("ysb", u, v), V("ps%d" % (4 + k), 0, v - u), OPT["yq"][k])
+        store(OPT["ysq"][k], T.y[:, u:v], V("ysb", u, v), T.ysb[:, u:v])
+    for k, (u, v) in enumerate(_cut(OPT["fin"])):
+        store(OPT["ocq"][k], T.oc[:, 4 * u:4 * v], V("fin", u, v), T.fin[:, u:v].bitcast(dt.uint8))
     for k in range(4):
-        store("scalar", T.osc[4 * k:4 * k + 4, 0:NU], V("fins", 0, NU), T.fins[32 * k:32 * k + 4, 0:NU])
+        store(OPT["oscq"][k], T.osc[4 * k:4 * k + 4, 0:NU], V("fins", 0, NU), T.fins[32 * k:32 * k + 4, 0:NU])
     _record(rec, "sync", "end", None, [], [], stores)
     return rec["ops"], local
 

@@ -7,24 +7,29 @@ AF = ActivationFunctionType
 NU, NT, NR = 384, 96, 2
 OWN, PAR, MRG, WIN = 384, 512, 608, 736
 XQ = 96
-MK, XL, ONE, LX, EX = 96, 102, 102, 122, 128
+MK, UC, XL, ONE, EX = 96, 102, 103, 103, 128
+BP, BO, BS = 8, 32, 56
+LX = 48
 OFF = 8192.0
 LO = 192.0 + 7 * OFF
-MT, NTL, X0, ZZ, X1, KB = 0, 384, 768, 1152, 1280, 1664
 BIG = 16384.0
+MT, NTL, X0, ZZ, X1, KB = 0, 384, 768, 1152, 1280, 1664
 F4, F32, BF, U16, I32, U8 = "float8_e4m3fn_x4", "float32", "bfloat16", "uint16", "int32", "uint8"
-OPT = {"load": (256, 128), "tab": (192, 192), "fin": (192, 192), "bs": ((192, 192), (192, 192)), "early": ("apart", "list"),
-       "ntq": "sssv", "c1q": "s", "yq": "vv", "lq": "ysyy", "cq": "svvs", "gq": "ssss", "dq": "ssss", "flq": "vv", "x1q": "vv",
-       "oscq": "ssyy", "ysq": "yyy", "ocq": "yyy"}
-ORDER = [0, 1, 6, 31, 12, 5, 2, 14, 15, 16, 23, 7, 32, 17, 33, 13, 24, 37, 11, 36, 28, 25, 18, 29, 54, 19, 38, 45, 42, 39, 41, 66, 43, 46, 40, 34,
-         9, 21, 35, 44, 69, 30, 10, 20, 22, 57, 3, 70, 56, 4, 72, 71, 73, 78, 47, 26, 74, 8, 48, 55, 79, 80, 63, 76, 75, 81, 27, 77, 58, 82, 83,
-         84, 60, 85, 59, 86, 87, 64, 65, 91, 97, 88, 92, 61, 90, 89, 49, 98, 52, 62, 94, 50, 93, 99, 95, 104, 96, 100, 105, 106, 103, 53, 101,
-         51, 102, 110, 113, 114, 111, 112, 107, 108, 122, 126, 109, 124, 68, 115, 128, 117, 118, 127, 123, 116, 135, 119, 125, 131, 121, 133,
-         129, 137, 120, 138, 130, 134, 67, 132, 139, 136, 145, 143, 140, 158, 144, 146, 141, 157, 156, 147, 142, 148, 149, 152, 153, 150, 151,
-         154, 155, 160, 161, 162, 163, 165, 164, 166, 178, 167, 172, 173, 168, 159, 179, 169, 171, 170, 180, 176, 181, 177, 187, 188, 182, 174,
-         175, 183, 185, 186, 192, 193, 184, 189, 196, 197, 190, 207, 201, 191, 203, 198, 208, 205, 200, 202, 204, 199, 206, 194, 217, 209, 211,
-         215, 218, 220, 213, 195, 210, 212, 216, 222, 214, 223, 225, 224, 221, 226, 219, 229, 230, 227, 228, 238, 234, 235, 237, 231, 239, 236,
-         240, 232, 241, 233, 242, 243]
+OPT = {"load": (224, 160), "tab": (192, 192), "fin": (192, 192), "yp": (192, 192), "ysp": (384,), "ocp": (384,),
+       "lq": "ffff", "oscq": "ffff", "ysq": "fff", "ocq": "fff", "rq": "f"}
+SQ = [int(x) for x in """
+13 18 19 20 21 22 23 25 26 27 28 29 30 33 34 35 36 37 38 41 42 43 44 46 47 48 49 50 51 52 53 54 85 96 98 100 102 109 110 111 113 114 118 129 131 135
+140 143 147 150 156 165 169 179 182 192 196 200 205 206 209 210 225 229 231 236 240 241 245 248 251 259 261 267 271 275 276
+""".split()]
+ORDER = [int(x) for x in """
+6 1 39 0 2 40 3 5 14 7 22 15 13 36 11 16 24 49 12 30 32 25 9 31 17 18 28 20 72 69 59 60 73 75 76 21 27 29 23 19 4 35 74 33 57 77 80 67 8 34 38 37 82
+46 83 66 84 58 86 85 50 108 81 78 26 44 87 79 52 61 88 90 68 51 93 94 62 47 53 43 63 111 110 48 109 89 91 92 137 136 115 117 95 64 96 118 112 65 97 41
+54 119 99 101 98 120 10 56 103 100 122 104 102 123 105 138 106 132 124 55 130 139 114 107 121 113 116 45 42 128 160 143 134 140 129 146 141 126 144
+133 145 125 135 148 131 142 147 127 151 154 161 153 157 149 150 156 155 152 162 158 163 159 70 165 164 166 175 169 168 167 170 171 71 177 178 176 180
+181 179 204 173 184 183 211 172 208 207 186 189 182 209 206 190 187 213 191 205 192 214 185 215 174 210 193 199 200 212 188 195 216 197 218 196 194
+198 232 234 219 201 222 226 221 230 233 228 220 241 217 262 235 236 229 202 203 227 231 237 223 242 238 224 239 243 263 225 244 251 248 254 264 252
+255 253 249 246 245 256 250 247 265 257 266 240 258 268 259 273 260 261 270 271 269 267 272 276 277 275 274 278
+""".split()]
 
 
 def _decl():
@@ -39,35 +44,34 @@ def _decl():
     for b in range(NR):
         pair("tab%d" % b, WIN)
         pair("xq%d" % b, XQ + 128)
-        pair("xl%d" % b, 128)
-        pair("xf%d" % b, EX + 32)
-        for n in ("lown", "land", "look", "lx"):
-            add("%s%d" % (n, b), 8, U16)
-        add("src%d" % b, 480, F32)
+        pair("xl%d" % b, EX + 32)
+        pair("xb%d" % b, BO + 128)
         add("win%d" % b, 1, F32)
+        add("lown%d" % b, 8, U16)
+        add("look%d" % b, 8, U16)
     for n in ("e1", "e3"):
         pair(n, 512)
-    for n in ("r16", "r1", "negw"):
+    for n in ("r16", "r1", "negw", "ao", "ap"):
         pair(n, 128)
         add("t" + n, 512, BF)
     pair("wq", 128)
     pair("fin", NU)
     for n in range(8):
         add("ps%d" % n, 512, F32, "psum")
-    for n, w, t in (("tl", KB + 4 * NU, BF), ("te", 520, BF), ("wt", 512, BF), ("xtile", 512, BF), ("dd", 128, BF), ("mask", XL, BF),
-                    ("junk", 2 * NU, BF), ("dg", NU, BF), ("mb", XL, BF), ("cmod", 128, BF), ("eq16", 128, BF), ("ma", 16, BF),
-                    ("mc", 16, BF), ("mw", NU, BF), ("cdig", 24, BF), ("pre", 24, BF),
-                    ("ip", 1, I32), ("pi", 2, I32), ("clist", 6, U16), ("blist", 24, U16)):
+    for n, w, t in (("tl", KB + 4 * NU, BF), ("te", 520, BF), ("wt", 512, BF), ("xtile", 512, BF), ("btile", 512, BF), ("dd", 128, BF),
+                    ("mask", XL, BF), ("junk", 2 * NU, BF), ("dg", NU, BF), ("src", 480, BF), ("jown", NT, BF), ("mc", NT, BF),
+                    ("mw", NT, BF), ("cdig", 24, BF), ("mb", XL, BF), ("cmod", 128, BF), ("krow", 24, BF), ("pre", 216, BF),
+                    ("ip", 1, I32), ("pi", 2, I32), ("lx", 6, U16), ("clist", 6, U16), ("blist", 24, U16)):
         add(n, w, t)
-    for n, w in (("jown", NT), ("jpar", NT), ("pf", 2), ("p", NU), ("zz", 25), ("h1", 1), ("flag", 1), ("pmo", 1), ("esc0", 1), ("esc", 1),
-                 ("c1", NT), ("c2", NT), ("both", NT), ("val", NT), ("srcs", NU), ("ysb", NU)):
+    for n, w in (("pf", 2), ("pg", 2), ("pmo", 1), ("esc", 1), ("c1", NT), ("c2", NT), ("p", NU), ("zz", 25), ("h1", 1), ("flag", 1),
+                 ("cl", 24), ("sl", 24), ("bl", 24), ("ysb", NU), ("yw", MRG + NT)):
         add(n, w, F32)
     return s
 
 
 SCRATCH = _decl()
 NCOMP, NHW = 100, 24
-REMOTE = ["%s%d" % (n, b) for b in range(NR) for n in ("ae", "al", "ac")] + ["le", "ll", "lc"]
+REMOTE = ["%s%d" % (n, b) for b in range(NR) for n in ("ae", "al", "ac", "au")] + ["le", "ll", "lc"]
 SEMAPHORES = ["c%d" % i for i in range(NCOMP)] + ["h%d" % i for i in range(NHW)] + REMOTE
 
 
@@ -87,7 +91,7 @@ def _record(rec, queue, kind, call, reads, writes, extra=(), tag=None):
                 if v[0][:2] == "ps":
                     if uq == "tensor" and queue == "tensor":
                         soft.add(j)
-                    elif uq != queue or uw:
+                    else:
                         deps.add(j)
                 elif (w or uw) and _clash(u, v):
                     deps.add(j)
@@ -98,8 +102,7 @@ def _record(rec, queue, kind, call, reads, writes, extra=(), tag=None):
         if deps:
             raise ValueError("a landing buffer is in use")
         soft = set(j for j in range(i) if ops[j]["tag"] == call[0])
-    ops.append({"queue": queue, "kind": kind, "call": call, "deps": deps, "soft": soft, "need": False, "tag": tag,
-                "out": writes[0] if writes else (reads[0] if reads else None)})
+    ops.append({"queue": queue, "kind": kind, "call": call, "deps": deps, "soft": soft, "need": False, "tag": tag})
     return i
 
 
@@ -162,7 +165,7 @@ def _calls(core, T, topo):
     rank = T.rank_of(core)
     rec = {"ops": [], "acc": {}}
     local = {"le": 0, "ll": 0, "lc": 0}
-    eng = {"v": "vector", "s": "scalar", "y": "sync"}
+    eng = {"s": "scalar", "y": "sync"}
 
     def ap(v):
         return T[v[0]][v[4]:v[5], v[1]:v[2]] if v[3] == 1 else T[v[0]][v[4]:v[5], v[1]:v[2]:v[3]]
@@ -182,15 +185,7 @@ def _calls(core, T, topo):
     def memset(out, c):
         _record(rec, "vector", "comp", lambda q: q.memset(ap(out), c), [], [out])
 
-    def copy(out, in_, queue="v", scale=None, bias=None, off=None, func=None, accum=None):
-        if queue == "v":
-            if bias is not None:
-                return ts(out, in_, scale, A.mult, bias, A.add)
-            if scale is not None:
-                return ts(out, in_, scale, A.mult)
-            _record(rec, "vector", "comp", lambda q: q.tensor_copy(ap(out), by(in_, off)), views(in_, off), [out])
-            return
-        f = func or (AF.Copy if bias is None else AF.Identity)
+    def act(out, in_, func, scale=None, bias=None, off=None, accum=None):
         kw = {}
         if scale is not None:
             kw["scale"] = val(scale)
@@ -198,14 +193,28 @@ def _calls(core, T, topo):
             kw["bias"] = val(bias)
         if accum is not None:
             kw["accum_out"] = ap(accum)
-        _record(rec, "scalar", "comp", lambda q: q.activation(ap(out), by(in_, off), f, **kw), views(in_, scale, bias, off), views(accum, out))
+        _record(rec, "scalar", "comp", lambda q: q.activation(ap(out), by(in_, off), func, **kw), views(in_, scale, bias, off), views(accum, out))
 
-    def ts(out, in0, s1, op0, s2=None, op1=None, off=None):
+    def copy(out, in_, scale=None, bias=None, off=None):
+        if len(rec["ops"]) in SQ:
+            return act(out, in_, AF.Copy if bias is None else AF.Identity, scale, bias, off)
+        if bias is not None and scale is not None:
+            return ts(out, in_, scale, A.mult, bias, A.add)
+        if bias is not None:
+            return ts(out, in_, bias, A.add)
+        if scale is not None:
+            return ts(out, in_, scale, A.mult)
+        vcopy(out, in_, off)
+
+    def vcopy(out, in_, off=None):
+        _record(rec, "vector", "comp", lambda q: q.tensor_copy(ap(out), by(in_, off)), views(in_, off), [out])
+
+    def ts(out, in0, s1, op0, s2=None, op1=None):
         def call(q):
             if op1 is None:
-                return q.tensor_scalar(ap(out), by(in0, off), val(s1), None, op0)
-            return q.tensor_scalar(ap(out), by(in0, off), val(s1), val(s2), op0, op1)
-        _record(rec, "vector", "comp", call, views(in0, s1, s2, off), [out])
+                return q.tensor_scalar(ap(out), ap(in0), val(s1), None, op0)
+            return q.tensor_scalar(ap(out), ap(in0), val(s1), val(s2), op0, op1)
+        _record(rec, "vector", "comp", call, views(in0, s1, s2), [out])
 
     def tt(out, in0, in1, op):
         _record(rec, "vector", "comp", lambda q: q.tensor_tensor(ap(out), ap(in0), ap(in1), op), [in0, in1], [out])
@@ -236,8 +245,7 @@ def _calls(core, T, topo):
     def pick(out, win, off):
         _record(rec, "vector", "comp",
                 lambda q: q.tensor_copy(ap(out).bitcast(dt.uint32), ap(win).bitcast(dt.uint32).indirect(ap(off))), [win, off], [out])
-        _record(rec, "scalar", "comp", lambda q: q.activation(ap(sc(out)), ap(sc(win)).indirect(ap(off)), AF.Copy),
-                [sc(win), off], [sc(out)])
+        copy(sc(out), sc(win), off=off)
 
     def iota(out, pattern, base, cm):
         f = SCRATCH[out[0]][2] != I32
@@ -248,22 +256,35 @@ def _calls(core, T, topo):
             return q.iota(ap(out), pattern, base, cm)
         _record(rec, "gpsimd", "comp", call, [], [out])
 
+    def fill(name, a, b, c, st=1):
+        n = len(range(a, b, st))
+        if n > 128:
+            return memset(V(name, a, b, st), c)
+        copy(V(name, a, b, st), V("dd", 0, n), scale=0.0, bias=c if c else None)
+
+    def dq(queue):
+        return eng[queue] if queue in eng else "scalar" if len(rec["ops"]) in SQ else "sync"
+
     def load(queue, out, src, after=()):
-        return _record(rec, eng[queue], "dma", lambda q: q.dma_start(ap(out), src), [], [out], after)
+        return _record(rec, dq(queue), "dma", lambda q: q.dma_start(ap(out), src), [], [out], after)
 
     stores = []
 
     def store(queue, dst, in_, view):
-        stores.append(_record(rec, eng[queue], "dma", lambda q: q.dma_start(dst, view), [in_], []))
+        stores.append(_record(rec, dq(queue), "dma", lambda q: q.dma_start(dst, view), [in_], []))
 
     def raw(v):
         return ap(v).bitcast(dt.uint8) if SCRATCH[v[0]][2] == F4 else ap(v)
 
-    def send(dst, out, in_, arr, loc):
+    def send1(dst, out, in_, arr, loc):
         rid, pid, _s = topo.addr(dst)
         local[loc] += len(topo.engines(core, dst))
         _record(rec, "gpsimd", "remote", lambda q: q.remote_dma(raw(out), raw(in_), T.sem[arr], T.sem[loc], pid, rid, topo.mask(core, dst)),
                 [in_], [], tag=arr)
+
+    def send(dst, out, in_, arr, loc):
+        send1(dst, out, in_, arr, loc)
+        send1(dst, sc(out), sc(in_), arr, loc)
 
     def send2(dst, outs, ins, arr, loc):
         rid, pid, _s = topo.addr(dst)
@@ -283,58 +304,55 @@ def _calls(core, T, topo):
     first = [load(OPT["lq"][0], V("tl", X0, X0 + 384), T.x[:, 0:384])]
     for k, (u, v) in enumerate(_cut(OPT["load"])):
         first.append(load(OPT["lq"][k + 1], V("tl", KB + 4 * u, KB + 4 * v), T.kb[:, 4 * u:4 * v]))
-    load("y", V("tl", X1, X1 + 384), T.x[:, 384:768], first)
-    load("y", V("wt", 0, 512), T.w[:, 0:512], first)
+    load(OPT["rq"], V("tl", X1, X1 + 384), T.x[:, 384:768], first)
+    load(OPT["rq"], V("wt", 0, 512), T.w[:, 0:512], first)
 
     iota(V("dd", 0, 128), [[1, 128]], 0, -1)
     iota(V("ip", 0, 1), [[0, 1]], 0, 1)
     iota(V("cmod", 0, 128), [[0, 8], [1, 16]], 0, 0)
-    iota(V("jown", 0, NT), [[1, NT]], OWN, 0)
-    iota(V("jpar", 0, NT), [[1, NT]], PAR, 0)
-    for b in range(NR):
-        iota(V("src%d" % b, 0, 480), [[1, 480]], 0, 0)
+    iota(V("krow", 0, 24), [[16, 24]], -192, 0)
+    iota(V("jown", 0, NT), [[1, NT]], 0, 0)
+    fill("src", 0, 480, 0.0)
     memset(V("te", 0, 520), 0.0)
     ts(V("te", 4, 516, 4), V("dd", 0, 128), 0.0, A.is_equal, 0.5, A.mult)
-    memset(V("tl", ZZ, ZZ + 128), 0.0)
+    fill("tl", ZZ, ZZ + 128, 0.0)
     ts(V("pi", 0, 1), V("ip", 0, 1), 15, A.bitwise_and)
     ts(V("pi", 1, 2), V("ip", 0, 1), 4, A.logical_shift_right)
-    copy(V("pf", 0, 2), V("pi", 0, 2))
-    ts(V("eq16", 0, 128), V("cmod", 0, 128), pm, A.is_equal)
-    cq = OPT["cq"]
-    for t in range(4):
-        copy(V("tr16", t, 512, 4), V("eq16", 0, 128), cq[0], scale=16.0 if t == 3 else 1.0)
-    for n, c, q in (("tr1", 1.0, cq[1]), ("tnegw", -1.0, cq[2])):
-        if q == "v":
-            memset(V(n, 0, 512), c)
-        else:
-            for t in range(3):
-                copy(V(n, t, 512, 4), V("dd", 0, 128), q, scale=0.0, bias=c)
+    vcopy(V("pf", 0, 2), V("pi", 0, 2))
+    ts(V("tr16", 0, 512, 4), V("cmod", 0, 128), pm, A.is_equal)
+    for t in range(1, 4):
+        copy(V("tr16", t, 512, 4), V("tr16", 0, 512, 4), scale=16.0 if t == 3 else 1.0)
+    for t in range(3):
+        copy(V("tr1", t, 512, 4), V("dd", 0, 128), scale=0.0, bias=1.0)
     ts(V("tr1", 3, 512, 4), V("dd", 0, 128), 0.0, A.is_le, 512.0, A.mult)
-    copy(V("tnegw", 3, 512, 4), V("dd", 0, 128), cq[2], scale=0.0)
-    copy(V("tnegw", 4 * MK, 4 * ONE + 4), V("dd", 0, 28), cq[2], scale=0.0)
-    q = cq[3]
-    copy(V("mask", 0, MK), V("te", 4, 4 + 4 * MK, 4), q, scale=2.0)
-    ts(V("mask", MK, XL), V("cmod", 0, 6), pd, A.is_equal)
-    copy(V("mb", 0, XL), V("mask", 0, XL), q, scale=OFF, bias=-OFF - 192.0)
-    memset(V("zz", 24, 25), -192.0)
-    copy(V("xtile", 4 * NT, 512), V("dd", 0, 128), q, scale=0.0)
-    copy(V("xtile", 2, 4 * NT, 4), V("dd", 0, NT), q, scale=0.0)
-    copy(V("xtile", 3, 4 * NT, 4), V("mask", 0, NT), q)
-    copy(V("xtile", 4 * ONE + 2, 4 * ONE + 3), V("mask", 0, 1), q)
-    copy(V("xtile", 4 * LX, 4 * LX + 24, 4, 96, 112), V("dd", 0, 6, 1, 96, 112), q, scale=0.0, bias=V("pf", 0, 1, 1, 96, 112))
-    copy(V("xtile", 4 * LX + 1, 4 * LX + 24, 4, 96, 112), V("dd", 0, 6, 1, 96, 112), q, scale=0.0, bias=192.0)
-    copy(V("xtile", 4 * LX + 3, 4 * LX + 24, 4, 96, 112), V("cmod", 0, 6, 1, 96, 112), q)
-    copy(V("pmo", 0, 1), pm, q, scale=1.0, bias=OFF)
+    for t in range(4):
+        copy(V("tnegw", t, 4 * MK, 4), V("dd", 0, MK), scale=0.0, bias=-1.0 if t < 3 else None)
+    fill("tnegw", 4 * MK, 512, 0.0)
+    copy(V("mask", 0, MK), V("te", 4, 4 + 4 * MK, 4), scale=2.0)
+    ts(V("mask", MK, UC), V("cmod", 0, 6), pd, A.is_equal)
+    ts(V("mask", UC, XL), pd, 5.5, A.is_le)
+    copy(V("mb", 0, XL), V("mask", 0, XL), scale=OFF, bias=-OFF - 192.0)
+    fill("zz", 24, 25, -192.0)
+    fill("xtile", 4 * NT, 512, 0.0)
+    fill("xtile", 2, 4 * NT, 0.0, 4)
+    copy(V("xtile", 3, 4 * NT, 4), V("mask", 0, NT))
+    copy(V("xtile", 4 * ONE + 2, 4 * ONE + 3), V("mask", 0, 1))
+    fill("btile", 0, 512, 0.0)
+    fill("pre", 0, 192, 0.0)
+    for n in ("tao", "tap"):
+        fill(n, 3, 512, 0.0, 4)
+    copy(V("pg", 0, 1), pm, scale=1.0 / PAR)
+    copy(V("pg", 1, 2), pd, scale=16.0 / PAR)
+    ts(V("cl", 0, 24), V("krow", 0, 24), pm, A.add, 192.0, A.add)
+    copy(V("btile", 4 * LX, 4 * LX + 24, 4, 96, 112), V("dd", 0, 6, 1, 96, 112), scale=0.0, bias=V("pf", 0, 1, 1, 96, 112))
+    copy(V("btile", 4 * LX + 1, 4 * LX + 24, 4, 96, 112), V("dd", 0, 6, 1, 96, 112), scale=0.0, bias=192.0)
+    copy(V("btile", 4 * LX + 3, 4 * LX + 24, 4, 96, 112), V("cmod", 0, 6, 1, 96, 112))
+    copy(V("pmo", 0, 1), pm, bias=OFF)
     for t, s in enumerate((V("pmo", 0, 1), 0.0, 192.0, pd)):
-        copy(V("cdig", t, 24, 4), V("mask", MK, XL), q, scale=s, bias=None if t else -OFF)
-    copy(V("ma", 0, 16), V("eq16", 0, 16), "s", scale=-1.0, bias=1.0)
-    copy(V("mc", 0, 1), V("eq16", 0, 1), "s", scale=0.0)
-    copy(V("mc", 1, 16), V("eq16", 0, 15), "s", scale=BIG)
-    tt(V("mw", 0, 16), V("ma", 0, 16), V("mc", 0, 16), A.max)
-    for c, n in ((16, 16), (32, 32), (64, 64), (128, 128), (256, 128))[:5 if max(max(x) for x in OPT["bs"]) > 256 else 4]:
-        copy(V("mw", c, c + n), V("mw", 0, n), "s")
-    copy(V("esc0", 0, 1), pm, "s", bias=-14.0, func=AF.Relu)
-    copy(V("esc", 0, 1), V("esc0", 0, 1), "s", scale=1.0 - 1.0 / BIG, bias=1.0 / BIG)
+        copy(V("cdig", t, 24, 4), V("mask", MK, UC), scale=s, bias=None if t else -OFF)
+    copy(V("mc", 0, NT), V("tr16", 60, 60 + 4 * NT, 4), scale=BIG, bias=1.0)
+    tt(V("mw", 0, NT), V("mc", 0, NT), V("tr16", 0, 4 * NT, 4), A.subtract)
+    ts(V("esc", 0, 1), pm, 15.0, A.is_equal, 1.0 / BIG, A.max)
     for n in ("e1", "e3"):
         if n == "e3":
             ts(V("te", 4, 516, 4), V("dd", 0, 128), 0.0, A.is_equal, 1.5, A.mult)
@@ -346,7 +364,7 @@ def _calls(core, T, topo):
     quant(V("xq1", XQ, XQ + 128), V("tl", X1, X1 + 512))
     quant(V("wq", 0, 128), V("wt", 0, 512))
 
-    def E(n, t):
+    def E(t, n="e1"):
         return V(n, 128 * t, 128 * t + 128)
 
     def score(b, k, u, v):
@@ -355,89 +373,102 @@ def _calls(core, T, topo):
     def run_max(k, u, v):
         scan(V("p", u, v), V("te", 1, 1 + 2 * (v - u), 2), V("ps%d" % (4 + k), 0, v - u), V("p", u - 1, u) if u else -1e29, A.add, A.max)
 
+    def ypart(ps, tab, u, v, pad=0):
+        mm(ps, V("wq", 0, 128), V(tab, u - pad, max(v, u - pad + 128)))
+        copy(V("yw", u, v), V("ps%d" % ps, pad, pad + v - u))
+
     for k, (u, v) in enumerate(_cut(OPT["load"])):
         quant(V("tab0", u, v), V("tl", KB + 4 * u, KB + 4 * v))
         score(0, k, u, v)
         run_max(k, u, v)
 
     for b in range(NR):
-        tab, xq, nxt = "tab%d" % b, "xq%d" % b, "tab%d" % (b + 1) if b + 1 < NR else "fin"
-        win, src = V("win%d" % b, 0, 1), V("src%d" % b, 0, 480)
-        lown, lx, land, look = [V("%s%d" % (n, b), 0, 6) for n in ("lown", "lx", "land", "look")]
-        xl, xf = V("xl%d" % b, 0, 128), "xf%d" % b
+        tab, xq, xl, xb = ["%s%d" % (n, b) for n in ("tab", "xq", "xl", "xb")]
+        nxt = "tab%d" % (b + 1) if b + 1 < NR else "fin"
+        win, lown, look, cl = V("win%d" % b, 0, 1), V("lown%d" % b, 0, 6), V("look%d" % b, 0, 6), V("cl", 0, 24)
         partner = T.cores[rank ^ (1 << b)]
         for t in range(4):
-            mm(t, E("e1", t), V(xq, XQ, XQ + 128), True, False)
+            mm(t, E(t), V(xq, XQ, XQ + 128), True, False)
         last, h1 = V("p", NU - 1, NU), V("h1", 0, 1)
-        copy(V("junk", 0, NU), V("p", 0, NU), "s", scale=-1.0, bias=last, func=AF.Sign, accum=win)
+        act(V("junk", 0, NU), V("p", 0, NU), AF.Sign, scale=-1.0, bias=last, accum=win)
         ts(V("zz", 0, 24), V("p", 15, NU, 16), last, A.is_lt, 16.0, A.mult)
         reduce(h1, V("zz", 0, 25), A.add)
-        copy(V("xtile", 1, 4 * XL, 4), V("mask", 0, XL), OPT["x1q"][b], scale=h1)
+        copy(V("xtile", 1, 4 * XL, 4), V("mask", 0, XL), scale=h1)
         ts(V("xtile", 0, 4 * XL, 4), V("mb", 0, XL), win, A.add, h1, A.subtract)
-        store("y", T.ch[b:b + 1, 0:NT], win, T[win[0]][0:NT, 0:1])
-        quant(xl, V("xtile", 0, 512))
-        apart = OPT["early"][b] == "apart"
-        if apart:
-            send2(partner, (V(xf, EX, EX + 6), V(xf + "s", EX, EX + 24)), (V(xl[0], MK, XL), V(xl[0] + "s", MK, MK + 24)), "ae%d" % b, "le")
-        mm(6, V("r16", 0, 128), xl)
-        ts(lown, V("ps6", MK, XL), LO, A.add)
-        if not apart:
-            send(partner, look, lown, "ae%d" % b, "le")
+        if b + 1 == NR:
+            ypart(4, tab, 0, NU)
+        store(OPT["rq"], T.ch[b:b + 1, 0:NT], win, T[win[0]][0:NT, 0:1])
+        quant(V(xl, 0, 128), V("xtile", 0, 512))
+        send2(partner, (V(xl, EX, EX + 2), V(xl + "s", EX, EX + 8)), (V(xl, UC, UC + 2), V(xl + "s", UC, UC + 8)), "au%d" % b, "le")
+        mm(6, V("r16", 0, 128), V(xl, 0, 128))
+        ts(lown, V("ps6", MK, UC), LO, A.add)
+        send1(partner, look, lown, "ae%d" % b, "le")
+        mm(7, V("r1", 0, 128), V(xl, 0, 128), True, False)
+        mm(7, V(xl, 0, 128), V("negw", 0, 128), False, True)
         pick(V(xq, 0, NT), V(tab, 0, NU), lown)
-        mm(7, V("r1", 0, 128), xl, True, False)
-        mm(7, xl, V("negw", 0, 128), False, True)
         for t in range(4):
-            mm(t, E("e3", t), V(xq, 0, 128), False, True)
-        tt(V("pre", 0, 24), V("xtile", 4 * MK, 4 * XL), V("cdig", 0, 24), A.subtract)
-        reduce(V("flag", 0, 1), V("ps7", 0, ONE + 1), A.min, absv=True)
-        copy(V("xtile", 4 * LX, 4 * LX + 24, 1, 0, NT), V("pre", 0, 24, 1, 0, NT), OPT["flq"][b], scale=V("flag", 0, 1, 1, 0, NT))
-        quant(V(xf, 0, 128), V("xtile", 0, 512))
-        mm(4, V("r16", 0, 128), V(xf, 0, 128))
-        ts(lx, V("ps4", LX, 128), 192.0, A.add)
-        if not apart:
-            arrive([look], "ae%d" % b, partner)
-        for t in range(4):
-            copy(V("tl", NTL + t, NTL + 4 * NT, 4), V("ps%d" % t, 0, NT), OPT["ntq"][t], scale=0.5)
-        if apart:
-            arrive([V(xf, EX, EX + 6), V(xf + "s", EX, EX + 24)], "ae%d" % b, partner)
-            mm(0, V("r16", 0, 128), V(xf, 6, 134))
-            ts(look, V("ps0", LX, 128), LO, A.add)
+            mm(t, E(t, "e3"), V(xq, 0, 128), False, True)
+            copy(V("tl", NTL + t, NTL + 4 * NT, 4), V("ps%d" % t, 0, NT), scale=0.5)
         quant(V(tab, OWN, OWN + 128), V("tl", NTL, NTL + 512))
-        for x in (tab, tab + "s"):
-            send(partner, V(x, PAR, PAR + NT), V(x, OWN, OWN + NT), "ac%d" % b, "lc")
-        send(partner, land, lx, "al%d" % b, "ll")
-        scatter(src, lx, V("jown", 0, NT))
-        arrive([land], "al%d" % b, partner)
-        arrive([V(tab, PAR, PAR + NT), V(tab + "s", PAR, PAR + NT)], "ac%d" % b, partner, 2)
-        copy(V("c1", 0, NT), src, OPT["c1q"], off=look)
-        ts(V("both", 0, NT), src, OWN - 0.5, A.is_ge, float(MRG - PAR), A.mult, off=look)
+        send(partner, V(tab, PAR, PAR + NT), V(tab, OWN, OWN + NT), "ac%d" % b, "lc")
+        ts(V("pre", 98, 192, 4), V("krow", 0, 24), h1, A.is_equal, float(PAR), A.mult)
+        copy(V("pre", 96, 192, 4), V("pre", 98, 192, 4), scale=V("pg", 0, 1))
+        copy(V("pre", 97, 192, 4), V("pre", 98, 192, 4), scale=V("pg", 1, 2))
+        copy(V("pre", 0, 96, 4), V("pre", 98, 192, 4), scale=(MRG - PAR) / float(PAR))
+        ts(V("tao", 0, 512, 4), V("cmod", 0, 128), V("xtile", 4 * UC, 4 * UC + 1), A.is_equal)
+        for t in (1, 2):
+            copy(V("tao", t, 512, 4), V("tao", 0, 512, 4), scale=1.0 if t == 1 else OWN / float(PAR))
+        tt(V("pre", 192, 216), V("xtile", 4 * MK, 4 * UC), V("cdig", 0, 24), A.subtract)
+        quant(V("ao", 0, 128), V("tao", 0, 512))
+        reduce(V("flag", 0, 1), V("ps7", 0, ONE + 1), A.min, absv=True)
+        copy(V("btile", 0, 216, 1, 0, NT), V("pre", 0, 216, 1, 0, NT), scale=V("flag", 0, 1, 1, 0, NT))
+        quant(V(xb, BO, BO + 128), V("btile", 0, 512))
+        send(partner, V(xb, BP, BP + 24), V(xb, BS, BS + 24), "al%d" % b, "ll")
+        mm(6, V("r16", 0, 128), V(xb, BO, BO + 128))
+        ts(V("lx", 0, 6), V("ps6", LX, LX + 6), 192.0, A.add)
+        scatter(V("src", 0, 480), V("lx", 0, 6), V("jown", 0, NT))
+        mm(4, V("ao", 0, 128), V(xb, BO, BO + 128))
+        mm(5, V("ao", 0, 128), V(xb, BO, BO + 128), True, False)
+        tt(V("sl", 0, 24), V("ps4", BS - BO, BS - BO + 24), cl, A.max)
+        for t in range(4):
+            mm(t, E(t), V(tab, OWN, OWN + 128))
+            copy(V("junk", NU + NT * t, NU + NT * t + NT), V("ps%d" % t, 0, NT))
+        arrive([V(xl, EX, EX + 2), V(xl + "s", EX, EX + 8)], "au%d" % b, partner)
+        arrive([look], "ae%d" % b, partner)
+        mm(7, E(0), V(xl, 2, 130))
+        ts(V("tap", 0, 512, 4), V("cmod", 0, 128), 0.5, A.mult, V("ps7", 126, 127), A.is_equal)
+        for t in (1, 2):
+            copy(V("tap", t, 512, 4), V("tap", 0, 512, 4))
+        quant(V("ap", 0, 128), V("tap", 0, 512))
+        if b + 1 == NR:
+            ypart(7, tab, OWN, OWN + 128)
+        copy(V("c1", 0, NT), V("src", 0, 480), off=look)
         scan(V("c2", 0, NT), V("mw", 0, NT), V("c1", 0, NT), 0.0, A.mult, A.add)
         ts(V("clist", 0, 6), V("c2", 15, NT, 16), V("esc", 0, 1), A.mult, -0.34, A.add)
-        tt(V("val", 0, NT), V("both", 0, NT), V("jpar", 0, NT), A.add)
+        arrive([V(tab, PAR, PAR + NT), V(tab + "s", PAR, PAR + NT)], "ac%d" % b, partner, 2)
         for t in range(4):
-            mm(4 + t, E("e1", t), V(tab, OWN, OWN + 128))
-            copy(V("junk", NU + NT * t, NU + NT * t + NT), V("ps%d" % (4 + t), 0, NT), OPT["dq"][t])
-        for t in range(4):
-            copy(V("dg", NT * t, NT * t + NT), V("junk", NT * t, NU + NT * t + NT), OPT["gq"][t], off=V("clist", 0, 6))
-            mm(t, E("e1", t), V(tab, PAR - 32, PAR + NT))
-        scatter(src, land, V("val", 0, NT))
-        for u, v in _cut(OPT["bs"][b]):
-            scan(V("srcs", u, v), V("mw", 0, v - u), V(src[0], u, v), 0.0, A.mult, A.add)
-            ts(V("blist", u // 16, v // 16), V("srcs", u + 15, v, 16), V("esc", 0, 1), A.mult, -0.34, A.add)
-        for t in range(4):
+            copy(V("dg", NT * t, NT * t + NT), V("junk", NU + NT * t, NU + NT * t + NT), off=V("clist", 0, 6))
+            mm(t, E(t), V(tab, PAR - 32, PAR + NT))
             tt(V("tl", MT + t, MT + 4 * NT, 4), V("dg", NT * t, NT * t + NT), V("ps%d" % t, 32, 128), A.add)
         quant(V(tab, MRG, MRG + 128), V("tl", MT, MT + 512))
+        if b + 1 == NR:
+            ypart(7, tab, PAR, PAR + NT, 32)
+            ypart(6, tab, MRG, MRG + NT)
+        arrive([V(xb, BP, BP + 24), V(xb + "s", BP, BP + 24)], "al%d" % b, partner, 2)
+        mm(5, V("ap", 0, 128), V(xb, BP, BP + 128), False, True)
+        tt(V("bl", 0, 24), V("ps5", 0, 24), V("sl", 0, 24), A.max)
+        vcopy(V("blist", 0, 24), V("bl", 0, 24))
         for k, (u, v) in enumerate(_cut(OPT["tab" if b + 1 < NR else "fin"])):
             pick(V(nxt, u, v), V(tab, 0, WIN), V("blist", u // 16, v // 16))
             if b + 1 < NR:
                 score(b + 1, k, u, v)
                 run_max(k, u, v)
 
-    for k, (u, v) in enumerate(_cut(OPT["fin"])):
-        mm(4 + k, V("wq", 0, 128), V("fin", u, v))
-        copy(V("ysb", u, v), V("ps%d" % (4 + k), 0, v - u), OPT["yq"][k])
+    for k, (u, v) in enumerate(_cut(OPT["yp"])):
+        copy(V("ysb", u, v), V("yw", 0, MRG + NT), off=V("blist", u // 16, v // 16))
+    for k, (u, v) in enumerate(_cut(OPT["ysp"])):
         store(OPT["ysq"][k], T.y[:, u:v], V("ysb", u, v), T.ysb[:, u:v])
-    for k, (u, v) in enumerate(_cut(OPT["fin"])):
+    for k, (u, v) in enumerate(_cut(OPT["ocp"])):
         store(OPT["ocq"][k], T.oc[:, 4 * u:4 * v], V("fin", u, v), T.fin[:, u:v].bitcast(dt.uint8))
     for k in range(4):
         store(OPT["oscq"][k], T.osc[4 * k:4 * k + 4, 0:NU], V("fins", 0, NU), T.fins[32 * k:32 * k + 4, 0:NU])

@@ -4,31 +4,33 @@ from concourse.mybir import dt, AluOpType, AxisListType, ActivationFunctionType
 
 A = AluOpType
 AF = ActivationFunctionType
-NU, NT, NR = 384, 96, 2
-OWN, PAR, MRG, WIN = 384, 512, 608, 736
-XQ = 96
-MK, UC, XL, ONE, EX = 96, 102, 103, 103, 128
-BP, BO, BS = 8, 32, 56
-LX = 48
+NU, NT, NR, NM = 384, 96, 2, 24
+PAR, OWN, MRG, WIN = 384, 512, 1024, 1152
+XQ, PK = 0, 128
+UC, MK, M4, XL = 24, 26, 32, 56
 OFF = 8192.0
 LO = 192.0 + 7 * OFF
-BIG = 16384.0
-MT, NTL, X0, ZZ, X1, KB = 0, 384, 768, 1152, 1280, 1664
+L4 = 4 * (192.0 + 31 * OFF)
+RATIO, TOP, NONE = 1.54, 2.0 ** 29.7, 2.0 ** -62
+STEP = 2 * math.log(RATIO)
+MID = 2 * math.log(TOP) + 0.25
+EDGE = MID - 96.3 * STEP
+MT, XT, X0, KB, NTL, X1, WT = 0, 384, 608, 992, 2528, 2912, 3296
 F4, F32, BF, U16, I32, U8 = "float8_e4m3fn_x4", "float32", "bfloat16", "uint16", "int32", "uint8"
-OPT = {"load": (224, 160), "tab": (192, 192), "fin": (192, 192), "yp": (192, 192), "ysp": (384,), "ocp": (384,),
-       "lq": "ffff", "oscq": "ffff", "ysq": "fff", "ocq": "fff", "rq": "f"}
+OPT = {"load": (224, 160), "tab": (192, 192), "fin": (192, 192), "ysp": (384,), "ocp": (192, 192),
+       "lq": "fff", "oscq": "ffff", "ysq": "fff", "ocq": "fff", "rq": "y", "dkp": ((224, 160), (192, 192)), "up": (384,), "pf": (0, 0)}
 SQ = [int(x) for x in """
-13 18 19 20 21 22 23 25 26 27 28 29 30 33 34 35 36 37 38 41 42 43 44 46 47 48 49 50 51 52 53 54 85 96 98 100 102 109 110 111 113 114 118 129 131 135
-140 143 147 150 156 165 169 179 182 192 196 200 205 206 209 210 225 229 231 236 240 241 245 248 251 259 261 267 271 275 276
+0 22 27 28 30 32 35 36 37 39 50 52 54 64 66 68 70 72 76 78 82 96 98 100 102 109 110 114 119 140 142 147 151 155 157 161 163 165 169 173 177 194
+195 199 204 218 227 229 234 236 238 240 242 248 249
 """.split()]
 ORDER = [int(x) for x in """
-6 1 39 0 2 40 3 5 14 7 22 15 13 36 11 16 24 49 12 30 32 25 9 31 17 18 28 20 72 69 59 60 73 75 76 21 27 29 23 19 4 35 74 33 57 77 80 67 8 34 38 37 82
-46 83 66 84 58 86 85 50 108 81 78 26 44 87 79 52 61 88 90 68 51 93 94 62 47 53 43 63 111 110 48 109 89 91 92 137 136 115 117 95 64 96 118 112 65 97 41
-54 119 99 101 98 120 10 56 103 100 122 104 102 123 105 138 106 132 124 55 130 139 114 107 121 113 116 45 42 128 160 143 134 140 129 146 141 126 144
-133 145 125 135 148 131 142 147 127 151 154 161 153 157 149 150 156 155 152 162 158 163 159 70 165 164 166 175 169 168 167 170 171 71 177 178 176 180
-181 179 204 173 184 183 211 172 208 207 186 189 182 209 206 190 187 213 191 205 192 214 185 215 174 210 193 199 200 212 188 195 216 197 218 196 194
-198 232 234 219 201 222 226 221 230 233 228 220 241 217 262 235 236 229 202 203 227 231 237 223 242 238 224 239 243 263 225 244 251 248 254 264 252
-255 253 249 246 245 256 250 247 265 257 266 240 258 268 259 273 260 261 270 271 269 267 272 276 277 275 274 278
+5 11 1 0 13 2 14 40 6 41 7 12 35 15 57 16 63 46 58 8 23 3 9 37 36 42 17 60 32 43 49 4 67 61 59 64 65 71 10 18 31 24 50 62 33 25 80 51 29 68 69
+66 20 79 26 81 52 34 82 19 21 75 73 83 70 84 45 53 55 30 54 86 72 56 103 77 27 76 88 74 104 78 89 105 90 47 95 97 91 87 106 22 38 107 115 101
+102 92 96 44 28 93 39 114 123 113 120 116 121 110 117 108 99 100 94 122 125 118 98 119 124 109 111 136 112 127 126 128 132 133 129 139 137 134
+141 138 142 130 135 140 143 144 131 145 147 146 151 148 150 156 152 154 149 48 157 155 158 160 153 171 172 159 170 174 164 173 175 162 161 165
+163 179 188 166 168 167 189 169 182 178 190 191 183 181 184 200 192 195 205 185 85 201 206 202 199 198 204 207 176 193 203 180 208 186 187 194
+196 197 217 209 210 212 219 221 211 218 220 214 223 222 213 215 177 230 228 231 229 226 227 224 225 216 232 233 234 235 238 237 241 236 245 239
+242 243 246 240 250 249 247 248 244 251
 """.split()]
 
 
@@ -43,35 +45,31 @@ def _decl():
         add(n + "s", w, U8)
     for b in range(NR):
         pair("tab%d" % b, WIN)
-        pair("xq%d" % b, XQ + 128)
-        pair("xl%d" % b, EX + 32)
-        pair("xb%d" % b, BO + 128)
+        pair("xq%d" % b, PK + NT)
+        pair("tbu%d" % b, NU)
+        pair("xl%d" % b, M4 + 128)
         add("win%d" % b, 1, F32)
-        add("lown%d" % b, 8, U16)
         add("look%d" % b, 8, U16)
-    for n in ("e1", "e3"):
-        pair(n, 512)
-    for n in ("r16", "r1", "negw", "ao", "ap"):
+        add("dx%d" % b, 4 * NT, BF)
+    pair("e1", 512)
+    for n in ("r16", "r4", "ao", "ap", "wq"):
         pair(n, 128)
-        add("t" + n, 512, BF)
-    pair("wq", 128)
     pair("fin", NU)
     for n in range(8):
         add("ps%d" % n, 512, F32, "psum")
-    for n, w, t in (("tl", KB + 4 * NU, BF), ("te", 520, BF), ("wt", 512, BF), ("xtile", 512, BF), ("btile", 512, BF), ("dd", 128, BF),
-                    ("mask", XL, BF), ("junk", 2 * NU, BF), ("dg", NU, BF), ("src", 480, BF), ("jown", NT, BF), ("mc", NT, BF),
-                    ("mw", NT, BF), ("cdig", 24, BF), ("mb", XL, BF), ("cmod", 128, BF), ("krow", 24, BF), ("pre", 216, BF),
-                    ("ip", 1, I32), ("pi", 2, I32), ("lx", 6, U16), ("clist", 6, U16), ("blist", 24, U16)):
+    for n, w, t in (("tl", WT + 512, BF), ("te", 520, BF), ("tr", 520, BF), ("dd", 128, BF), ("chalf", 128, BF), ("wh", 1, BF),
+                    ("dk", 4 * NU, BF), ("mask", 32, BF), ("junk", NU, BF), ("mb", 32, BF), ("cmod", 128, BF),
+                    ("cm4", 128, BF), ("krow", 24, BF), ("ip", 2, I32), ("pi", 4, I32), ("ulist", 24, U16), ("blist", 24, U16), ("l4", 24, U16)):
         add(n, w, t)
-    for n, w in (("pf", 2), ("pg", 2), ("pmo", 1), ("esc", 1), ("c1", NT), ("c2", NT), ("p", NU), ("zz", 25), ("h1", 1), ("flag", 1),
-                 ("cl", 24), ("sl", 24), ("bl", 24), ("ysb", NU), ("yw", MRG + NT)):
+    for n, w in (("pf", 4), ("pg", 2), ("p", NU), ("zz", 25), ("h1", 1), ("lc", 2), ("wa", NT), ("wb", 1), ("wt", 1),
+                 ("cl", 24), ("sl", 24), ("lo", 24), ("lp", 24), ("lf", 24), ("la", 24), ("yo", 24), ("ysb", NU), ("yw", MRG + NT)):
         add(n, w, F32)
     return s
 
 
 SCRATCH = _decl()
 NCOMP, NHW = 100, 24
-REMOTE = ["%s%d" % (n, b) for b in range(NR) for n in ("ae", "al", "ac", "au")] + ["le", "ll", "lc"]
+REMOTE = ["%s%d" % (n, b) for b in range(NR) for n in ("ae", "au", "ac")] + ["le", "lc"]
 SEMAPHORES = ["c%d" % i for i in range(NCOMP)] + ["h%d" % i for i in range(NHW)] + REMOTE
 
 
@@ -89,7 +87,7 @@ def _record(rec, queue, kind, call, reads, writes, extra=(), tag=None):
         for v in vs:
             for (u, uw, j, uq) in acc.get(v[0], []):
                 if v[0][:2] == "ps":
-                    if uq == "tensor" and queue == "tensor":
+                    if uq == queue and (queue == "tensor" or not (w or uw)):
                         soft.add(j)
                     else:
                         deps.add(j)
@@ -164,7 +162,7 @@ def _cut(sizes):
 def _calls(core, T, topo):
     rank = T.rank_of(core)
     rec = {"ops": [], "acc": {}}
-    local = {"le": 0, "ll": 0, "lc": 0}
+    local = {"le": 0, "lc": 0}
     eng = {"s": "scalar", "y": "sync"}
 
     def ap(v):
@@ -216,18 +214,11 @@ def _calls(core, T, topo):
             return q.tensor_scalar(ap(out), ap(in0), val(s1), val(s2), op0, op1)
         _record(rec, "vector", "comp", call, views(in0, s1, s2), [out])
 
-    def tt(out, in0, in1, op):
-        _record(rec, "vector", "comp", lambda q: q.tensor_tensor(ap(out), ap(in0), ap(in1), op), [in0, in1], [out])
+    def tt(out, in0, in1, op, off=None):
+        _record(rec, "vector", "comp", lambda q: q.tensor_tensor(ap(out), by(in0, off), ap(in1), op), views(in0, off, in1), [out])
 
-    def scatter(win, off, in_):
-        _record(rec, "vector", "comp", lambda q: q.tensor_copy(ap(win).indirect(ap(off)), ap(in_)), [win, off, in_], [win])
-
-    def reduce(out, in_, op, absv=False):
-        def call(q):
-            if absv:
-                return q.tensor_reduce(ap(out), ap(in_), AxisListType.X, op, apply_absolute_value=True)
-            return q.tensor_reduce(ap(out), ap(in_), AxisListType.X, op)
-        _record(rec, "vector", "comp", call, [in_], [out])
+    def reduce(out, in_, op):
+        _record(rec, "vector", "comp", lambda q: q.tensor_reduce(ap(out), ap(in_), AxisListType.X, op), [in_], [out])
 
     def scan(out, d0, d1, init, op0, op1):
         _record(rec, "vector", "comp", lambda q: q.tensor_tensor_scan(ap(out), ap(d0), ap(d1), val(init), op0, op1),
@@ -256,11 +247,10 @@ def _calls(core, T, topo):
             return q.iota(ap(out), pattern, base, cm)
         _record(rec, "gpsimd", "comp", call, [], [out])
 
-    def fill(name, a, b, c, st=1):
-        n = len(range(a, b, st))
-        if n > 128:
-            return memset(V(name, a, b, st), c)
-        copy(V(name, a, b, st), V("dd", 0, n), scale=0.0, bias=c if c else None)
+    def fill(name, a, b, c):
+        if b - a > 128:
+            return memset(V(name, a, b), c)
+        copy(V(name, a, b), V("dd", 0, b - a), scale=0.0, bias=c if c else None)
 
     def dq(queue):
         return eng[queue] if queue in eng else "scalar" if len(rec["ops"]) in SQ else "sync"
@@ -300,72 +290,59 @@ def _calls(core, T, topo):
     def arrive(writes, sem, src, calls=1):
         _record(rec, "network", "arr", (sem, calls * len(topo.engines(src, core))), [], writes)
 
-    pm, pd = V("pf", 0, 1), V("pf", 1, 2)
+    pm, pd, p4, pq, wt = V("pf", 0, 1), V("pf", 1, 2), V("pf", 2, 3), V("pf", 3, 4), V("wt", 0, 1)
     first = [load(OPT["lq"][0], V("tl", X0, X0 + 384), T.x[:, 0:384])]
     for k, (u, v) in enumerate(_cut(OPT["load"])):
         first.append(load(OPT["lq"][k + 1], V("tl", KB + 4 * u, KB + 4 * v), T.kb[:, 4 * u:4 * v]))
     load(OPT["rq"], V("tl", X1, X1 + 384), T.x[:, 384:768], first)
-    load(OPT["rq"], V("wt", 0, 512), T.w[:, 0:512], first)
+    load(OPT["rq"], V("tl", WT, WT + 512), T.w[:, 0:512], first)
 
     iota(V("dd", 0, 128), [[1, 128]], 0, -1)
     iota(V("ip", 0, 1), [[0, 1]], 0, 1)
+    iota(V("ip", 1, 2), [[0, 1]], 0, 4)
     iota(V("cmod", 0, 128), [[0, 8], [1, 16]], 0, 0)
     iota(V("krow", 0, 24), [[16, 24]], -192, 0)
-    iota(V("jown", 0, NT), [[1, NT]], 0, 0)
-    fill("src", 0, 480, 0.0)
-    memset(V("te", 0, 520), 0.0)
+    iota(V("cm4", 0, 128), [[0, 8], [4, 4], [0, 4]], 0, 0)
+    memset(V("lc", 0, 1), math.exp(MID))
+    act(V("lc", 1, 2), V("lc", 0, 1), AF.Ln)
+    fill("te", 0, 520, 0.0)
     ts(V("te", 4, 516, 4), V("dd", 0, 128), 0.0, A.is_equal, 0.5, A.mult)
-    fill("tl", ZZ, ZZ + 128, 0.0)
-    ts(V("pi", 0, 1), V("ip", 0, 1), 15, A.bitwise_and)
-    ts(V("pi", 1, 2), V("ip", 0, 1), 4, A.logical_shift_right)
-    vcopy(V("pf", 0, 2), V("pi", 0, 2))
-    ts(V("tr16", 0, 512, 4), V("cmod", 0, 128), pm, A.is_equal)
-    for t in range(1, 4):
-        copy(V("tr16", t, 512, 4), V("tr16", 0, 512, 4), scale=16.0 if t == 3 else 1.0)
-    for t in range(3):
-        copy(V("tr1", t, 512, 4), V("dd", 0, 128), scale=0.0, bias=1.0)
-    ts(V("tr1", 3, 512, 4), V("dd", 0, 128), 0.0, A.is_le, 512.0, A.mult)
-    for t in range(4):
-        copy(V("tnegw", t, 4 * MK, 4), V("dd", 0, MK), scale=0.0, bias=-1.0 if t < 3 else None)
-    fill("tnegw", 4 * MK, 512, 0.0)
-    copy(V("mask", 0, MK), V("te", 4, 4 + 4 * MK, 4), scale=2.0)
-    ts(V("mask", MK, UC), V("cmod", 0, 6), pd, A.is_equal)
-    ts(V("mask", UC, XL), pd, 5.5, A.is_le)
-    copy(V("mb", 0, XL), V("mask", 0, XL), scale=OFF, bias=-OFF - 192.0)
+    ts(V("pi", 0, 4, 2), V("ip", 0, 2), 15, A.bitwise_and)
+    ts(V("pi", 1, 4, 2), V("ip", 0, 2), 4, A.logical_shift_right)
+    vcopy(V("pf", 0, 4), V("pi", 0, 4))
+    ts(V("tr", 2, 512, 4), V("cmod", 0, 128), pm, A.is_equal)
+    copy(V("tr", 3, 512, 4), V("tr", 2, 512, 4))
+    ts(V("tr", 0, 512, 4), V("cm4", 0, 128), p4, A.is_equal, 4.0, A.mult)
+    copy(V("tr", 1, 512, 4), V("tr", 0, 512, 4))
+    fill("tr", 512, 514, 0.0)
+    iota(V("wa", 0, NT), [[0, NT]], 1, 0)
+    _record(rec, "gpsimd", "comp", lambda q: q.affine_select(T.wa[:, 0:NT], T.wa[:, 0:NT], [[1, NT]], A.is_gt, 1.0 / RATIO, 0, -1),
+            [V("wa", 0, NT)], [V("wa", 0, NT)])
+    reduce(V("wb", 0, 1), V("wa", 0, NT), A.mult)
+    copy(wt, V("wb", 0, 1), scale=TOP * RATIO)
+    copy(V("pg", 1, 2), p4, scale=0.25, bias=L4)
+    copy(V("chalf", 0, 128), V("cmod", 0, 128), scale=0.5)
+    ts(V("mask", 0, 2), V("pf", 1, 3), 5.5, A.is_le)
+    copy(V("wh", 0, 1), V("wb", 0, 1), scale=TOP * RATIO)
+    ts(V("mask", MK - UC, M4 - UC), V("cmod", 0, 6), pd, A.is_equal)
+    copy(V("pg", 0, 1), pq, scale=16.0, bias=-192.0)
+    ts(V("mask", M4 - UC, XL - UC), V("krow", 0, 24), V("pg", 0, 1), A.is_equal)
+    copy(V("mb", 0, XL - UC), V("mask", 0, XL - UC), scale=OFF, bias=-OFF - 192.0)
     fill("zz", 24, 25, -192.0)
-    fill("xtile", 4 * NT, 512, 0.0)
-    fill("xtile", 2, 4 * NT, 0.0, 4)
-    copy(V("xtile", 3, 4 * NT, 4), V("mask", 0, NT))
-    copy(V("xtile", 4 * ONE + 2, 4 * ONE + 3), V("mask", 0, 1))
-    fill("btile", 0, 512, 0.0)
-    fill("pre", 0, 192, 0.0)
-    for n in ("tao", "tap"):
-        fill(n, 3, 512, 0.0, 4)
-    copy(V("pg", 0, 1), pm, scale=1.0 / PAR)
-    copy(V("pg", 1, 2), pd, scale=16.0 / PAR)
+    fill("tl", XT, XT + 128, 0.0)
+    fill("tl", XT + 128, XT + 4 * XL, 0.0)
     ts(V("cl", 0, 24), V("krow", 0, 24), pm, A.add, 192.0, A.add)
-    copy(V("btile", 4 * LX, 4 * LX + 24, 4, 96, 112), V("dd", 0, 6, 1, 96, 112), scale=0.0, bias=V("pf", 0, 1, 1, 96, 112))
-    copy(V("btile", 4 * LX + 1, 4 * LX + 24, 4, 96, 112), V("dd", 0, 6, 1, 96, 112), scale=0.0, bias=192.0)
-    copy(V("btile", 4 * LX + 3, 4 * LX + 24, 4, 96, 112), V("cmod", 0, 6, 1, 96, 112))
-    copy(V("pmo", 0, 1), pm, bias=OFF)
-    for t, s in enumerate((V("pmo", 0, 1), 0.0, 192.0, pd)):
-        copy(V("cdig", t, 24, 4), V("mask", MK, UC), scale=s, bias=None if t else -OFF)
-    copy(V("mc", 0, NT), V("tr16", 60, 60 + 4 * NT, 4), scale=BIG, bias=1.0)
-    tt(V("mw", 0, NT), V("mc", 0, NT), V("tr16", 0, 4 * NT, 4), A.subtract)
-    ts(V("esc", 0, 1), pm, 15.0, A.is_equal, 1.0 / BIG, A.max)
-    for n in ("e1", "e3"):
-        if n == "e3":
-            ts(V("te", 4, 516, 4), V("dd", 0, 128), 0.0, A.is_equal, 1.5, A.mult)
-        for t in range(4):
-            quant(V(n, 128 * t, 128 * t + 128), V("te", 4 - t, 516 - t))
-    for n in ("r16", "r1", "negw"):
-        quant(V(n, 0, 128), V("t" + n, 0, 512))
+    copy(V("cl", 0, 24), V("cl", 0, 24), scale=STEP)
+    for t in range(4):
+        quant(V("e1", 128 * t, 128 * t + 128), V("te", 4 - t, 516 - t))
+    quant(V("r16", 0, 128), V("tr", 2, 514))
+    quant(V("r4", 0, 128), V("tr", 0, 512))
     quant(V("xq0", XQ, XQ + 128), V("tl", X0, X0 + 512))
     quant(V("xq1", XQ, XQ + 128), V("tl", X1, X1 + 512))
-    quant(V("wq", 0, 128), V("wt", 0, 512))
+    quant(V("wq", 0, 128), V("tl", WT, WT + 512))
 
-    def E(t, n="e1"):
-        return V(n, 128 * t, 128 * t + 128)
+    def E(t):
+        return V("e1", 128 * t, 128 * t + 128)
 
     def score(b, k, u, v):
         mm(4 + k, V("xq%d" % b, XQ, XQ + 128), V("tab%d" % b, u, v))
@@ -377,94 +354,101 @@ def _calls(core, T, topo):
         mm(ps, V("wq", 0, 128), V(tab, u - pad, max(v, u - pad + 128)))
         copy(V("yw", u, v), V("ps%d" % ps, pad, pad + v - u))
 
+    def tokens(b, banks):
+        for t in range(4):
+            mm(banks[t], E(t), V("xq%d" % b, XQ, XQ + 128))
+            copy(V("dx%d" % b, t, 4 * NT, 4), V("ps%d" % banks[t], 0, NT), scale=0.5)
+
+    tokens(0, (6, 7, 6, 7))
     for k, (u, v) in enumerate(_cut(OPT["load"])):
         quant(V("tab0", u, v), V("tl", KB + 4 * u, KB + 4 * v))
         score(0, k, u, v)
         run_max(k, u, v)
 
     for b in range(NR):
-        tab, xq, xl, xb = ["%s%d" % (n, b) for n in ("tab", "xq", "xl", "xb")]
+        tab, xq, xl, tbu = ["%s%d" % (n, b) for n in ("tab", "xq", "xl", "tbu")]
         nxt = "tab%d" % (b + 1) if b + 1 < NR else "fin"
-        win, lown, look, cl = V("win%d" % b, 0, 1), V("lown%d" % b, 0, 6), V("look%d" % b, 0, 6), V("cl", 0, 24)
+        win, look, cl = V("win%d" % b, 0, 1), V("look%d" % b, 0, 6), V("cl", 0, 24)
+        ao, lt, pl, pe = V("ao", 0, 128), V(xl, M4, M4 + 128), V(xl, 0, 128), V(xl, UC, UC + 128)
+        lo, lp, lf, la, yo, sl = [V(n, 0, NM) for n in ("lo", "lp", "lf", "la", "yo", "sl")]
         partner = T.cores[rank ^ (1 << b)]
-        for t in range(4):
-            mm(t, E(t), V(xq, XQ, XQ + 128), True, False)
+        for (u, v) in _cut(OPT["dkp"][b]):
+            for t in range(4):
+                mm(t, E(t), V(tab, u, v))
+                copy(V("dk", 4 * u + t, 4 * v, 4), V("ps%d" % t, 0, v - u), scale=1.5)
         last, h1 = V("p", NU - 1, NU), V("h1", 0, 1)
         act(V("junk", 0, NU), V("p", 0, NU), AF.Sign, scale=-1.0, bias=last, accum=win)
         ts(V("zz", 0, 24), V("p", 15, NU, 16), last, A.is_lt, 16.0, A.mult)
         reduce(h1, V("zz", 0, 25), A.add)
-        copy(V("xtile", 1, 4 * XL, 4), V("mask", 0, XL), scale=h1)
-        ts(V("xtile", 0, 4 * XL, 4), V("mb", 0, XL), win, A.add, h1, A.subtract)
+        copy(V("tl", XT + 4 * UC + 1, XT + 4 * XL, 4), V("mask", 0, XL - UC), scale=h1)
+        ts(V("tl", XT, XT + 4 * NM, 4), V("krow", 0, NM), h1, A.is_equal, wt, A.mult)
+        ts(V("tl", XT + 4 * UC, XT + 4 * XL, 4), V("mb", 0, XL - UC), win, A.add, h1, A.subtract)
         if b + 1 == NR:
             ypart(4, tab, 0, NU)
         store(OPT["rq"], T.ch[b:b + 1, 0:NT], win, T[win[0]][0:NT, 0:1])
-        quant(V(xl, 0, 128), V("xtile", 0, 512))
-        send2(partner, (V(xl, EX, EX + 2), V(xl + "s", EX, EX + 8)), (V(xl, UC, UC + 2), V(xl + "s", UC, UC + 8)), "au%d" % b, "le")
-        mm(6, V("r16", 0, 128), V(xl, 0, 128))
-        ts(lown, V("ps6", MK, UC), LO, A.add)
-        send1(partner, look, lown, "ae%d" % b, "le")
-        mm(7, V("r1", 0, 128), V(xl, 0, 128), True, False)
-        mm(7, V(xl, 0, 128), V("negw", 0, 128), False, True)
-        pick(V(xq, 0, NT), V(tab, 0, NU), lown)
-        for t in range(4):
-            mm(t, E(t, "e3"), V(xq, 0, 128), False, True)
-            copy(V("tl", NTL + t, NTL + 4 * NT, 4), V("ps%d" % t, 0, NT), scale=0.5)
+        quant(lt, V("tl", XT, XT + 512))
+        send1(partner, V(xl, 0, UC), V(xl, M4, M4 + UC), "ae%d" % b, "le")
+        send2(partner, (V(xl, UC, M4), V(xl + "s", 0, M4)), (V(xl, M4 + UC, 2 * M4), V(xl + "s", M4, 2 * M4)), "au%d" % b, "le")
+        mm(6, V("r4", 0, 128), lt)
+        ts(V("l4", 0, 24), V("ps6", M4, XL), V("pg", 1, 2), A.add)
+        tt(V("tl", NTL, NTL + 4 * NT), V("dk", 0, 4 * NU), V("dx%d" % b, 0, 4 * NT), A.add, V("l4", 0, 24))
         quant(V(tab, OWN, OWN + 128), V("tl", NTL, NTL + 512))
         send(partner, V(tab, PAR, PAR + NT), V(tab, OWN, OWN + NT), "ac%d" % b, "lc")
-        ts(V("pre", 98, 192, 4), V("krow", 0, 24), h1, A.is_equal, float(PAR), A.mult)
-        copy(V("pre", 96, 192, 4), V("pre", 98, 192, 4), scale=V("pg", 0, 1))
-        copy(V("pre", 97, 192, 4), V("pre", 98, 192, 4), scale=V("pg", 1, 2))
-        copy(V("pre", 0, 96, 4), V("pre", 98, 192, 4), scale=(MRG - PAR) / float(PAR))
-        ts(V("tao", 0, 512, 4), V("cmod", 0, 128), V("xtile", 4 * UC, 4 * UC + 1), A.is_equal)
-        for t in (1, 2):
-            copy(V("tao", t, 512, 4), V("tao", 0, 512, 4), scale=1.0 if t == 1 else OWN / float(PAR))
-        tt(V("pre", 192, 216), V("xtile", 4 * MK, 4 * UC), V("cdig", 0, 24), A.subtract)
-        quant(V("ao", 0, 128), V("tao", 0, 512))
-        reduce(V("flag", 0, 1), V("ps7", 0, ONE + 1), A.min, absv=True)
-        copy(V("btile", 0, 216, 1, 0, NT), V("pre", 0, 216, 1, 0, NT), scale=V("flag", 0, 1, 1, 0, NT))
-        quant(V(xb, BO, BO + 128), V("btile", 0, 512))
-        send(partner, V(xb, BP, BP + 24), V(xb, BS, BS + 24), "al%d" % b, "ll")
-        mm(6, V("r16", 0, 128), V(xb, BO, BO + 128))
-        ts(V("lx", 0, 6), V("ps6", LX, LX + 6), 192.0, A.add)
-        scatter(V("src", 0, 480), V("lx", 0, 6), V("jown", 0, NT))
-        mm(4, V("ao", 0, 128), V(xb, BO, BO + 128))
-        mm(5, V("ao", 0, 128), V(xb, BO, BO + 128), True, False)
-        tt(V("sl", 0, 24), V("ps4", BS - BO, BS - BO + 24), cl, A.max)
-        for t in range(4):
-            mm(t, E(t), V(tab, OWN, OWN + 128))
-            copy(V("junk", NU + NT * t, NU + NT * t + NT), V("ps%d" % t, 0, NT))
-        arrive([V(xl, EX, EX + 2), V(xl + "s", EX, EX + 8)], "au%d" % b, partner)
-        arrive([look], "ae%d" % b, partner)
-        mm(7, E(0), V(xl, 2, 130))
-        ts(V("tap", 0, 512, 4), V("cmod", 0, 128), 0.5, A.mult, V("ps7", 126, 127), A.is_equal)
-        for t in (1, 2):
-            copy(V("tap", t, 512, 4), V("tap", 0, 512, 4))
-        quant(V("ap", 0, 128), V("tap", 0, 512))
+        if b + 1 < NR:
+            tokens(b + 1, range(4))
+        ts(V("te", 0, 512, 4), V("cmod", 0, 128), V("tl", XT + 4 * UC, XT + 4 * UC + 1), A.is_equal, V("wh", 0, 1), A.mult)
+        quant(ao, V("te", 0, 512))
+        mm(7, ao, lt)
+        act(lo, V("ps7", 0, NM), AF.Ln, bias=NONE)
+        ts(V("ulist", 0, 24), lo, V("lc", 1, 2), A.subtract, -1.0 / STEP, A.mult)
+        ts(lf, lo, EDGE, A.is_gt, (MRG - PAR) * STEP, A.mult)
+        copy(la, lf, bias=MID + PAR * STEP)
+        copy(yo, lo, scale=-1.0, bias=MID + OWN * STEP)
+        tt(yo, yo, lf, A.min)
+        tt(sl, yo, cl, A.max)
+        for (u, v) in _cut(OPT["up"]):
+            pick(V(tbu, u, v), V(tab, OWN, OWN + 128), V("ulist", u // 16, v // 16))
+        arrive([V(xl, UC, M4), V(xl + "s", 0, M4)], "au%d" % b, partner)
+        mm(6, V("r16", 0, 128), pe)
+        ts(look, V("ps6", MK - UC, M4 - UC), LO, A.add)
+        pick(V(xq, PK, PK + NT), V(tbu, 0, NU), look)
+        mm(7, E(0), pe)
+        ts(V("te", 2, 514, 4), V("chalf", 0, 128), V("ps7", 0, 1), A.is_equal, wt, A.mult)
+        quant(V("ap", 0, 128), V("te", 2, 514))
+        arrive([V(xl, 0, UC)], "ae%d" % b, partner)
+        mm(5, V("ap", 0, 128), pl)
+        mm(7, V("ap", 0, 128), pl)
+        act(lp, V("ps5", 0, NM), AF.Ln, bias=NONE)
+        ts(lf, V("ps7", 0, NM), 0.0, A.is_gt, WIN * STEP, A.mult)
+        tt(lf, lf, sl, A.add)
+        tt(la, la, lp, A.subtract)
+        tt(la, la, lf, A.min)
+        ts(V("blist", 0, 24), la, 1.0 / STEP, A.mult)
         if b + 1 == NR:
-            ypart(7, tab, OWN, OWN + 128)
-        copy(V("c1", 0, NT), V("src", 0, 480), off=look)
-        scan(V("c2", 0, NT), V("mw", 0, NT), V("c1", 0, NT), 0.0, A.mult, A.add)
-        ts(V("clist", 0, 6), V("c2", 15, NT, 16), V("esc", 0, 1), A.mult, -0.34, A.add)
+            ypart(6, tab, OWN, OWN + NT)
+        pf = OPT["pf"][b]
+        for t in range(4 - pf):
+            mm(t, E(t), V(xq, PK - 32, PK + NT), True, False)
         arrive([V(tab, PAR, PAR + NT), V(tab + "s", PAR, PAR + NT)], "ac%d" % b, partner, 2)
         for t in range(4):
-            copy(V("dg", NT * t, NT * t + NT), V("junk", NU + NT * t, NU + NT * t + NT), off=V("clist", 0, 6))
-            mm(t, E(t), V(tab, PAR - 32, PAR + NT))
-            tt(V("tl", MT + t, MT + 4 * NT, 4), V("dg", NT * t, NT * t + NT), V("ps%d" % t, 32, 128), A.add)
+            mm(t, E(t), V(tab, PAR - 32, PAR + NT), t >= 4 - pf, t < 4 - pf)
+            if t >= 4 - pf:
+                mm(t, E(t), V(xq, PK - 32, PK + NT), False, True)
+            copy(V("tl", MT + t, MT + 4 * NT, 4), V("ps%d" % t, 32, 128))
         quant(V(tab, MRG, MRG + 128), V("tl", MT, MT + 512))
         if b + 1 == NR:
-            ypart(7, tab, PAR, PAR + NT, 32)
+            ypart(7, tab, PAR, PAR + NT, pad=32)
             ypart(6, tab, MRG, MRG + NT)
-        arrive([V(xb, BP, BP + 24), V(xb + "s", BP, BP + 24)], "al%d" % b, partner, 2)
-        mm(5, V("ap", 0, 128), V(xb, BP, BP + 128), False, True)
-        tt(V("bl", 0, 24), V("ps5", 0, 24), V("sl", 0, 24), A.max)
-        vcopy(V("blist", 0, 24), V("bl", 0, 24))
         for k, (u, v) in enumerate(_cut(OPT["tab" if b + 1 < NR else "fin"])):
             pick(V(nxt, u, v), V(tab, 0, WIN), V("blist", u // 16, v // 16))
             if b + 1 < NR:
                 score(b + 1, k, u, v)
                 run_max(k, u, v)
+            elif k == 0:
+                mm(4, V("wq", 0, 128), V(nxt, u, v))
+                copy(V("ysb", u, v), V("ps4", 0, v - u))
 
-    for k, (u, v) in enumerate(_cut(OPT["yp"])):
+    for k, (u, v) in enumerate(_cut(OPT["fin"])[1:]):
         copy(V("ysb", u, v), V("yw", 0, MRG + NT), off=V("blist", u // 16, v // 16))
     for k, (u, v) in enumerate(_cut(OPT["ysp"])):
         store(OPT["ysq"][k], T.y[:, u:v], V("ysb", u, v), T.ysb[:, u:v])

import math
from concourse.bass import DstId, RemoteDMATransfer
from concourse.mybir import dt, AluOpType, AxisListType, ActivationFunctionType

A = AluOpType
AF = ActivationFunctionType
NU, NT, NR, NM = 384, 96, 2, 24
PAR, OWN, MRG, WIN = 384, 512, 1024, 1152
XQ, PK = 0, 128
UC, MK, M4, XL = 24, 26, 32, 56
OFF = 8192.0
LO = 192.0 + 7 * OFF
L4 = 4 * (192.0 + 31 * OFF)
RATIO, TOP, NONE = 1.54, 2.0 ** 29.7, 2.0 ** -62
STEP = 2 * math.log(RATIO)
MID = 2 * math.log(TOP) + 0.25
EDGE = MID - 96.3 * STEP
MT, XT, X0, KB, NTL, X1, WT = 0, 384, 608, 992, 2528, 2912, 3296
F4, F32, BF, U16, I32, U8 = "float8_e4m3fn_x4", "float32", "bfloat16", "uint16", "int32", "uint8"
OPT = {"load": (224, 160), "tab": (192, 192), "fin": (192, 192), "ysp": (384,), "ocp": (192, 192),
       "lq": "fff", "oscq": "ffff", "ysq": "fff", "ocq": "fff", "rq": "y", "dkp": ((224, 160), (192, 192)), "up": (384,), "pf": (0, 0)}
SQ = [int(x) for x in """
0 22 27 28 30 32 35 36 37 39 50 52 54 64 66 68 70 72 76 78 82 96 98 100 102 109 110 114 119 140 142 147 151 155 157 161 163 165 169 173 177 194
195 199 204 218 227 229 234 236 238 240 242 248 249
""".split()]
ORDER = [int(x) for x in """
5 11 1 0 13 2 14 40 6 41 7 12 35 15 57 16 63 46 58 8 23 3 9 37 36 42 17 60 32 43 49 4 67 61 59 64 65 71 10 18 31 24 50 62 33 25 80 51 29 68 69
66 20 79 26 81 52 34 82 19 21 75 73 83 70 84 45 53 55 30 54 86 72 56 103 77 27 76 88 74 104 78 89 105 90 47 95 97 91 87 106 22 38 107 115 101
102 92 96 44 28 93 39 114 123 113 120 116 121 110 117 108 99 100 94 122 125 118 98 119 124 109 111 136 112 127 126 128 132 133 129 139 137 134
141 138 142 130 135 140 143 144 131 145 147 146 151 148 150 156 152 154 149 48 157 155 158 160 153 171 172 159 170 174 164 173 175 162 161 165
163 179 188 166 168 167 189 169 182 178 190 191 183 181 184 200 192 195 205 185 85 201 206 202 199 198 204 207 176 193 203 180 208 186 187 194
196 197 217 209 210 212 219 221 211 218 220 214 223 222 213 215 177 230 228 231 229 226 227 224 225 216 232 233 234 235 238 237 241 236 245 239
242 243 246 240 250 249 247 248 244 251
""".split()]


def _decl():
    s = {}

    def add(n, w, t, where="sbuf"):
        s[n] = (where, [128, w], t)

    def pair(n, w):
        add(n, w, F4)
        add(n + "s", w, U8)
    for b in range(NR):
        pair("tab%d" % b, WIN)
        pair("xq%d" % b, PK + NT)
        pair("tbu%d" % b, NU)
        pair("xl%d" % b, M4 + 128)
        add("win%d" % b, 1, F32)
        add("look%d" % b, 8, U16)
        add("dx%d" % b, 4 * NT, BF)
    pair("e1", 512)
    for n in ("r16", "r4", "ao", "ap", "wq"):
        pair(n, 128)
    pair("fin", NU)
    for n in range(8):
        add("ps%d" % n, 512, F32, "psum")
    for n, w, t in (("tl", WT + 512, BF), ("te", 520, BF), ("tr", 520, BF), ("dd", 128, BF), ("chalf", 128, BF), ("wh", 1, BF),
                    ("dk", 4 * NU, BF), ("mask", 32, BF), ("junk", NU, BF), ("mb", 32, BF), ("cmod", 128, BF),
                    ("cm4", 128, BF), ("krow", 24, BF), ("ip", 2, I32), ("pi", 4, I32), ("ulist", 24, U16), ("blist", 24, U16), ("l4", 24, U16)):
        add(n, w, t)
    for n, w in (("pf", 4), ("pg", 2), ("p", NU), ("zz", 25), ("h1", 1), ("lc", 2), ("wa", NT), ("wb", 1), ("wt", 1),
                 ("cl", 24), ("sl", 24), ("lo", 24), ("lp", 24), ("lf", 24), ("la", 24), ("yo", 24), ("ysb", NU), ("yw", MRG + NT)):
        add(n, w, F32)
    return s


SCRATCH = _decl()
NCOMP, NHW = 100, 24
REMOTE = ["%s%d" % (n, b) for b in range(NR) for n in ("ae", "au", "ac")] + ["le", "lc"]
SEMAPHORES = ["c%d" % i for i in range(NCOMP)] + ["h%d" % i for i in range(NHW)] + REMOTE


def _clash(u, v):
    if u[1] >= v[2] or v[1] >= u[2] or u[4] >= v[5] or v[4] >= u[5]:
        return False
    return (u[1] - v[1]) % math.gcd(u[3], v[3]) == 0


def _record(rec, queue, kind, call, reads, writes, extra=(), tag=None):
    ops, acc = rec["ops"], rec["acc"]
    i = len(ops)
    deps, soft = set(extra), set()
    for vs, w in ((reads, False), (writes, True)):
        for v in vs:
            for (u, uw, j, uq) in acc.get(v[0], []):
                if v[0][:2] == "ps":
                    if uq == queue and (queue == "tensor" or not (w or uw)):
                        soft.add(j)
                    else:
                        deps.add(j)
                elif (w or uw) and _clash(u, v):
                    deps.add(j)
    for vs, w in ((reads, False), (writes, True)):
        for v in vs:
            acc.setdefault(v[0], []).append((v, w, i, queue))
    if kind == "arr":
        if deps:
            raise ValueError("a landing buffer is in use")
        soft = set(j for j in range(i) if ops[j]["tag"] == call[0])
    ops.append({"queue": queue, "kind": kind, "call": call, "deps": deps, "soft": soft, "need": False, "tag": tag})
    return i


def _issue(ops, order, queues, sems):
    place = {j: k for k, j in enumerate(order)}
    if len(place) != len(ops):
        raise ValueError("the order doesn't name every call once")
    seen = {}
    for i in order:
        o = ops[i]
        if any(place[j] > place[i] for j in o["deps"] | o["soft"]):
            raise ValueError("the order puts a call ahead of what it needs")
        known = seen.setdefault(o["queue"], set()) if o["kind"] != "arr" else set()
        o["waits"] = []
        for j in sorted(o["deps"], key=lambda j: -place[j]):
            if j not in known:
                o["waits"].append(j)
                known.add(j)
                known |= ops[j]["known"]
                ops[j]["need"] = True
        o["known"] = set(known)
    last, total = {}, {}
    for i in order:
        o = ops[i]
        if o["kind"] == "arr":
            o["sem"], o["val"] = o["call"]
            continue
        q = queues[o["queue"]]
        for j in reversed(o["waits"]):
            q.wait_ge(sems[ops[j]["sem"]], ops[j]["val"])
        if o["kind"] == "end":
            continue
        ins = o["call"](q)
        if not o["need"] or o["kind"] == "remote":
            continue
        pool = ["h%d" % k for k in range(NHW)] if o["kind"] == "dma" else ["c%d" % k for k in range(NCOMP)]
        name = None
        for s in pool:
            if s not in last or last[s] in o["known"]:
                name = s
                break
        if name is None:
            raise ValueError("out of semaphores")
        n = 16 if o["kind"] == "dma" else 1
        ins.then_inc(sems[name], n)
        last[name] = i
        total[name] = total.get(name, 0) + n
        o["sem"], o["val"] = name, total[name]


def V(name, a, b, s=1, p0=0, p1=128):
    return (name, a, b, s, p0, p1)


def _cut(sizes):
    return [(sum(sizes[:k]), sum(sizes[:k + 1])) for k in range(len(sizes))]


def _calls(core, T, topo):
    rank = T.rank_of(core)
    rec = {"ops": [], "acc": {}}
    local = {"le": 0, "lc": 0}
    eng = {"s": "scalar", "y": "sync"}

    def ap(v):
        return T[v[0]][v[4]:v[5], v[1]:v[2]] if v[3] == 1 else T[v[0]][v[4]:v[5], v[1]:v[2]:v[3]]

    def sc(v):
        return V(v[0] + "s", v[1], v[2])

    def views(*xs):
        return [x for x in xs if isinstance(x, tuple)]

    def val(x):
        return ap(x) if isinstance(x, tuple) else x

    def by(v, off):
        return ap(v) if off is None else ap(v).indirect(ap(off))

    def memset(out, c):
        _record(rec, "vector", "comp", lambda q: q.memset(ap(out), c), [], [out])

    def act(out, in_, func, scale=None, bias=None, off=None, accum=None):
        kw = {}
        if scale is not None:
            kw["scale"] = val(scale)
        if bias is not None:
            kw["bias"] = val(bias)
        if accum is not None:
            kw["accum_out"] = ap(accum)
        _record(rec, "scalar", "comp", lambda q: q.activation(ap(out), by(in_, off), func, **kw), views(in_, scale, bias, off), views(accum, out))

    def copy(out, in_, scale=None, bias=None, off=None):
        if len(rec["ops"]) in SQ:
            return act(out, in_, AF.Copy if bias is None else AF.Identity, scale, bias, off)
        if bias is not None and scale is not None:
            return ts(out, in_, scale, A.mult, bias, A.add)
        if bias is not None:
            return ts(out, in_, bias, A.add)
        if scale is not None:
            return ts(out, in_, scale, A.mult)
        vcopy(out, in_, off)

    def vcopy(out, in_, off=None):
        _record(rec, "vector", "comp", lambda q: q.tensor_copy(ap(out), by(in_, off)), views(in_, off), [out])

    def ts(out, in0, s1, op0, s2=None, op1=None):
        def call(q):
            if op1 is None:
                return q.tensor_scalar(ap(out), ap(in0), val(s1), None, op0)
            return q.tensor_scalar(ap(out), ap(in0), val(s1), val(s2), op0, op1)
        _record(rec, "vector", "comp", call, views(in0, s1, s2), [out])

    def tt(out, in0, in1, op, off=None):
        _record(rec, "vector", "comp", lambda q: q.tensor_tensor(ap(out), by(in0, off), ap(in1), op), views(in0, off, in1), [out])

    def reduce(out, in_, op):
        _record(rec, "vector", "comp", lambda q: q.tensor_reduce(ap(out), ap(in_), AxisListType.X, op), [in_], [out])

    def scan(out, d0, d1, init, op0, op1):
        _record(rec, "vector", "comp", lambda q: q.tensor_tensor_scan(ap(out), ap(d0), ap(d1), val(init), op0, op1),
                views(d0, d1, init), [out])

    def quant(out, in_):
        _record(rec, "vector", "comp", lambda q: q.quantize_mx(ap(out), ap(sc(out)), ap(in_)), [in_], [out, sc(out)])

    def mm(ps, w, x, start=True, stop=True):
        n = x[2] - x[1]
        _record(rec, "tensor", "comp",
                lambda q: q.matmul_mx(T["ps%d" % ps][:, 0:n], ap(w), ap(sc(w)), ap(x), ap(sc(x)), start, stop),
                [w, sc(w), x, sc(x)], [V("ps%d" % ps, 0, n)])

    def pick(out, win, off):
        _record(rec, "vector", "comp",
                lambda q: q.tensor_copy(ap(out).bitcast(dt.uint32), ap(win).bitcast(dt.uint32).indirect(ap(off))), [win, off], [out])
        copy(sc(out), sc(win), off=off)

    def iota(out, pattern, base, cm):
        f = SCRATCH[out[0]][2] != I32

        def call(q):
            if f:
                return q.iota(ap(out), pattern, base, cm, allow_small_or_imprecise_dtypes=True)
            return q.iota(ap(out), pattern, base, cm)
        _record(rec, "gpsimd", "comp", call, [], [out])

    def fill(name, a, b, c):
        if b - a > 128:
            return memset(V(name, a, b), c)
        copy(V(name, a, b), V("dd", 0, b - a), scale=0.0, bias=c if c else None)

    def dq(queue):
        return eng[queue] if queue in eng else "scalar" if len(rec["ops"]) in SQ else "sync"

    def load(queue, out, src, after=()):
        return _record(rec, dq(queue), "dma", lambda q: q.dma_start(ap(out), src), [], [out], after)

    stores = []

    def store(queue, dst, in_, view):
        stores.append(_record(rec, dq(queue), "dma", lambda q: q.dma_start(dst, view), [in_], []))

    def raw(v):
        return ap(v).bitcast(dt.uint8) if SCRATCH[v[0]][2] == F4 else ap(v)

    def send1(dst, out, in_, arr, loc):
        rid, pid, _s = topo.addr(dst)
        local[loc] += len(topo.engines(core, dst))
        _record(rec, "gpsimd", "remote", lambda q: q.remote_dma(raw(out), raw(in_), T.sem[arr], T.sem[loc], pid, rid, topo.mask(core, dst)),
                [in_], [], tag=arr)

    def send(dst, out, in_, arr, loc):
        send1(dst, out, in_, arr, loc)
        send1(dst, sc(out), sc(in_), arr, loc)

    def send2(dst, outs, ins, arr, loc):
        rid, pid, _s = topo.addr(dst)
        es = topo.engines(core, dst)
        local[loc] += len(es)

        def call(q):
            return q.remote_dma_fused([RemoteDMATransfer(dst_ids=[DstId(rid=rid, pnc=pid)], dma_engine_mask=sum(1 << e for e in es[k::2]),
                                                         remote_sem=T.sem[arr], src=raw(ins[k]), dst=raw(outs[k])) for k in range(2)],
                                      local_sem=T.sem[loc])
        _record(rec, "gpsimd", "remote", call, list(ins), [], tag=arr)

    def arrive(writes, sem, src, calls=1):
        _record(rec, "network", "arr", (sem, calls * len(topo.engines(src, core))), [], writes)

    pm, pd, p4, pq, wt = V("pf", 0, 1), V("pf", 1, 2), V("pf", 2, 3), V("pf", 3, 4), V("wt", 0, 1)
    first = [load(OPT["lq"][0], V("tl", X0, X0 + 384), T.x[:, 0:384])]
    for k, (u, v) in enumerate(_cut(OPT["load"])):
        first.append(load(OPT["lq"][k + 1], V("tl", KB + 4 * u, KB + 4 * v), T.kb[:, 4 * u:4 * v]))
    load(OPT["rq"], V("tl", X1, X1 + 384), T.x[:, 384:768], first)
    load(OPT["rq"], V("tl", WT, WT + 512), T.w[:, 0:512], first)

    iota(V("dd", 0, 128), [[1, 128]], 0, -1)
    iota(V("ip", 0, 1), [[0, 1]], 0, 1)
    iota(V("ip", 1, 2), [[0, 1]], 0, 4)
    iota(V("cmod", 0, 128), [[0, 8], [1, 16]], 0, 0)
    iota(V("krow", 0, 24), [[16, 24]], -192, 0)
    iota(V("cm4", 0, 128), [[0, 8], [4, 4], [0, 4]], 0, 0)
    memset(V("lc", 0, 1), math.exp(MID))
    act(V("lc", 1, 2), V("lc", 0, 1), AF.Ln)
    fill("te", 0, 520, 0.0)
    ts(V("te", 4, 516, 4), V("dd", 0, 128), 0.0, A.is_equal, 0.5, A.mult)
    ts(V("pi", 0, 4, 2), V("ip", 0, 2), 15, A.bitwise_and)
    ts(V("pi", 1, 4, 2), V("ip", 0, 2), 4, A.logical_shift_right)
    vcopy(V("pf", 0, 4), V("pi", 0, 4))
    ts(V("tr", 2, 512, 4), V("cmod", 0, 128), pm, A.is_equal)
    copy(V("tr", 3, 512, 4), V("tr", 2, 512, 4))
    ts(V("tr", 0, 512, 4), V("cm4", 0, 128), p4, A.is_equal, 4.0, A.mult)
    copy(V("tr", 1, 512, 4), V("tr", 0, 512, 4))
    fill("tr", 512, 514, 0.0)
    iota(V("wa", 0, NT), [[0, NT]], 1, 0)
    _record(rec, "gpsimd", "comp", lambda q: q.affine_select(T.wa[:, 0:NT], T.wa[:, 0:NT], [[1, NT]], A.is_gt, 1.0 / RATIO, 0, -1),
            [V("wa", 0, NT)], [V("wa", 0, NT)])
    reduce(V("wb", 0, 1), V("wa", 0, NT), A.mult)
    copy(wt, V("wb", 0, 1), scale=TOP * RATIO)
    copy(V("pg", 1, 2), p4, scale=0.25, bias=L4)
    copy(V("chalf", 0, 128), V("cmod", 0, 128), scale=0.5)
    ts(V("mask", 0, 2), V("pf", 1, 3), 5.5, A.is_le)
    copy(V("wh", 0, 1), V("wb", 0, 1), scale=TOP * RATIO)
    ts(V("mask", MK - UC, M4 - UC), V("cmod", 0, 6), pd, A.is_equal)
    copy(V("pg", 0, 1), pq, scale=16.0, bias=-192.0)
    ts(V("mask", M4 - UC, XL - UC), V("krow", 0, 24), V("pg", 0, 1), A.is_equal)
    copy(V("mb", 0, XL - UC), V("mask", 0, XL - UC), scale=OFF, bias=-OFF - 192.0)
    fill("zz", 24, 25, -192.0)
    fill("tl", XT, XT + 128, 0.0)
    fill("tl", XT + 128, XT + 4 * XL, 0.0)
    ts(V("cl", 0, 24), V("krow", 0, 24), pm, A.add, 192.0, A.add)
    copy(V("cl", 0, 24), V("cl", 0, 24), scale=STEP)
    for t in range(4):
        quant(V("e1", 128 * t, 128 * t + 128), V("te", 4 - t, 516 - t))
    quant(V("r16", 0, 128), V("tr", 2, 514))
    quant(V("r4", 0, 128), V("tr", 0, 512))
    quant(V("xq0", XQ, XQ + 128), V("tl", X0, X0 + 512))
    quant(V("xq1", XQ, XQ + 128), V("tl", X1, X1 + 512))
    quant(V("wq", 0, 128), V("tl", WT, WT + 512))

    def E(t):
        return V("e1", 128 * t, 128 * t + 128)

    def score(b, k, u, v):
        mm(4 + k, V("xq%d" % b, XQ, XQ + 128), V("tab%d" % b, u, v))

    def run_max(k, u, v):
        scan(V("p", u, v), V("te", 1, 1 + 2 * (v - u), 2), V("ps%d" % (4 + k), 0, v - u), V("p", u - 1, u) if u else -1e29, A.add, A.max)

    def ypart(ps, tab, u, v, pad=0):
        mm(ps, V("wq", 0, 128), V(tab, u - pad, max(v, u - pad + 128)))
        copy(V("yw", u, v), V("ps%d" % ps, pad, pad + v - u))

    def tokens(b, banks):
        for t in range(4):
            mm(banks[t], E(t), V("xq%d" % b, XQ, XQ + 128))
            copy(V("dx%d" % b, t, 4 * NT, 4), V("ps%d" % banks[t], 0, NT), scale=0.5)

    tokens(0, (6, 7, 6, 7))
    for k, (u, v) in enumerate(_cut(OPT["load"])):
        quant(V("tab0", u, v), V("tl", KB + 4 * u, KB + 4 * v))
        score(0, k, u, v)
        run_max(k, u, v)

    for b in range(NR):
        tab, xq, xl, tbu = ["%s%d" % (n, b) for n in ("tab", "xq", "xl", "tbu")]
        nxt = "tab%d" % (b + 1) if b + 1 < NR else "fin"
        win, look, cl = V("win%d" % b, 0, 1), V("look%d" % b, 0, 6), V("cl", 0, 24)
        ao, lt, pl, pe = V("ao", 0, 128), V(xl, M4, M4 + 128), V(xl, 0, 128), V(xl, UC, UC + 128)
        lo, lp, lf, la, yo, sl = [V(n, 0, NM) for n in ("lo", "lp", "lf", "la", "yo", "sl")]
        partner = T.cores[rank ^ (1 << b)]
        for (u, v) in _cut(OPT["dkp"][b]):
            for t in range(4):
                mm(t, E(t), V(tab, u, v))
                copy(V("dk", 4 * u + t, 4 * v, 4), V("ps%d" % t, 0, v - u), scale=1.5)
        last, h1 = V("p", NU - 1, NU), V("h1", 0, 1)
        act(V("junk", 0, NU), V("p", 0, NU), AF.Sign, scale=-1.0, bias=last, accum=win)
        ts(V("zz", 0, 24), V("p", 15, NU, 16), last, A.is_lt, 16.0, A.mult)
        reduce(h1, V("zz", 0, 25), A.add)
        copy(V("tl", XT + 4 * UC + 1, XT + 4 * XL, 4), V("mask", 0, XL - UC), scale=h1)
        ts(V("tl", XT, XT + 4 * NM, 4), V("krow", 0, NM), h1, A.is_equal, wt, A.mult)
        ts(V("tl", XT + 4 * UC, XT + 4 * XL, 4), V("mb", 0, XL - UC), win, A.add, h1, A.subtract)
        if b + 1 == NR:
            ypart(4, tab, 0, NU)
        store(OPT["rq"], T.ch[b:b + 1, 0:NT], win, T[win[0]][0:NT, 0:1])
        quant(lt, V("tl", XT, XT + 512))
        send1(partner, V(xl, 0, UC), V(xl, M4, M4 + UC), "ae%d" % b, "le")
        send2(partner, (V(xl, UC, M4), V(xl + "s", 0, M4)), (V(xl, M4 + UC, 2 * M4), V(xl + "s", M4, 2 * M4)), "au%d" % b, "le")
        mm(6, V("r4", 0, 128), lt)
        ts(V("l4", 0, 24), V("ps6", M4, XL), V("pg", 1, 2), A.add)
        tt(V("tl", NTL, NTL + 4 * NT), V("dk", 0, 4 * NU), V("dx%d" % b, 0, 4 * NT), A.add, V("l4", 0, 24))
        quant(V(tab, OWN, OWN + 128), V("tl", NTL, NTL + 512))
        send(partner, V(tab, PAR, PAR + NT), V(tab, OWN, OWN + NT), "ac%d" % b, "lc")
        if b + 1 < NR:
            tokens(b + 1, range(4))
        ts(V("te", 0, 512, 4), V("cmod", 0, 128), V("tl", XT + 4 * UC, XT + 4 * UC + 1), A.is_equal, V("wh", 0, 1), A.mult)
        quant(ao, V("te", 0, 512))
        mm(7, ao, lt)
        act(lo, V("ps7", 0, NM), AF.Ln, bias=NONE)
        ts(V("ulist", 0, 24), lo, V("lc", 1, 2), A.subtract, -1.0 / STEP, A.mult)
        ts(lf, lo, EDGE, A.is_gt, (MRG - PAR) * STEP, A.mult)
        copy(la, lf, bias=MID + PAR * STEP)
        copy(yo, lo, scale=-1.0, bias=MID + OWN * STEP)
        tt(yo, yo, lf, A.min)
        tt(sl, yo, cl, A.max)
        for (u, v) in _cut(OPT["up"]):
            pick(V(tbu, u, v), V(tab, OWN, OWN + 128), V("ulist", u // 16, v // 16))
        arrive([V(xl, UC, M4), V(xl + "s", 0, M4)], "au%d" % b, partner)
        mm(6, V("r16", 0, 128), pe)
        ts(look, V("ps6", MK - UC, M4 - UC), LO, A.add)
        pick(V(xq, PK, PK + NT), V(tbu, 0, NU), look)
        mm(7, E(0), pe)
        ts(V("te", 2, 514, 4), V("chalf", 0, 128), V("ps7", 0, 1), A.is_equal, wt, A.mult)
        quant(V("ap", 0, 128), V("te", 2, 514))
        arrive([V(xl, 0, UC)], "ae%d" % b, partner)
        mm(5, V("ap", 0, 128), pl)
        mm(7, V("ap", 0, 128), pl)
        act(lp, V("ps5", 0, NM), AF.Ln, bias=NONE)
        ts(lf, V("ps7", 0, NM), 0.0, A.is_gt, WIN * STEP, A.mult)
        tt(lf, lf, sl, A.add)
        tt(la, la, lp, A.subtract)
        tt(la, la, lf, A.min)
        ts(V("blist", 0, 24), la, 1.0 / STEP, A.mult)
        if b + 1 == NR:
            ypart(6, tab, OWN, OWN + NT)
        pf = OPT["pf"][b]
        for t in range(4 - pf):
            mm(t, E(t), V(xq, PK - 32, PK + NT), True, False)
        arrive([V(tab, PAR, PAR + NT), V(tab + "s", PAR, PAR + NT)], "ac%d" % b, partner, 2)
        for t in range(4):
            mm(t, E(t), V(tab, PAR - 32, PAR + NT), t >= 4 - pf, t < 4 - pf)
            if t >= 4 - pf:
                mm(t, E(t), V(xq, PK - 32, PK + NT), False, True)
            copy(V("tl", MT + t, MT + 4 * NT, 4), V("ps%d" % t, 32, 128))
        quant(V(tab, MRG, MRG + 128), V("tl", MT, MT + 512))
        if b + 1 == NR:
            ypart(7, tab, PAR, PAR + NT, pad=32)
            ypart(6, tab, MRG, MRG + NT)
        for k, (u, v) in enumerate(_cut(OPT["tab" if b + 1 < NR else "fin"])):
            pick(V(nxt, u, v), V(tab, 0, WIN), V("blist", u // 16, v // 16))
            if b + 1 < NR:
                score(b + 1, k, u, v)
                run_max(k, u, v)
            elif k == 0:
                mm(4, V("wq", 0, 128), V(nxt, u, v))
                copy(V("ysb", u, v), V("ps4", 0, v - u))

    for k, (u, v) in enumerate(_cut(OPT["fin"])[1:]):
        copy(V("ysb", u, v), V("yw", 0, MRG + NT), off=V("blist", u // 16, v // 16))
    for k, (u, v) in enumerate(_cut(OPT["ysp"])):
        store(OPT["ysq"][k], T.y[:, u:v], V("ysb", u, v), T.ysb[:, u:v])
    for k, (u, v) in enumerate(_cut(OPT["ocp"])):
        store(OPT["ocq"][k], T.oc[:, 4 * u:4 * v], V("fin", u, v), T.fin[:, u:v].bitcast(dt.uint8))
    for k in range(4):
        store(OPT["oscq"][k], T.osc[4 * k:4 * k + 4, 0:NU], V("fins", 0, NU), T.fins[32 * k:32 * k + 4, 0:NU])
    _record(rec, "sync", "end", None, [], [], stores)
    return rec["ops"], local


def rank_program(g, core, T, topo):
    if T.rank_of(core) is None:
        return
    ops, local = _calls(core, T, topo)
    _issue(ops, ORDER or list(range(len(ops))), {"vector": g.vector, "scalar": g.scalar, "tensor": g.tensor, "gpsimd": g, "sync": g.sync}, T.sem)
    for n in sorted(local):
        g.wait_ge(T.sem[n], local[n])
